import numpy as np, ml_dtypes
CORES = [1,5,17,21,33,37,49,53]
N = 8
import mx_ref
BF = ml_dtypes.bfloat16
def gentries(a):
    return np.ascontiguousarray(a.reshape(8, 16, -1).transpose(0, 2, 1)).reshape(8, -1)
def gtable(e):
    e = np.asarray(e); return np.ascontiguousarray(e.reshape(8, -1, 16).transpose(0, 2, 1)).reshape(128, -1).astype(np.int32)
def gcols(t, e):
    v = np.concatenate([t.reshape(8, 16, -1, 4), np.zeros((8, 16, 1, 4), BF)], axis=2)
    return np.ascontiguousarray(np.stack([v[g][:, e[g]] for g in range(8)])).reshape(128, -1)
def tile(rs):
    return np.stack(rs, axis=2).reshape(128, -1).astype(BF)
def pick(q, e):
    c = np.concatenate([q[0].reshape(128, -1, 4), np.zeros((128, 1, 4), np.uint8)], axis=1); s = np.concatenate([q[1], np.ones((16, 1), np.uint8)], axis=1)
    return (np.ascontiguousarray(c[:, e].reshape(128, -1)), np.ascontiguousarray(s[:, e]))
def join(*qs):
    return (np.concatenate([q[0] for q in qs], axis=1), np.concatenate([q[1] for q in qs], axis=1))
def put(q, e, v):
    c, s = q[0].reshape(128, -1, 4).copy(), q[1].copy(); c[:, e] = v[0].reshape(128, -1, 4); s[:, e] = v[1]
    return (c.reshape(128, -1), s)
def pk(c, s):
    return (np.ascontiguousarray(c), mx_ref.live(s))
def emit(q):
    return q[0], q[1]
def packed(v, rng):
    q = [mx_ref.quantize(np.ascontiguousarray(v[r])) for r in range(N)]
    return np.stack([a for a, b in q]), np.stack([mx_ref.plane(b, rng) for a, b in q])
def values_of_codes():
    e, c = np.zeros((128, 128, 4), np.float32), np.zeros((128, 2, 4), np.uint8)
    e[np.arange(128), np.arange(128), 0] = 1
    c[:127, :, 0] = np.arange(256).reshape(2, 128).T[:127]
    return mx_ref.matmul(mx_ref.quantize(e.reshape(128, 512).astype(BF)), (c.reshape(128, 8), np.full((16, 2), 127, np.uint8))).T.reshape(-1).astype(np.float64)
CODE_VALUE, SCALE_VALUE = values_of_codes(), 2.0 ** (np.arange(256) - 127.0)
def decode(q):
    return (CODE_VALUE[q[0]].reshape(16, 8, -1, 4) * SCALE_VALUE[q[1]][:, None, :, None] + 0.0).reshape(128, -1).astype(np.float32)
def f(rng, *shape):
    return mx_ref.flush((rng.standard_normal(shape, dtype=np.float32) * np.exp2(rng.integers(-2, 3, shape[:-1] + (1,)))).astype(BF))
def wide(rng, *shape, cols=0):
    v = rng.standard_normal(shape, dtype=np.float32) * np.exp2(rng.integers(-12, 13, shape)).astype(np.float32)
    if cols: v *= np.repeat(np.exp2(rng.integers(-cols, cols + 1, shape[:-2] + (1, shape[-1] // 4))) * (rng.random(shape[:-2] + (1, shape[-1] // 4)) > 0.0625), 4, axis=-1).astype(np.float32)
    return mx_ref.flush(v.astype(BF))
C, R = 384, 3
STEP = [1, 2, 4]
def big(v):
    v = v.astype(np.float32)
    v[np.abs(v) < np.float32(2.0 ** -16)] = 0
    return v.astype(BF)
def numbers_of(rng):
    return {"x": big(f(rng, N, 128, 4 * C)), "u": np.array(f(rng, N, 128, 512)), "v": np.array(f(rng, N, 128, 512))}
def layers(rng):
    return big(f(rng, N, 128, 2048)).reshape(N, 8, 16, 4, 8, 16, 4)
def weights(rng, w):
    c, p = packed(np.ascontiguousarray(w).reshape(N, 128, 2048), rng)
    return {"wc": c, "ws": p}
def stored(e):
    return {"vg": np.stack([gtable(e[r]) for r in range(N)])}
def pointers(rng):
    return stored(rng.integers(0, 2 * C, (N, 8, C)))
def setup_inputs(rng):
    return {**numbers_of(rng), **weights(rng, layers(rng)), **pointers(rng)}
def setup_inputs_ties(rng):
    d = numbers_of(rng)
    e = rng.permutation(N)
    lo, hi = sorted((int(e[0]), int(e[0]) ^ STEP[0]))
    u = d["u"].reshape(N, 128, 128, 4)
    for r in range(N):
        k = np.zeros(8, int) if r in (lo, hi) else rng.permutation(8) % 3
        a = u[r][:, 1:4].copy()
        a[:, 2] = 0
        u[r][:, ::16] = a[:, k]
    d["x"][e[1]] = 0
    p = rng.integers(0, 2 * C, (N, 8, C))
    p[lo, 7] = np.arange(C)
    p[hi, 7] = rng.permutation(C)
    return {"x": d["x"], "u": u.reshape(N, 128, 512), "v": d["v"], **weights(rng, layers(rng)), **stored(p)}
def setup_inputs_near(rng):
    d = numbers_of(rng)
    x = d["x"].astype(np.float32).reshape(N, 8, 16, C, 4)
    s = rng.integers(0, 4, (2, N, 8, C))
    x[:, :, 0] = 0
    x[:, :, 0, :, 0] = 1
    x[:, :, 8:10] = 0
    for i, k in ((0, 2.0 ** -22), (1, 2.0 ** -29)):
        x[:, :, 8 + i, :, 0] = (s[i] & 1) * k
        x[:, :, 8 + i, :, 1] = (s[i] >> 1) * (2 * k)
    x[:, :, 10:] = rng.integers(4, 8, (N, 8, 6, C, 4)) * 2.0 ** -25
    n = rng.integers(0, 4, (N, 8, C))
    x[:, :, 10, :, 0] = (8 + 2 * n) * 2.0 ** -33
    x[:, :, 11, :, 0] = (14 - 2 * n) * 2.0 ** -33
    u = d["u"].reshape(N, 128, 128, 4)
    u[:, :, ::16] = 0
    o = rng.permutation(N) % 4
    for r in range(N):
        k = (1.0, -1.0, 2.0 ** -30, 2.0 ** -30)[o[r]]
        for h in range(0, 128, 16):
            if o[r] < 3:
                u[r, h, h, 0] = k
                u[r, h + 8, h, :2] = abs(k)
            else:
                u[r, h + 9, h, :2] = k
                u[r, h + 10, h, 0] = 9 * 2.0 ** -33
                u[r, h + 11, h, 0] = 8 * 2.0 ** -33
        if o[r] == 3:
            h = 16 * int(rng.integers(8))
            u[r, h, h, 0] = 1.0
    w = layers(rng)
    for i in (0, 8, 9, 10, 11, 12, 13, 14, 15):
        w[:, :, i] = 0
        w[:, :, :, :, :, i] = 0
    return {"x": x.reshape(N, 128, 4 * C).astype(BF), "u": u.reshape(N, 128, 512), "v": d["v"], **weights(rng, w), **pointers(rng)}
def setup_inputs_huge(rng):
    d = numbers_of(rng)
    x = -2.0 ** 30 * (0.55 + 0.2 * rng.random((N, 8, 1, C, 1)) + 0.05 * rng.random((N, 8, 16, C, 4)))
    u = d["u"].reshape(N, 128, 128, 4)
    o = rng.permutation(N) % 4
    s = np.stack([np.full(8, 1.0 - 2.0 * o[r]) if o[r] < 2 else rng.permutation(8) % 2 * 2.0 - 1.0 for r in range(N)])
    own = np.where(np.arange(128)[:, None] // 16 == np.arange(8), 1.0, 0.75)
    a = 2.0 ** 30 * (1 - 0.1 * rng.random((N, 128, 8, 4))) * own[None, :, :, None] * s[:, None, :, None]
    u[:, :, ::16] = a.astype(np.float32).astype(BF)
    w = np.zeros((N, 128, 4, 128, 4), np.float32)
    i = np.arange(128)
    for b in range(4): w[:, i, b, i, b] = -1
    return {"x": x.astype(np.float32).reshape(N, 128, 4 * C).astype(BF), "u": u.reshape(N, 128, 512), "v": d["v"], **weights(rng, w.astype(BF)), **pointers(rng)}
def setup_inputs_asks(rng):
    d = numbers_of(rng)
    e = np.zeros((N, 8, C), int)
    first = [r for r in range(N) if r < (r ^ STEP[0])]
    for i, r in enumerate(rng.permutation(first)):
        m, o = np.arange(2 * C), rng.permutation(2 * C)
        if i == 0:
            k = C + rng.permutation(C)
            m[:C] = k
            m[k] = np.arange(C)
        if i == 1:
            m[o[C // 2:C]] = o[0]
            k = np.sort(o[C:])
            m[k[:-1]] = k[1:]
        if i == 2: m[:] = o[0]
        e[r] = m[:C]
        e[r ^ STEP[0]] = m[C:]
    return {**d, **weights(rng, layers(rng)), **stored(e)}
def setup_inputs_spread(rng):
    d = setup_inputs(rng)
    d["x"] = big(wide(rng, N, 128, 4 * C, cols=6))
    return d
def check_inputs(d):
    b = []
    for k in ("x", "u", "v"):
        a = np.abs(d[k].astype(np.float32))
        if not (np.isfinite(a).all() and ((a == 0) | (a >= 2.0 ** -30) & (a <= 2.0 ** 30)).all()): b.append("a value of " + k)
    if ((d["wc"] & 0x7F) == 0x7F).any(): b.append("a code of wc that is no number")
    none, least, most = [emit(mx_ref.quantize(np.full((128, 16), k, np.float32).astype(BF)))[1][0, 0] for k in (0.0, 2.0 ** -30, 2.0 ** 30)]
    for r in range(N):
        s = mx_ref.live(d["ws"][r])
        if ((s != none) & ((s < least) | (s > most))).any(): b.append("a scale of ws")
    if ((d["vg"] < 0) | (d["vg"] >= 2 * C)).any(): b.append("a pointer of vg")
    return b
def swapped(p, s):
    n = np.arange(2 * C)
    o = np.argsort(-(s + np.float32(0.0)), axis=0, kind="stable")
    a = p[o[7], n]
    asks = a != n
    low = np.where(asks, n, 2 * C)
    np.minimum.at(low, a[asks], n[asks])
    c = n[asks & (low == n) & (low[a] == n)]
    k, new = a[c], p.copy()
    for m in range(4):
        g = o[m, c]
        new[g, c], new[g, k] = p[g, k], p[g, c]
    g = o[7, c]
    new[g, c], new[g, k] = p[g, k], c
    return new
def reference(x, u, v, wc, ws, vg):
    qu = [mx_ref.quantize(u[r]) for r in range(N)]
    lay = [pk(wc[r], ws[r]) for r in range(N)]
    now = [x[r] for r in range(N)]
    at = [gentries(vg[r]) for r in range(N)]
    for t in range(R):
        had = [decode(mx_ref.quantize(now[r])).astype(BF) for r in range(N)]
        score = []
        for r in range(N):
            one, two = min(r, r ^ STEP[t]), max(r, r ^ STEP[t])
            z = np.concatenate([had[one], had[two]], axis=1)
            p = np.concatenate([at[one], at[two]], axis=1)
            a, b = gcols(z, at[r]), gcols(z, np.take_along_axis(p, at[r], axis=1))
            q = mx_ref.quantize(((a.astype(np.float32) + b.astype(np.float32)) * np.float32(0.5)).astype(BF))
            score.append(mx_ref.matmul(qu[r], q)[::16])
            now[r] = tile([np.maximum(mx_ref.matmul(pick(lay[r], np.arange(128 * i, 128 * i + 128)), q), np.float32(0.0)) * np.float32(0.03125) + had[r][:, i::4].astype(np.float32) for i in range(4)])
        for r in range(N):
            e = r ^ STEP[t]
            if r < e:
                p = swapped(np.concatenate([at[r], at[e]], axis=1), np.concatenate([score[r], score[e]], axis=1))
                at[r], at[e] = p[:, :C], p[:, C:]
    y, ov = np.zeros((N, 128, C), np.float32), np.zeros((N, 8, C), np.float32)
    oc, osc = np.zeros((N, 128, 4 * C), np.uint8), np.zeros((N, 16, C), np.uint8)
    for r in range(N):
        q = mx_ref.quantize(now[r])
        y[r] = mx_ref.matmul(mx_ref.quantize(v[r]), q)
        ov[r] = at[r]
        oc[r], osc[r] = emit(q)
    return {"y": y, "ov": ov, "oc": oc, "osc": osc}

@@ -1,0 +1,515 @@
+from concourse.mybir import dt, AluOpType, ActivationFunctionType
+
+C = 384
+STEP = [1, 2, 4]
+Q8, U8, BF, F32, F16, I32, U16 = "float8_e4m3fn_x4", "uint8", "bfloat16", "float32", "float16", "int32", "uint16"
+LS = 4096.0
+NONE = 768 * LS
+
+
+def sb(n, d):
+    return ("sbuf", [128, n], d)
+
+
+SCRATCH = {
+    "xin": sb(4 * C, BF), "xt": sb(4 * C, BF), "yt": sb(4 * C, BF), "ct": sb(4 * C, BF),
+    "ut": sb(512, BF), "vt": sb(512, BF), "e0": sb(528, BF), "et": sb(2048, BF), "kt": sb(512, BF),
+    "uq": sb(128, Q8), "us": sb(128, U8), "upq": sb(256, Q8), "ups": sb(256, U8),
+    "vq": sb(128, Q8), "vs": sb(128, U8), "eq": sb(512, Q8), "es": sb(512, U8),
+    "kq": sb(128, Q8), "ks": sb(128, U8), "wq": sb(512, Q8), "wsc": sb(512, U8),
+    "yq": sb(C, Q8), "ys": sb(C, U8), "cq": sb(C, Q8), "cs": sb(C, U8),
+    "fw": sb(4 * 2 * C, BF), "aw": sb(4 * 2 * C, BF), "ac": sb(4 * C, BF),
+    "sa": sb(C, F32), "rl": sb(4 * C, F32), "yo": sb(C, F32),
+    "vgi": sb(24, I32), "t32": sb(C, F32), "key": sb(96, F32), "ksc": sb(96, F32), "p8": sb(96, F32),
+    "z32": sb(C, F16), "m32": sb(C, BF), "af": sb(C, F16), "ar": sb(C, F16),
+    "dd": sb(6 * C, BF), "ones": sb(C, BF), "so": sb(6 * C, F16), "rel": sb(24, F32), "selfd": sb(48, F32),
+    "low": sb(48, F32), "wb": sb(48, F32), "wf": sb(2 * C, F32),
+    "wr": sb(2 * C + 32, F32), "gv": sb(C, F32), "vt32": sb(C, F32), "vi": sb(48, I32),
+    "sm": sb(28 * 24, F32), "pm": sb(24, F32), "mseg": sb(96, F32),
+    "swi": sb(64, F32), "swx": sb(64, F32), "swz": sb(64, F32), "swo": sb(64, F32), "cand": sb(32, U16),
+    "ovi": sb(32, F32), "ovo": sb(32, F32),
+    "ci": sb(448, I32), "sc": sb(32, I32), "cf": sb(512, F32), "kk": sb(256, F32), "lu": sb(16, U16),
+    "lsw": sb(4, U16), "lfin": sb(2, U16), "lrep": sb(24, U16), "lrel": sb(4, U16),
+}
+for _t in range(4):
+    SCRATCH["xq%d" % _t] = sb(C, Q8)
+    SCRATCH["xs%d" % _t] = sb(C, U8)
+for _t in range(3):
+    SCRATCH["lq%d" % _t] = sb(C, Q8)
+    SCRATCH["ls%d" % _t] = sb(C, U8)
+    SCRATCH["pl%d" % _t] = sb(32, U16)
+    SCRATCH["plp%d" % _t] = sb(24, U16)
+    SCRATCH["h1s%d" % _t] = sb(72, F32)
+    SCRATCH["h1r%d" % _t] = sb(72, F32)
+for _b in range(8):
+    SCRATCH["pb%d" % _b] = ("psum", [128, 512], F32)
+
+SEMAPHORES = (["sV", "sS", "sP", "sG", "sent", "st"] + ["ld%d" % i for i in range(7)]
+              + ["a%s%d" % (k, t) for k in "xph" for t in range(3)])
+
+A = AluOpType
+FN = ActivationFunctionType
+
+
+def rank_program(g, core, T, topo):
+    rank = T.rank_of(core)
+    if rank is None:
+        return
+    eng = {"V": g.vector, "S": g.scalar, "P": g.tensor, "G": g, "Y": g.sync}
+    count, known, wrote, read = {}, {q: {} for q in eng}, {}, {}
+
+    def wait(q, toks):
+        need = {}
+        for s, n in toks:
+            if n > need.get(s, 0):
+                need[s] = n
+        for s, n in need.items():
+            if known[q].get(s, 0) < n:
+                eng[q].wait_ge(T.sem[s], n)
+                known[q][s] = n
+
+    def op(q, r, w, call, sem=None, inc=1):
+        r, w = r.split(), w.split()
+        toks = [wrote[k] for k in r + w if k in wrote]
+        for k in w:
+            toks += read.get(k, [])
+        for k in r:
+            if k.startswith("pb"):
+                toks += [x for x in read.get(k, []) if x[0] != "s" + q]
+        wait(q, toks)
+        sem = sem or "s" + q
+        count[sem] = count.get(sem, 0) + inc
+        call().then_inc(T.sem[sem], inc)
+        for k in r:
+            read.setdefault(k, []).append((sem, count[sem]))
+        for k in w:
+            wrote[k] = (sem, count[sem])
+            read[k] = []
+
+    def tt(r, w, out, a, b, o):
+        op("V", r, w, lambda: g.vector.tensor_tensor(out, a, b, o))
+
+    def ts(r, w, out, a, s1, o1, s2=None, o2=None):
+        if o2 is None:
+            op("V", r, w, lambda: g.vector.tensor_scalar(out, a, s1, None, o1))
+        else:
+            op("V", r, w, lambda: g.vector.tensor_scalar(out, a, s1, s2, o1, o2))
+
+    def cp(r, w, out, a):
+        op("V", r, w, lambda: g.vector.tensor_copy(out, a))
+
+    def tr(r, w, out, a):
+        op("V", r, w, lambda: g.vector.transpose(out, a))
+
+    def ms(w, out, v):
+        op("V", "", w, lambda: g.vector.memset(out, v))
+
+    def scan(r, w, out, a, b, init, o0, o1):
+        op("V", r, w, lambda: g.vector.tensor_tensor_scan(out, a, b, init, o0, o1))
+
+    def quant(r, w, q, s, t):
+        op("V", r, w, lambda: g.vector.quantize_mx(q, s, t))
+
+    def act(r, w, out, a, fn, **kw):
+        op("S", r, w, lambda: g.scalar.activation(out, a, fn, **kw))
+
+    def move(q, r, w, out, a, k=1.0):
+        if q == "S":
+            act(r, w, out, a, FN.Copy, scale=k)
+        else:
+            ts(r, w, out, a, k, A.mult)
+
+    def mm(r, bank, wq, ws, xq, xs):
+        op("P", r, "pb%d" % bank, lambda: g.tensor.matmul_mx(T["pb%d" % bank][:, 0:C], wq, ws, xq, xs, True, True))
+
+    def iota(w, out, pattern, base, cm):
+        op("G", "", w, lambda: g.iota(out, pattern, base, cm))
+
+    def fill(w, out, n, v):
+        op("G", "", w, lambda: g.iota(out, [[0, n]], v, 0, allow_small_or_imprecise_dtypes=True))
+
+    def dma(q, r, w, out, a, sem):
+        op(q, r, w, lambda: eng[q].dma_start(out, a), sem, 16)
+
+    def send(t, kind, r, pairs, lands):
+        dst = T.cores[rank ^ STEP[t]]
+        rid, pid, _ = topo.addr(dst)
+        sem = "a%s%d" % (kind, t)
+        wait("G", [wrote[k] for k in r.split()])
+        for out, a in pairs:
+            g.remote_dma(out, a, T.sem[sem], T.sem.sent, pid, rid, topo.mask(core, dst))
+            count["sent"] = count.get("sent", 0) + len(topo.engines(core, dst))
+        count[sem] = len(pairs) * len(topo.engines(dst, core))
+        wrote[lands] = (sem, count[sem])
+
+    def u8(v):
+        return v.bitcast(dt.uint8)
+
+    def sm(i, n=24):
+        return T.sm[:, 24 * i:24 * i + n]
+
+    up = [(rank & s) != 0 for s in STEP]
+    cf, ci, sc = T.cf, T.ci, T.sc
+    c_row, c_gm, c_xk, c_xn, c_p = cf[:, 0:128], cf[:, 352:376], 376, 384, cf[:, 392:393]
+    k_i, k_j, k_r, k_15, k_q, k_odd, k_h, k_8 = (cf[:, 400 + k:401 + k] for k in range(8))
+
+    def cd(t, big):
+        return 256 + 24 * (2 * big + int(up[t]))
+
+    def exchange_x(t, tile, keys):
+        xq, xs = T["xq%d" % t], T["xs%d" % t]
+        quant(keys, "xq%d" % t, xq[:], xs[:], tile[:])
+        if t < 3:
+            send(t, "x", "xq%d" % t, [(u8(T["lq%d" % t][:]), u8(xq[:])), (T["ls%d" % t][:], xs[:])], "lq%d" % t)
+
+    def decode(t, mine):
+        q, s = ("xq%d" % t, "xs%d" % t) if mine else ("lq%d" % t, "ls%d" % t)
+        for b in (0, 1, 3, 2):
+            mm("eq " + q, b + (0 if mine else 4), T.eq[:, 128 * b:128 * b + 128], T.es[:, 128 * b:128 * b + 128], T[q][:], T[s][:])
+
+    def half(t, mine):
+        return C * int(up[t] == mine)
+
+    def unload(q, t, mine, b):
+        bank = b + (0 if mine else 4)
+        a = 2 * C * b + half(t, mine)
+        move(q, "pb%d" % bank, "fw%d%d" % (b, mine), T.fw[:, a:a + C], T["pb%d" % bank][:, 0:C], 0.5)
+
+    def gather_a(q, t, mine, b, lo=0, hi=24):
+        name = ("pl%d" if mine else "plp%d") % t
+        a = 2 * C * b + half(t, mine)
+        win = T.fw[:, 2 * C * b:2 * C * (b + 1)].indirect(T[name][:, lo:hi])
+        out = T.aw[:, a + 16 * lo:a + 16 * hi]
+        r = "fw%d0 fw%d1 %s" % (b, b, name)
+        w = " ".join("aw%d%d%d" % (b, mine, k) for k in range(lo // 12, hi // 12))
+        if q == "S":
+            act(r, w, out, win, FN.Copy)
+        else:
+            cp(r, w, out, win)
+
+    def double(q, t, b):
+        a = 2 * C * b + half(t, True)
+        r, w, out, src = "aw%d10 aw%d11" % (b, b), "ac%d" % b, T.ac[:, C * b:C * b + C], T.aw[:, a:a + C]
+        if q == "G":
+            op("G", r, w, lambda: g.affine_select(out, src, [[0, C]], A.is_gt, 0.0, 1, 0))
+        else:
+            move(q, r, w, out, src)
+
+    def gather_b(t, b):
+        r = " ".join("aw%d%d%d" % (b, m, k) for m in range(2) for k in range(2)) + " pl%d ac%d" % (t, b)
+        tt(r, "yt%d" % b, T.yt[:, b:4 * C:4], T.aw[:, 2 * C * b:2 * C * (b + 1)].indirect(T["pl%d" % t][:, 0:24]),
+           T.ac[:, C * b:C * b + C], A.add)
+
+    steps = [lambda: tr("swi0 swi1", "swx", T.swx[:], T.swi[:]),
+             lambda: cp("swx lsw", "swz", T.swz[:], T.swx[:].indirect(T.lsw[:])),
+             lambda: tr("swz", "swo", T.swo[:], T.swz[:])]
+
+    def to_list(name):
+        cp("swo lfin", name, T[name][:], T.swo[:].indirect(T.lfin[:]))
+
+    def spread(t, e):
+        tt("pm cd0 cd1", "s24", sm(24), T.pm[:], cf[:, cd(t, 0):cd(t, 0) + 24], A.is_equal)
+        tt("pm c_gm", "s25", sm(25), T.pm[:], c_gm, A.add)
+        ts("s24", "s26", sm(26), sm(24), 1024.0, A.mult)
+        tt("s25 s26", "s27", sm(27), sm(25), sm(26), A.add)
+        k = 1.0 / 2048
+        move(e, "s27", "p8a", T.p8[:, 0:96:4], sm(27), k)
+        move(e, "s27", "p8b", T.p8[0:64, 2:96:4], T.sm[64:128, 648:672], k)
+        move(e, "s27", "p8c", T.p8[64:128, 2:96:4], T.sm[0:64, 648:672], k)
+        for q in range(4):
+            s = 32 * ((q + 1) % 4)
+            move(e, "p8a p8b p8c", "p8d%d" % q, T.p8[32 * q:32 * q + 32, 1:96:2], T.p8[s:s + 32, 0:96:2])
+
+    dma("Y", "", "vgi", T.vgi[:], T.vg[:], "ld0")
+    dma("Y", "", "xin0", T.xin[:, 0:768], T.x[:, 0:768], "ld1")
+    dma("S", "", "xin1", T.xin[:, 768:1536], T.x[:, 768:1536], "ld2")
+    wait("Y", [wrote["xin0"]])
+    dma("Y", "", "ut", T.ut[:], T.u[:], "ld3")
+    dma("Y", "", "wq", u8(T.wq[:]), T.wc[:], "ld4")
+    dma("Y", "", "wsc", T.wsc[:], T.ws[:], "ld5")
+    dma("Y", "", "vt", T.vt[:], T.v[:], "ld6")
+
+    ip = ci[:, 128:129]
+    iota("i_p", ip, [[1, 1]], 0, 1)
+    iota("i_row", ci[:, 0:128], [[1, 128]], 0, 0)
+    iota("i_sw", ci[:, 312:316], [[16, 2], [32, 2]], 0, 0)
+    iota("i_cd", ci[:, 258:282], [[32, 12], [0, 2]], 0, 0)
+    iota("i_e", ci[:, 282:306], [[0, 12], [2048, 2]], 0, 0)
+    iota("i_xk", ci[:, 306:312], [[128, 6]], 0, 1)
+    ms("e0", T.e0[:], 0.0)
+    ms("swi0 swi1", T.swi[:], 0.0)
+    ms("kt", T.kt[:], 0.0)
+    cp("i_p", "c_p", c_p, ip)
+    ts("i_p", "k0", sc[:, 0:1], ip, 3, A.arith_shift_right)
+    ts("i_p", "k1", sc[:, 1:2], ip, 7, A.bitwise_and)
+    ts("i_p", "k2", sc[:, 2:3], ip, 31, A.bitwise_and)
+    ts("i_p", "k3", sc[:, 3:4], ip, 15, A.bitwise_and)
+    cp("i_row", "c_row", c_row, ci[:, 0:128])
+    ts("i_p", "k4", sc[:, 4:5], ip, 5, A.arith_shift_right)
+    ts("c_row c_p e0", "e0", T.e0[:, 3:515:4], c_row, c_p, A.is_equal)
+    for b in range(4):
+        act("e0", "et%d" % b, T.et[:, 512 * b:512 * b + 512], T.e0[:, 3 - b:515 - b], FN.Copy)
+    ts("i_p", "k5", sc[:, 5:6], ip, 1, A.bitwise_and)
+    ts("i_p", "k6", sc[:, 6:7], ip, 1, A.arith_shift_right, 7, A.bitwise_and)
+    ts("i_p", "k7", sc[:, 7:8], ip, 3, A.arith_shift_right, 1, A.bitwise_and)
+    ms("mseg", T.mseg[:], 0.0)
+    cp("k0 k1 k2 k3 k4 k5 k6 k7", "kf", cf[:, 400:408], sc[:, 0:8])
+    ts("k6", "k20", sc[:, 24:25], sc[:, 6:7], 3, A.bitwise_and)
+    ts("k6", "k21", sc[:, 25:26], sc[:, 6:7], 2, A.arith_shift_right)
+    ms("mseg", T.mseg[:, 0:96:8], -100.0)
+    ts("i_sw kf", "lsw", T.lsw[:], ci[:, 312:316], k_15, A.add)
+    ts("kf", "k9", cf[:, 408:409], k_odd, 32.0, A.mult, k_h, A.add)
+    cp("vgi", "pl0", T.pl0[:, 0:24], T.vgi[:])
+    send(0, "p", "pl0", [(T.plp0[:], T.pl0[:, 0:24])], "plp0")
+    cp("vgi", "swi0", T.swi[:, 0:12], T.vgi[:, 0:24:2])
+    cp("vgi", "swi1", T.swi[:, 32:44], T.vgi[:, 1:24:2])
+    exchange_x(0, T.xin, "xin0 xin1")
+    quant("et0 et1 et2 et3", "eq", T.eq[:], T.es[:], T.et[:])
+    decode(0, True)
+    for b in (0, 1, 3, 2):
+        unload("S", 0, True, b)
+    iota("i_a", ci[:, 130:258], [[2, 4], [1, 2], [0, 16]], 0, 0)
+    iota("i_b", ci[:, 320:448], [[0, 8], [2, 4], [0, 4]], 0, 0)
+    fill("ct", T.ct[:], 4 * C, 0)
+
+    steps[0]()
+    ts("c_row kf", "k11", sc[:, 8:16], c_row[:, 0:16:2], k_8, A.add)
+    ts("c_row kf", "k12", cf[:, 424:432], c_row[:, 0:8], 0.0, A.mult, k_j, A.add)
+    steps[1]()
+    ts("k11", "k13", sc[:, 16:24], sc[:, 8:16], 7, A.bitwise_and)
+    ts("k12", "lub", T.lu[:, 8:16], cf[:, 424:432], 16.0, A.mult)
+    steps[2]()
+    ts("k13", "lua", T.lu[:, 0:8], sc[:, 16:24], 16.0, A.mult)
+    ts("i_cd kf", "cd0", cf[:, 256:280], ci[:, 258:282], k_r, A.add)
+    cp("swo", "pma", T.pm[:, 0:24:2], T.swo[:, 0:12])
+    cp("swo", "pm", T.pm[:, 1:24:2], T.swo[:, 32:44])
+    ts("i_cd kf", "cd1", cf[:, 280:304], ci[:, 258:282], k_r, A.add, float(C), A.add)
+    ts("kf", "k15", cf[:, 409:410], k_q, 4096.0, A.mult)
+    tt("kf", "k16", cf[:, 410:411], k_i, k_j, A.is_lt)
+    tt("i_a i_b", "k14", ci[:, 130:258], ci[:, 130:258], ci[:, 320:448], A.add)
+    ts("i_e k15", "c_gm", c_gm, ci[:, 282:306], cf[:, 409:410], A.add)
+    quant("ut", "uq", T.uq[:], T.us[:], T.ut[:])
+    ts("k14", "k17", ci[:, 320:448], ci[:, 130:258], 7, A.bitwise_and)
+    cp("uq lua lub", "upq", T.upq[:].bitcast(dt.uint32), T.uq[:].bitcast(dt.uint32).indirect(T.lu[:]))
+    act("uq lua lub", "ups", T.ups[:], T.us[:].indirect(T.lu[:]), FN.Copy)
+    spread(0, "S")
+    ts("k17 kf k16", "k18", T.kk[:, 0:128], ci[:, 320:448], k_i, A.is_equal, cf[:, 410:411], A.mult)
+    ts("k17 kf k16", "k19", T.kk[:, 128:256], ci[:, 320:448], k_j, A.is_equal, cf[:, 410:411], A.mult)
+    ts("k20 kf", "k22", sc[:, 26:27], sc[:, 24:25], k_q, A.subtract, 4.0, A.add)
+    tt("k18 k19 kt", "kt", T.kt[:, 0:512:4], T.kk[:, 0:128], T.kk[:, 128:256], A.subtract)
+    ts("k22", "k23", sc[:, 27:28], sc[:, 26:27], 1, A.bitwise_and)
+    ts("k22", "k24", sc[:, 28:29], sc[:, 26:27], 1, A.arith_shift_right, 1, A.bitwise_and)
+    quant("kt", "kq", T.kq[:], T.ks[:], T.kt[:])
+
+    def late_constants():
+        ts("k23", "k25", cf[:, 411:412], sc[:, 27:28], 12.0, A.mult)
+        ts("k24", "k26", cf[:, 412:413], sc[:, 28:29], 6.0, A.mult)
+        cp("k21", "k27", cf[:, 413:414], sc[:, 25:26])
+        ts("cd0 cd1", "c_cd", cf[:, 304:352], cf[:, 256:304], LS, A.mult)
+        cp("i_xk", "c_xk", cf[:, c_xk:c_xk + 6], ci[:, 306:312])
+        ts("i_xk", "c_xn", cf[:, c_xn:c_xn + 6], ci[:, 306:312], -1024.0, A.mult)
+        ts("k25 k26 k27", "k28", cf[:, 414:415], cf[:, 411:412], cf[:, 412:413], A.add, cf[:, 413:414], A.add)
+        ts("c_row k9", "lfin", T.lfin[:], c_row[:, 0:16:8], cf[:, 408:409], A.add)
+        cp("c_row", "lrep", T.lrep[:], c_row[:, 0:24])
+        ts("c_row k28", "lrel", T.lrel[:, 0:3], c_row[:, 0:6:2], cf[:, 414:415], A.add)
+
+    decode(0, False)
+    unload("V", 0, False, 0)
+    unload("S", 0, False, 1)
+    unload("V", 0, False, 3)
+    unload("S", 0, False, 2)
+    gather_a("V", 0, True, 0)
+    gather_a("S", 0, True, 1)
+    gather_a("V", 0, True, 3)
+    gather_a("S", 0, True, 2)
+    double("V", 0, 0)
+    gather_a("V", 0, False, 0)
+    for b in (1, 3, 2):
+        gather_a("S", 0, False, b)
+        double("G", 0, b)
+    fill("ones", T.ones[:], C, 1)
+    op("G", "ones", "m32", lambda: g.affine_select(T.m32[:], T.ones[:], [[0, C // 32], [1, 32]], A.not_equal, 0.0, 0, 0))
+
+    for t in range(3):
+        own = 24 * int(up[t])
+        hs, hr = T["h1s%d" % t], T["h1r%d" % t]
+        ks_, kr = "h1s%d" % t, "h1r%d" % t
+        if t > 0:
+            gather_a("S", t, False, 0, 12, 24)
+            gather_a("V", t, False, 0, 0, 12)
+            for b in (1, 3, 2):
+                gather_a("S", t, False, b)
+        for b in (0, 1, 3, 2):
+            gather_b(t, b)
+        quant("yt0 yt1 yt2 yt3", "yq", T.yq[:], T.ys[:], T.yt[:])
+        mm("upq ups yq", 4, T.upq[:, 0:128], T.ups[:, 0:128], T.yq[:], T.ys[:])
+        mm("upq ups yq", 5, T.upq[:, 128:256], T.ups[:, 128:256], T.yq[:], T.ys[:])
+        banks = (6, 7, 5, 6)
+
+        def layer(b):
+            mm("wq wsc yq", banks[b], T.wq[:, 128 * b:128 * b + 128], T.wsc[:, 128 * b:128 * b + 128], T.yq[:], T.ys[:])
+
+        def relu(b):
+            act("pb%d" % banks[b], "rl%d" % b, T.rl[:, C * b:C * b + C], T["pb%d" % banks[b]][:, 0:C], FN.Relu, scale=0.03125)
+
+        def add(b):
+            tt("pb%d rl%d" % (b, b), "xt%d" % b, T.xt[:, b:4 * C:4], T["pb%d" % b][:, 0:C], T.rl[:, C * b:C * b + C], A.add)
+
+        layer(0)
+        layer(1)
+        for h in range(2):
+            act("pb4", "sa%d" % h, T.sa[:, 192 * h:192 * h + 192], T.pb4[:, 192 * h:192 * h + 192], FN.Copy)
+        ms("selfd selfd0 selfd1", T.selfd[:], NONE)
+        if t == 0:
+            late_constants()
+        else:
+            spread(t, "V")
+        for h in range(2):
+            tt("pb5 ct sa%d" % h, "ct%d" % h, T.ct[:, 768 * h:768 * h + 768:4], T.pb5[:, 192 * h:192 * h + 192],
+               T.sa[:, 192 * h:192 * h + 192], A.is_gt)
+        relu(0)
+        relu(1)
+        quant("ct0 ct1", "cq", T.cq[:], T.cs[:], T.ct[:])
+        layer(2)
+        mm("kq cq", 4, T.kq[:], T.ks[:], T.cq[:], T.cs[:])
+        layer(3)
+        relu(2)
+        relu(3)
+        add(0)
+        if t == 0:
+            ts("ones", "z32", T.z32[:], T.ones[:], 0.0, A.mult)
+        tr("pb4", "t32", T.t32[:], T.pb4[:, 0:C])
+        tt("t32 p8a p8b p8c p8d0 p8d1 p8d2 p8d3", "key", T.key[:], T.t32[:, 0:C:4], T.p8[:], A.add)
+        scan("key mseg", "ksc", T.ksc[:], T.mseg[:], T.key[:], -100.0, A.add, A.max)
+        k0, k7 = T.key[:, 0:96:4], T.ksc[:, 7:96:8]
+        ts("key", "s4", sm(4), k0, 4.0, A.is_lt, 1024.0, A.mult)
+        ts("ksc", "z32", T.z32[:, 0:C:32], k7, 7.0, A.subtract, 2048.0, A.mult)
+        ts("key", "s5", sm(5), k0, 7.0, A.is_ge, 2048.0, A.mult)
+        scan("z32 m32", "af", T.af[:], T.m32[:], T.z32[:], 0.0, A.mult, A.add)
+        ts("ksc", "s7", sm(7, 12), k7, 7.5, A.is_ge, NONE, A.mult)
+        tr("af", "ar", T.ar[:], T.af[:])
+        tt("s4 s5", "s6", sm(6), sm(4), sm(5), A.add)
+        rev = T.ar[:, ::-1]
+
+        def differ(q, k):
+            out = T.dd[:, C * k:C * k + C]
+            if q == "S":
+                act("ar c_xn", "dd%d" % k, out, rev, FN.Abs, scale=1024.0, bias=cf[:, c_xn + k:c_xn + k + 1])
+            else:
+                ts("ar c_xk", "dd%d" % k, out, rev, cf[:, c_xk + k:c_xk + k + 1], A.not_equal, 1024.0, A.mult)
+
+        def first(k):
+            scan("dd%d ones" % k, "so%d" % k, T.so[:, C * k:C * k + C], T.ones[:], T.dd[:, C * k:C * k + C],
+                 0.0 if up[t] else float(C), A.add, A.min)
+
+        for k in range(2, 6):
+            differ("S", k)
+        differ("V", 0)
+        differ("V", 1)
+        for k in range(4):
+            first(k)
+        add(1)
+        first(4)
+        tt("s6 pm", ks_ + "p", hs[:, 48:72], sm(6), T.pm[:], A.add)
+        for e in range(2):
+            a = cd(t, 1)
+            tt("s7 c_cd", "selfd%d" % e, T.selfd[:, own + e:own + 24:2], sm(7, 12), cf[:, a:a + 24:2], A.max)
+        first(5)
+        sos = "so0 so1 so2 so3 so4 so5"
+        base = float(C) if up[t] else 0.0
+        ts(sos, "rel0", T.rel[:, 0:6], T.so[:, C - 1:6 * C:C], base, A.add, LS, A.mult)
+        ts(sos, "rel1", T.rel[0:64, 6:12], T.so[64:128, C - 1:6 * C:C], base, A.add, LS, A.mult)
+        ts(sos, "rel2", T.rel[64:128, 6:12], T.so[0:64, C - 1:6 * C:C], base, A.add, LS, A.mult)
+        for q in range(4):
+            s = 32 * ((q + 1) % 4)
+            move("VS"[q // 3], "rel0 rel1 rel2", "rel%d" % (3 + q), T.rel[32 * q:32 * q + 32, 12:24], T.rel[s:s + 32, 0:12])
+        tt("rel0 rel1 rel2 rel3 rel4 rel5 rel6 lrel selfd selfd0 selfd1", ks_ + "l", hs[:, 0:48],
+           T.rel[:].indirect(T.lrel[:, 0:3]), T.selfd[:], A.min)
+        send(t, "h", ks_ + "l " + ks_ + "p", [(hr[:], hs[:])], kr)
+        add(2)
+        add(3)
+        exchange_x(t + 1, T.xt, "xt0 xt1 xt2 xt3")
+        ts("ksc", "s8", sm(8, 12), k7, 7.0, A.subtract, 2048.0, A.mult)
+        ts("s6", "s9", sm(9), sm(6), 0.0, A.is_equal, LS, A.mult)
+        if t == 0:
+            ms("wrc", T.wr[:, 2 * C:2 * C + 32], 0.0)
+            ms("ovi0 ovi1", T.ovi[:], 0.0)
+            quant("vt", "vq", T.vq[:], T.vs[:], T.vt[:])
+        tt("s8 cd0 cd1", "s10", sm(10, 12), sm(8, 12), cf[:, cd(t, 0):cd(t, 0) + 24:2], A.subtract)
+        ts("s9", "s11", sm(11), sm(9), 1024.0, A.subtract)
+        if t < 2:
+            decode(t + 1, True)
+            for b in range(2):
+                unload("S", t + 1, True, b)
+        else:
+            mm("vq xq3", 4, T.vq[:], T.vs[:], T.xq3[:], T.xs3[:])
+            dma("Y", "xq3", "", T.oc[:], u8(T.xq3[:]), "st")
+            act("pb4", "yo", T.yo[:], T.pb4[:, 0:C], FN.Copy)
+            for k in range(4):
+                dma("Y", "xq3", "", T.osc[4 * k:4 * k + 4, :], T.xs3[32 * k:32 * k + 4, :], "st")
+            dma("Y", "yo", "", T.y[:], T.yo[:], "st")
+        lo_pf, up_pf = (hr, hs) if up[t] else (hs, hr)
+        both = ks_ + "l " + ks_ + "p " + kr
+        lown = T.low[:, own:own + 24]
+        tt(both, "low", T.low[:], hs[:, 0:48], hr[:, 0:48], A.min)
+        tt(both + " low", "wb0", T.wb[:, 0:24], T.low[:, 0:24], lo_pf[:, 48:72], A.add)
+        tt(both + " low", "wb1", T.wb[:, 24:48], T.low[:, 24:48], up_pf[:, 48:72], A.add)
+        for h in range(2):
+            act("lrep wb%d" % h, "wf%d" % h, T.wf[:, C * h:C * h + C], T.wb[:, 24 * h:24 * h + 24].indirect(T.lrep[:]), FN.Copy)
+        tt("low c_cd", "s12", sm(12), lown, cf[:, cd(t, 1):cd(t, 1) + 24], A.is_equal)
+        ts("low", "s13", sm(13), lown, 1.0 / LS, A.mult)
+        tt("s12 s10", "s14", sm(14, 12), T.sm[:, 24 * 12:24 * 13:2], sm(10, 12), A.mult)
+        ts("low", "s16", sm(16), lown, 1024.0, A.add)
+        for e in range(2):
+            tt("s14 s13", "swi%d" % e, T.swi[:, 32 * e:32 * e + 12], sm(14, 12), T.sm[:, 24 * 13:24 * 14:2], A.add)
+        tt("s12 s11", "s15", sm(15), sm(12), sm(11), A.mult)
+        steps[0]()
+        ts("s12", "s17", sm(17), sm(12), LS, A.mult, 2048.0, A.add)
+        steps[1]()
+        tr("wf0", "wr0", T.wr[:, 0:C], T.wf[:, 0:C])
+        steps[2]()
+        tt("s15 s16", "s18", sm(18), sm(15), sm(16), A.add)
+        to_list("cand")
+        tt("s17 low", "s19", sm(19), sm(17), lown, A.add)
+        tr("wf1", "wr1", T.wr[:, C:2 * C], T.wf[:, C:2 * C])
+        act("wr0 wr1 wrc cand", "gv1", T.gv[:, 192:C], T.wr[:].indirect(T.cand[:, 12:24]), FN.Copy)
+        cp("wr0 wr1 wrc cand", "gv0", T.gv[:, 0:192], T.wr[:].indirect(T.cand[:, 0:12]))
+        if t < 2:
+            decode(t + 1, False)
+            for mine, b in ((True, 3), (True, 2), (False, 0), (False, 1), (False, 3), (False, 2)):
+                unload("S", t + 1, mine, b)
+        tr("gv0 gv1", "vt32", T.vt32[:], T.gv[:])
+        v = T.vt32[:, 0:C:16]
+        cp("vt32", "vi", T.vi[:, 0:24], v)
+        tt("vt32 s18", "s20", sm(20), v, sm(18), A.is_ge)
+        tt("vt32 s19", "s21", sm(21), v, sm(19), A.is_ge)
+        tt("vt32 s18", "s22", sm(22), v, sm(18), A.is_lt)
+        ts("vi", "vi2", T.vi[:, 24:48], T.vi[:, 0:24], 1023, A.bitwise_and)
+        tt("s20 s21", "s0", sm(0), sm(20), sm(21), A.subtract)
+        tt("s21 s13", "s2", sm(2), sm(21), sm(13), A.mult)
+        tt("s22 pm", "s1", sm(1), sm(22), T.pm[:], A.mult)
+        tt("vi2 s0", "s3", sm(3), T.vi[:, 24:48], sm(0), A.mult)
+        tt("s1 s2", "s23", sm(23), sm(1), sm(2), A.add)
+        if t == 2:
+            for e in range(2):
+                tt("s3 s23", "ovi%d" % e, T.ovi[:, 12 * e:12 * e + 12], T.sm[:, 72 + e:96:2], T.sm[:, 552 + e:576:2], A.add)
+            tr("ovi0 ovi1", "ovo", T.ovo[:], T.ovi[:])
+            for q in range(4):
+                dma("YS"[q % 2], "ovo", "", T.ov[2 * q:2 * q + 2, :], T.ovo[32 * q:32 * q + 24, :], "st")
+            break
+        for e in range(2):
+            tt("s3 s23", "swi%d" % e, T.swi[:, 32 * e:32 * e + 12], T.sm[:, 72 + e:96:2], T.sm[:, 552 + e:576:2], A.add)
+        tt("s3 s23", "pm", T.pm[:], sm(3), sm(23), A.add)
+        steps[0]()
+        steps[1]()
+        steps[2]()
+        name = "pl%d" % (t + 1)
+        to_list(name)
+        send(t + 1, "p", name, [(T["plp%d" % (t + 1)][:], T[name][:, 0:24])], "plp%d" % (t + 1))
+        for b in (0, 1, 3):
+            gather_a("V", t + 1, True, b)
+            double("G", t + 1, b)
+        gather_a("S", t + 1, True, 2)
+        double("G", t + 1, 2)
+
+    wait("G", list(count.items()))

@@ -1,6 +1,7 @@
 from concourse.mybir import dt, AluOpType, ActivationFunctionType
 
 C = 384
+H = C // 2
 STEP = [1, 2, 4]
 Q8, U8, BF, F32, F16, I32, U16 = "float8_e4m3fn_x4", "uint8", "bfloat16", "float32", "float16", "int32", "uint16"
 LS = 4096.0
@@ -22,14 +23,14 @@ SCRATCH = {
     "sa": sb(C, F32), "rl": sb(4 * C, F32), "yo": sb(C, F32),
     "vgi": sb(24, I32), "t32": sb(C, F32), "key": sb(96, F32), "ksc": sb(96, F32), "p8": sb(96, F32),
     "z32": sb(C, F16), "m32": sb(C, BF), "af": sb(C, F16), "ar": sb(C, F16),
-    "dd": sb(6 * C, BF), "ones": sb(C, BF), "so": sb(6 * C, F16), "rel": sb(24, F32), "selfd": sb(48, F32),
+    "dd": sb(6 * C, BF), "ones": sb(C, BF), "so": sb(6 * C, F16), "rel": sb(24, F32), "selfd": sb(96, F32),
     "low": sb(48, F32), "wb": sb(48, F32), "wf": sb(2 * C, F32),
     "wr": sb(2 * C + 32, F32), "gv": sb(C, F32), "vt32": sb(C, F32), "vi": sb(48, I32),
     "sm": sb(28 * 24, F32), "pm": sb(24, F32), "mseg": sb(96, F32),
     "swi": sb(64, F32), "swx": sb(64, F32), "swz": sb(64, F32), "swo": sb(64, F32), "cand": sb(32, U16),
     "ovi": sb(32, F32), "ovo": sb(32, F32),
     "ci": sb(448, I32), "sc": sb(32, I32), "cf": sb(512, F32), "kk": sb(256, F32), "lu": sb(16, U16),
-    "lsw": sb(4, U16), "lfin": sb(2, U16), "lrep": sb(24, U16), "lrel": sb(4, U16),
+    "lsw": sb(4, U16), "lfin": sb(2, U16), "lrep": sb(48, U16), "lrel": sb(4, U16),
 }
 for _t in range(4):
     SCRATCH["xq%d" % _t] = sb(C, Q8)
@@ -119,14 +120,14 @@ def rank_program(g, core, T, topo):
         else:
             ts(r, w, out, a, k, A.mult)
 
-    def mm(r, bank, wq, ws, xq, xs):
-        op("P", r, "pb%d" % bank, lambda: g.tensor.matmul_mx(T["pb%d" % bank][:, 0:C], wq, ws, xq, xs, True, True))
+    def mm(r, bank, wq, ws, xq, xs, n=C):
+        op("P", r, "pb%d" % bank, lambda: g.tensor.matmul_mx(T["pb%d" % bank][:, 0:n], wq, ws, xq, xs, True, True))
 
     def iota(w, out, pattern, base, cm):
-        op("G", "", w, lambda: g.iota(out, pattern, base, cm))
+        op("G", "", w, lambda: g.iota(out, pattern, base, cm, allow_small_or_imprecise_dtypes=True))
 
     def fill(w, out, n, v):
-        op("G", "", w, lambda: g.iota(out, [[0, n]], v, 0, allow_small_or_imprecise_dtypes=True))
+        iota(w, out, [[0, n]], v, 0)
 
     def dma(q, r, w, out, a, sem):
         op(q, r, w, lambda: eng[q].dma_start(out, a), sem, 16)
@@ -195,10 +196,10 @@ def rank_program(g, core, T, topo):
         else:
             move(q, r, w, out, src)
 
-    def gather_b(t, b):
+    def gather_b(t, b, lo=0, hi=2):
         r = " ".join("aw%d%d%d" % (b, m, k) for m in range(2) for k in range(2)) + " pl%d ac%d" % (t, b)
-        tt(r, "yt%d" % b, T.yt[:, b:4 * C:4], T.aw[:, 2 * C * b:2 * C * (b + 1)].indirect(T["pl%d" % t][:, 0:24]),
-           T.ac[:, C * b:C * b + C], A.add)
+        tt(r, " ".join("yt%d%d" % (b, h) for h in range(lo, hi)), T.yt[:, 4 * H * lo + b:4 * H * hi:4],
+           T.aw[:, 2 * C * b:2 * C * (b + 1)].indirect(T["pl%d" % t][:, 12 * lo:12 * hi]), T.ac[:, C * b + H * lo:C * b + H * hi], A.add)
 
     steps = [lambda: tr("swi0 swi1", "swx", T.swx[:], T.swi[:]),
              lambda: cp("swx lsw", "swz", T.swz[:], T.swx[:].indirect(T.lsw[:])),
@@ -207,11 +208,13 @@ def rank_program(g, core, T, topo):
     def to_list(name):
         cp("swo lfin", name, T[name][:], T.swo[:].indirect(T.lfin[:]))
 
-    def spread(t, e):
+    def spread(t):
         tt("pm cd0 cd1", "s24", sm(24), T.pm[:], cf[:, cd(t, 0):cd(t, 0) + 24], A.is_equal)
         tt("pm c_gm", "s25", sm(25), T.pm[:], c_gm, A.add)
         ts("s24", "s26", sm(26), sm(24), 1024.0, A.mult)
         tt("s25 s26", "s27", sm(27), sm(25), sm(26), A.add)
+
+    def spread_out(e):
         k = 1.0 / 2048
         move(e, "s27", "p8a", T.p8[:, 0:96:4], sm(27), k)
         move(e, "s27", "p8b", T.p8[0:64, 2:96:4], T.sm[64:128, 648:672], k)
@@ -231,87 +234,67 @@ def rank_program(g, core, T, topo):
 
     ip = ci[:, 128:129]
     iota("i_p", ip, [[1, 1]], 0, 1)
-    iota("i_row", ci[:, 0:128], [[1, 128]], 0, 0)
+    iota("c_row", c_row, [[1, 128]], 0, 0)
+    iota("c_p", c_p, [[1, 1]], 0, 1)
     iota("i_sw", ci[:, 312:316], [[16, 2], [32, 2]], 0, 0)
-    iota("i_cd", ci[:, 258:282], [[32, 12], [0, 2]], 0, 0)
-    iota("i_e", ci[:, 282:306], [[0, 12], [2048, 2]], 0, 0)
-    iota("i_xk", ci[:, 306:312], [[128, 6]], 0, 1)
+    iota("i_cd", cf[:, 432:456], [[32, 12], [0, 2]], 0, 0)
+    iota("i_e", cf[:, 456:480], [[0, 12], [2048, 2]], 0, 0)
+    iota("i_16", ci[:, 304:312], [[0, 8]], 16, 0)
+    iota("c_x0", cf[:, c_xk:c_xk + 6], [[128, 6]], 0, 1)
     ms("e0", T.e0[:], 0.0)
     ms("swi0 swi1", T.swi[:], 0.0)
-    ms("kt", T.kt[:], 0.0)
-    cp("i_p", "c_p", c_p, ip)
     ts("i_p", "k0", sc[:, 0:1], ip, 3, A.arith_shift_right)
     ts("i_p", "k1", sc[:, 1:2], ip, 7, A.bitwise_and)
     ts("i_p", "k2", sc[:, 2:3], ip, 31, A.bitwise_and)
-    ts("i_p", "k3", sc[:, 3:4], ip, 15, A.bitwise_and)
-    cp("i_row", "c_row", c_row, ci[:, 0:128])
-    ts("i_p", "k4", sc[:, 4:5], ip, 5, A.arith_shift_right)
     ts("c_row c_p e0", "e0", T.e0[:, 3:515:4], c_row, c_p, A.is_equal)
     for b in range(4):
         act("e0", "et%d" % b, T.et[:, 512 * b:512 * b + 512], T.e0[:, 3 - b:515 - b], FN.Copy)
+    ts("i_p", "k3", sc[:, 3:4], ip, 15, A.bitwise_and)
+    ts("i_p", "k4", sc[:, 4:5], ip, 5, A.arith_shift_right)
     ts("i_p", "k5", sc[:, 5:6], ip, 1, A.bitwise_and)
     ts("i_p", "k6", sc[:, 6:7], ip, 1, A.arith_shift_right, 7, A.bitwise_and)
-    ts("i_p", "k7", sc[:, 7:8], ip, 3, A.arith_shift_right, 1, A.bitwise_and)
-    ms("mseg", T.mseg[:], 0.0)
+    ts("i_p", "k7", sc[:, 7:8], ip, 8, A.bitwise_and)
     cp("k0 k1 k2 k3 k4 k5 k6 k7", "kf", cf[:, 400:408], sc[:, 0:8])
-    ts("k6", "k20", sc[:, 24:25], sc[:, 6:7], 3, A.bitwise_and)
-    ts("k6", "k21", sc[:, 25:26], sc[:, 6:7], 2, A.arith_shift_right)
-    ms("mseg", T.mseg[:, 0:96:8], -100.0)
+    ts("k6", "k21", sc[:, 26:27], sc[:, 6:7], 4, A.bitwise_and)
     ts("i_sw kf", "lsw", T.lsw[:], ci[:, 312:316], k_15, A.add)
     ts("kf", "k9", cf[:, 408:409], k_odd, 32.0, A.mult, k_h, A.add)
     cp("vgi", "pl0", T.pl0[:, 0:24], T.vgi[:])
     send(0, "p", "pl0", [(T.plp0[:], T.pl0[:, 0:24])], "plp0")
     cp("vgi", "swi0", T.swi[:, 0:12], T.vgi[:, 0:24:2])
     cp("vgi", "swi1", T.swi[:, 32:44], T.vgi[:, 1:24:2])
+    tt("kf", "k16", cf[:, 410:411], k_i, k_j, A.is_lt)
+    ts("c_row kf", "k11", cf[:, 424:432], c_row[:, 0:128:16], k_8, A.add, 56.0, A.min)
     exchange_x(0, T.xin, "xin0 xin1")
-    quant("et0 et1 et2 et3", "eq", T.eq[:], T.es[:], T.et[:])
-    decode(0, True)
-    for b in (0, 1, 3, 2):
-        unload("S", 0, True, b)
     iota("i_a", ci[:, 130:258], [[2, 4], [1, 2], [0, 16]], 0, 0)
     iota("i_b", ci[:, 320:448], [[0, 8], [2, 4], [0, 4]], 0, 0)
+    fill("ones", T.ones[:], C, 1)
+    fill("kt", T.kt[:], 512, 0)
     fill("ct", T.ct[:], 4 * C, 0)
 
     steps[0]()
-    ts("c_row kf", "k11", sc[:, 8:16], c_row[:, 0:16:2], k_8, A.add)
-    ts("c_row kf", "k12", cf[:, 424:432], c_row[:, 0:8], 0.0, A.mult, k_j, A.add)
+    quant("et0 et1 et2 et3", "eq", T.eq[:], T.es[:], T.et[:])
+    act("i_cd kf", "cd0", cf[:, 256:280], cf[:, 432:456], FN.Identity, bias=k_r)
+    act("kf", "k15", cf[:, 409:410], k_q, FN.Copy, scale=4096.0)
+    act("cd0", "cd1", cf[:, 280:304], cf[:, 256:280], FN.Identity, bias=float(C))
+    act("i_e k15", "c_gm", c_gm, cf[:, 456:480], FN.Identity, bias=cf[:, 409:410])
+    decode(0, True)
     steps[1]()
-    ts("k11", "k13", sc[:, 16:24], sc[:, 8:16], 7, A.bitwise_and)
-    ts("k12", "lub", T.lu[:, 8:16], cf[:, 424:432], 16.0, A.mult)
+    ts("k11", "lua", T.lu[:, 0:8], cf[:, 424:432], 2.0, A.mult)
     steps[2]()
-    ts("k13", "lua", T.lu[:, 0:8], sc[:, 16:24], 16.0, A.mult)
-    ts("i_cd kf", "cd0", cf[:, 256:280], ci[:, 258:282], k_r, A.add)
+    ts("i_16 kf", "lub", T.lu[:, 8:16], ci[:, 304:312], k_j, A.mult)
     cp("swo", "pma", T.pm[:, 0:24:2], T.swo[:, 0:12])
     cp("swo", "pm", T.pm[:, 1:24:2], T.swo[:, 32:44])
-    ts("i_cd kf", "cd1", cf[:, 280:304], ci[:, 258:282], k_r, A.add, float(C), A.add)
-    ts("kf", "k15", cf[:, 409:410], k_q, 4096.0, A.mult)
-    tt("kf", "k16", cf[:, 410:411], k_i, k_j, A.is_lt)
-    tt("i_a i_b", "k14", ci[:, 130:258], ci[:, 130:258], ci[:, 320:448], A.add)
-    ts("i_e k15", "c_gm", c_gm, ci[:, 282:306], cf[:, 409:410], A.add)
+    for b in (0, 1, 3, 2):
+        unload("S", 0, True, b)
     quant("ut", "uq", T.uq[:], T.us[:], T.ut[:])
-    ts("k14", "k17", ci[:, 320:448], ci[:, 130:258], 7, A.bitwise_and)
+    tt("i_a i_b", "k14", ci[:, 130:258], ci[:, 130:258], ci[:, 320:448], A.add)
     cp("uq lua lub", "upq", T.upq[:].bitcast(dt.uint32), T.uq[:].bitcast(dt.uint32).indirect(T.lu[:]))
-    act("uq lua lub", "ups", T.ups[:], T.us[:].indirect(T.lu[:]), FN.Copy)
-    spread(0, "S")
+    ts("k14", "k17", ci[:, 320:448], ci[:, 130:258], 7, A.bitwise_and)
+    spread(0)
     ts("k17 kf k16", "k18", T.kk[:, 0:128], ci[:, 320:448], k_i, A.is_equal, cf[:, 410:411], A.mult)
     ts("k17 kf k16", "k19", T.kk[:, 128:256], ci[:, 320:448], k_j, A.is_equal, cf[:, 410:411], A.mult)
-    ts("k20 kf", "k22", sc[:, 26:27], sc[:, 24:25], k_q, A.subtract, 4.0, A.add)
+    ts("ones", "z32", T.z32[:], T.ones[:], 0.0, A.mult)
     tt("k18 k19 kt", "kt", T.kt[:, 0:512:4], T.kk[:, 0:128], T.kk[:, 128:256], A.subtract)
-    ts("k22", "k23", sc[:, 27:28], sc[:, 26:27], 1, A.bitwise_and)
-    ts("k22", "k24", sc[:, 28:29], sc[:, 26:27], 1, A.arith_shift_right, 1, A.bitwise_and)
-    quant("kt", "kq", T.kq[:], T.ks[:], T.kt[:])
-
-    def late_constants():
-        ts("k23", "k25", cf[:, 411:412], sc[:, 27:28], 12.0, A.mult)
-        ts("k24", "k26", cf[:, 412:413], sc[:, 28:29], 6.0, A.mult)
-        cp("k21", "k27", cf[:, 413:414], sc[:, 25:26])
-        ts("cd0 cd1", "c_cd", cf[:, 304:352], cf[:, 256:304], LS, A.mult)
-        cp("i_xk", "c_xk", cf[:, c_xk:c_xk + 6], ci[:, 306:312])
-        ts("i_xk", "c_xn", cf[:, c_xn:c_xn + 6], ci[:, 306:312], -1024.0, A.mult)
-        ts("k25 k26 k27", "k28", cf[:, 414:415], cf[:, 411:412], cf[:, 412:413], A.add, cf[:, 413:414], A.add)
-        ts("c_row k9", "lfin", T.lfin[:], c_row[:, 0:16:8], cf[:, 408:409], A.add)
-        cp("c_row", "lrep", T.lrep[:], c_row[:, 0:24])
-        ts("c_row k28", "lrel", T.lrel[:, 0:3], c_row[:, 0:6:2], cf[:, 414:415], A.add)
 
     decode(0, False)
     unload("V", 0, False, 0)
@@ -322,13 +305,19 @@ def rank_program(g, core, T, topo):
     gather_a("S", 0, True, 1)
     gather_a("V", 0, True, 3)
     gather_a("S", 0, True, 2)
-    double("V", 0, 0)
     gather_a("V", 0, False, 0)
     for b in (1, 3, 2):
         gather_a("S", 0, False, b)
+    for b in (0, 1, 3):
         double("G", 0, b)
-    fill("ones", T.ones[:], C, 1)
+    double("S", 0, 2)
+    act("uq lua lub", "ups", T.ups[:], T.us[:].indirect(T.lu[:]), FN.Copy)
+    fill("mseg", T.mseg[:], 96, 0)
+    op("G", "mseg", "mseg", lambda: g.affine_select(T.mseg[:], T.mseg[:], [[0, 12], [1, 8]], A.not_equal, -100.0, 0, 0))
     op("G", "ones", "m32", lambda: g.affine_select(T.m32[:], T.ones[:], [[0, C // 32], [1, 32]], A.not_equal, 0.0, 0, 0))
+    fill("selfd", T.selfd[:], 96, int(NONE))
+    fill("wrc", T.wr[:, 2 * C:2 * C + 32], 32, 0)
+    fill("ovi0 ovi1", T.ovi[:], 32, 0)
 
     for t in range(3):
         own = 24 * int(up[t])
@@ -339,15 +328,20 @@ def rank_program(g, core, T, topo):
             gather_a("V", t, False, 0, 0, 12)
             for b in (1, 3, 2):
                 gather_a("S", t, False, b)
-        for b in (0, 1, 3, 2):
+            spread_out("S")
+        for b in (0, 1, 3):
             gather_b(t, b)
-        quant("yt0 yt1 yt2 yt3", "yq", T.yq[:], T.ys[:], T.yt[:])
-        mm("upq ups yq", 4, T.upq[:, 0:128], T.ups[:, 0:128], T.yq[:], T.ys[:])
-        mm("upq ups yq", 5, T.upq[:, 128:256], T.ups[:, 128:256], T.yq[:], T.ys[:])
-        banks = (6, 7, 5, 6)
+        for h in range(2):
+            gather_b(t, 2, h, h + 1)
+            cs = slice(H * h, H * h + H)
+            quant("yt0%d yt1%d yt2%d yt3%d" % (h, h, h, h), "yq%d" % h, T.yq[:, cs], T.ys[:, cs], T.yt[:, 4 * H * h:4 * H * (h + 1)])
+            for k in range(2):
+                mm("upq ups yq%d" % h, 4 + 2 * h + k, T.upq[:, 128 * k:128 * k + 128], T.ups[:, 128 * k:128 * k + 128], T.yq[:, cs], T.ys[:, cs], H)
+            act("pb%d" % (4 + 2 * h), "sa%d" % h, T.sa[:, cs], T["pb%d" % (4 + 2 * h)][:, 0:H], FN.Copy)
+        banks = (5, 7, 4, 6)
 
         def layer(b):
-            mm("wq wsc yq", banks[b], T.wq[:, 128 * b:128 * b + 128], T.wsc[:, 128 * b:128 * b + 128], T.yq[:], T.ys[:])
+            mm("wq wsc yq0 yq1", banks[b], T.wq[:, 128 * b:128 * b + 128], T.wsc[:, 128 * b:128 * b + 128], T.yq[:], T.ys[:])
 
         def relu(b):
             act("pb%d" % banks[b], "rl%d" % b, T.rl[:, C * b:C * b + C], T["pb%d" % banks[b]][:, 0:C], FN.Relu, scale=0.03125)
@@ -355,38 +349,37 @@ def rank_program(g, core, T, topo):
         def add(b):
             tt("pb%d rl%d" % (b, b), "xt%d" % b, T.xt[:, b:4 * C:4], T["pb%d" % b][:, 0:C], T.rl[:, C * b:C * b + C], A.add)
 
-        layer(0)
+        if t == 0:
+            spread_out("S")
+            quant("kt", "kq", T.kq[:], T.ks[:], T.kt[:])
+        for h in range(2):
+            cs = slice(H * h, H * h + H)
+            tt("pb%d ct sa%d" % (5 + 2 * h, h), "ct%d" % h, T.ct[:, 4 * H * h:4 * H * (h + 1):4], T["pb%d" % (5 + 2 * h)][:, 0:H], T.sa[:, cs], A.is_gt)
+            quant("ct%d" % h, "cq%d" % h, T.cq[:, cs], T.cs[:, cs], T.ct[:, 4 * H * h:4 * H * (h + 1)])
+            if h == 0:
+                layer(0)
+            mm("kq cq%d" % h, 4 + 2 * h, T.kq[:], T.ks[:], T.cq[:, cs], T.cs[:, cs], H)
         layer(1)
-        for h in range(2):
-            act("pb4", "sa%d" % h, T.sa[:, 192 * h:192 * h + 192], T.pb4[:, 192 * h:192 * h + 192], FN.Copy)
-        ms("selfd selfd0 selfd1", T.selfd[:], NONE)
-        if t == 0:
-            late_constants()
-        else:
-            spread(t, "V")
-        for h in range(2):
-            tt("pb5 ct sa%d" % h, "ct%d" % h, T.ct[:, 768 * h:768 * h + 768:4], T.pb5[:, 192 * h:192 * h + 192],
-               T.sa[:, 192 * h:192 * h + 192], A.is_gt)
         relu(0)
-        relu(1)
-        quant("ct0 ct1", "cq", T.cq[:], T.cs[:], T.ct[:])
-        layer(2)
-        mm("kq cq", 4, T.kq[:], T.ks[:], T.cq[:], T.cs[:])
-        layer(3)
-        relu(2)
-        relu(3)
-        add(0)
         if t == 0:
-            ts("ones", "z32", T.z32[:], T.ones[:], 0.0, A.mult)
-        tr("pb4", "t32", T.t32[:], T.pb4[:, 0:C])
-        tt("t32 p8a p8b p8c p8d0 p8d1 p8d2 p8d3", "key", T.key[:], T.t32[:, 0:C:4], T.p8[:], A.add)
-        scan("key mseg", "ksc", T.ksc[:], T.mseg[:], T.key[:], -100.0, A.add, A.max)
+            act("cd0 cd1", "c_cd", cf[:, 304:352], cf[:, 256:304], FN.Copy, scale=LS)
+            act("c_x0", "c_x1", cf[:, c_xn:c_xn + 6], cf[:, c_xk:c_xk + 6], FN.Copy, scale=-1024.0)
+            ts("k6 kf", "k22", sc[:, 24:25], sc[:, 6:7], k_q, A.subtract, 4.0, A.add)
+        relu(1)
+        for h in range(2):
+            tr("pb%d" % (4 + 2 * h), "t32%d" % h, T.t32[:, H * h:H * h + H], T["pb%d" % (4 + 2 * h)][:, 0:H])
+            layer(2 + h)
+            tt("t32%d p8a p8b p8c p8d0 p8d1 p8d2 p8d3" % h, "key%d" % h, T.key[:, 48 * h:48 * h + 48], T.t32[:, H * h:H * h + H:4],
+               T.p8[:, 48 * h:48 * h + 48], A.add)
+        scan("key0 key1 mseg", "ksc", T.ksc[:], T.mseg[:], T.key[:], -100.0, A.add, A.max)
         k0, k7 = T.key[:, 0:96:4], T.ksc[:, 7:96:8]
-        ts("key", "s4", sm(4), k0, 4.0, A.is_lt, 1024.0, A.mult)
+        ts("key0 key1", "s4", sm(4), k0, 4.0, A.is_lt, 1024.0, A.mult)
         ts("ksc", "z32", T.z32[:, 0:C:32], k7, 7.0, A.subtract, 2048.0, A.mult)
-        ts("key", "s5", sm(5), k0, 7.0, A.is_ge, 2048.0, A.mult)
+        ts("key0 key1", "s5", sm(5), k0, 7.0, A.is_ge, 2048.0, A.mult)
         scan("z32 m32", "af", T.af[:], T.m32[:], T.z32[:], 0.0, A.mult, A.add)
-        ts("ksc", "s7", sm(7, 12), k7, 7.5, A.is_ge, NONE, A.mult)
+        act("ksc", "s7", sm(7, 12), k7, FN.Identity, scale=2.0 ** 34, bias=-(7.5 - 1.0 / LS) * 2.0 ** 34)
+        if t == 0:
+            ts("k22", "k23", sc[:, 25:26], sc[:, 24:25], 3, A.bitwise_and)
         tr("af", "ar", T.ar[:], T.af[:])
         tt("s4 s5", "s6", sm(6), sm(4), sm(5), A.add)
         rev = T.ar[:, ::-1]
@@ -394,9 +387,9 @@ def rank_program(g, core, T, topo):
         def differ(q, k):
             out = T.dd[:, C * k:C * k + C]
             if q == "S":
-                act("ar c_xn", "dd%d" % k, out, rev, FN.Abs, scale=1024.0, bias=cf[:, c_xn + k:c_xn + k + 1])
+                act("ar c_x1", "dd%d" % k, out, rev, FN.Abs, scale=1024.0, bias=cf[:, c_xn + k:c_xn + k + 1])
             else:
-                ts("ar c_xk", "dd%d" % k, out, rev, cf[:, c_xk + k:c_xk + k + 1], A.not_equal, 1024.0, A.mult)
+                ts("ar c_x0", "dd%d" % k, out, rev, cf[:, c_xk + k:c_xk + k + 1], A.not_equal, 1024.0, A.mult)
 
         def first(k):
             scan("dd%d ones" % k, "so%d" % k, T.so[:, C * k:C * k + C], T.ones[:], T.dd[:, C * k:C * k + C],
@@ -404,43 +397,45 @@ def rank_program(g, core, T, topo):
 
         for k in range(2, 6):
             differ("S", k)
-        differ("V", 0)
-        differ("V", 1)
-        for k in range(4):
+        for k in range(2):
+            differ("V", k)
+        if t == 0:
+            tt("k21 k23", "k28", cf[:, 414:415], sc[:, 25:26], sc[:, 26:27], A.add)
+        for k in range(5):
             first(k)
-        add(1)
-        first(4)
+        if t == 0:
+            ts("c_row k28", "lrel", T.lrel[:, 0:3], c_row[:, 0:24:8], cf[:, 414:415], A.add)
         tt("s6 pm", ks_ + "p", hs[:, 48:72], sm(6), T.pm[:], A.add)
         for e in range(2):
             a = cd(t, 1)
-            tt("s7 c_cd", "selfd%d" % e, T.selfd[:, own + e:own + 24:2], sm(7, 12), cf[:, a:a + 24:2], A.max)
+            tt("s7 c_cd selfd", "selfd%d" % e, T.selfd[:, 3 * own + e:3 * own + 24:2], sm(7, 12), cf[:, a:a + 24:2], A.max)
         first(5)
         sos = "so0 so1 so2 so3 so4 so5"
         base = float(C) if up[t] else 0.0
-        ts(sos, "rel0", T.rel[:, 0:6], T.so[:, C - 1:6 * C:C], base, A.add, LS, A.mult)
-        ts(sos, "rel1", T.rel[0:64, 6:12], T.so[64:128, C - 1:6 * C:C], base, A.add, LS, A.mult)
-        ts(sos, "rel2", T.rel[64:128, 6:12], T.so[0:64, C - 1:6 * C:C], base, A.add, LS, A.mult)
+        ts(sos, "rel0", T.rel[:, 0:24:4], T.so[:, C - 1:6 * C:C], base, A.add, LS, A.mult)
+        ts(sos, "rel1", T.rel[0:64, 2:24:4], T.so[64:128, C - 1:6 * C:C], base, A.add, LS, A.mult)
+        act(sos, "rel2", T.rel[64:128, 2:24:4], T.so[0:64, C - 1:6 * C:C], FN.Identity, scale=LS, bias=base * LS)
         for q in range(4):
             s = 32 * ((q + 1) % 4)
-            move("VS"[q // 3], "rel0 rel1 rel2", "rel%d" % (3 + q), T.rel[32 * q:32 * q + 32, 12:24], T.rel[s:s + 32, 0:12])
+            move("VS"[q // 2], "rel0 rel1 rel2", "rel%d" % (3 + q), T.rel[32 * q:32 * q + 32, 1:24:2], T.rel[s:s + 32, 0:24:2])
         tt("rel0 rel1 rel2 rel3 rel4 rel5 rel6 lrel selfd selfd0 selfd1", ks_ + "l", hs[:, 0:48],
-           T.rel[:].indirect(T.lrel[:, 0:3]), T.selfd[:], A.min)
+           T.rel[:].indirect(T.lrel[:, 0:3]), T.selfd[:, 2 * own:2 * own + 48], A.min)
+        relu(2)
+        relu(3)
         send(t, "h", ks_ + "l " + ks_ + "p", [(hr[:], hs[:])], kr)
-        add(2)
-        add(3)
+        for b in range(4):
+            add(b)
         exchange_x(t + 1, T.xt, "xt0 xt1 xt2 xt3")
-        ts("ksc", "s8", sm(8, 12), k7, 7.0, A.subtract, 2048.0, A.mult)
+        act("ksc", "s8", sm(8, 12), k7, FN.Identity, scale=2048.0, bias=-14336.0)
         ts("s6", "s9", sm(9), sm(6), 0.0, A.is_equal, LS, A.mult)
         if t == 0:
-            ms("wrc", T.wr[:, 2 * C:2 * C + 32], 0.0)
-            ms("ovi0 ovi1", T.ovi[:], 0.0)
-            quant("vt", "vq", T.vq[:], T.vs[:], T.vt[:])
+            ts("c_row k9", "lfin", T.lfin[:], c_row[:, 0:16:8], cf[:, 408:409], A.add)
+            cp("c_row", "lrep", T.lrep[:], c_row[:, 0:48])
         tt("s8 cd0 cd1", "s10", sm(10, 12), sm(8, 12), cf[:, cd(t, 0):cd(t, 0) + 24:2], A.subtract)
-        ts("s9", "s11", sm(11), sm(9), 1024.0, A.subtract)
+        act("s9", "s11", sm(11), sm(9), FN.Identity, bias=-1024.0)
         if t < 2:
             decode(t + 1, True)
-            for b in range(2):
-                unload("S", t + 1, True, b)
+            unload("S", t + 1, True, 0)
         else:
             mm("vq xq3", 4, T.vq[:], T.vs[:], T.xq3[:], T.xs3[:])
             dma("Y", "xq3", "", T.oc[:], u8(T.xq3[:]), "st")
@@ -454,8 +449,8 @@ def rank_program(g, core, T, topo):
         tt(both, "low", T.low[:], hs[:, 0:48], hr[:, 0:48], A.min)
         tt(both + " low", "wb0", T.wb[:, 0:24], T.low[:, 0:24], lo_pf[:, 48:72], A.add)
         tt(both + " low", "wb1", T.wb[:, 24:48], T.low[:, 24:48], up_pf[:, 48:72], A.add)
-        for h in range(2):
-            act("lrep wb%d" % h, "wf%d" % h, T.wf[:, C * h:C * h + C], T.wb[:, 24 * h:24 * h + 24].indirect(T.lrep[:]), FN.Copy)
+        act("lrep wb0", "wf0", T.wf[:, 0:C], T.wb[:, 0:24].indirect(T.lrep[:, 0:24]), FN.Copy)
+        act("lrep wb0 wb1", "wf1", T.wf[:, C:2 * C], T.wb[:].indirect(T.lrep[:, 24:48]), FN.Copy)
         tt("low c_cd", "s12", sm(12), lown, cf[:, cd(t, 1):cd(t, 1) + 24], A.is_equal)
         ts("low", "s13", sm(13), lown, 1.0 / LS, A.mult)
         tt("s12 s10", "s14", sm(14, 12), T.sm[:, 24 * 12:24 * 13:2], sm(10, 12), A.mult)
@@ -470,13 +465,13 @@ def rank_program(g, core, T, topo):
         steps[2]()
         tt("s15 s16", "s18", sm(18), sm(15), sm(16), A.add)
         to_list("cand")
-        tt("s17 low", "s19", sm(19), sm(17), lown, A.add)
         tr("wf1", "wr1", T.wr[:, C:2 * C], T.wf[:, C:2 * C])
-        act("wr0 wr1 wrc cand", "gv1", T.gv[:, 192:C], T.wr[:].indirect(T.cand[:, 12:24]), FN.Copy)
-        cp("wr0 wr1 wrc cand", "gv0", T.gv[:, 0:192], T.wr[:].indirect(T.cand[:, 0:12]))
+        tt("s17 low", "s19", sm(19), sm(17), lown, A.add)
+        act("wr0 wr1 wrc cand", "gv1", T.gv[:, H:C], T.wr[:].indirect(T.cand[:, 12:24]), FN.Copy)
+        cp("wr0 wr1 wrc cand", "gv0", T.gv[:, 0:H], T.wr[:].indirect(T.cand[:, 0:12]))
         if t < 2:
             decode(t + 1, False)
-            for mine, b in ((True, 3), (True, 2), (False, 0), (False, 1), (False, 3), (False, 2)):
+            for mine, b in ((True, 1), (True, 3), (True, 2), (False, 0), (False, 1), (False, 3), (False, 2)):
                 unload("S", t + 1, mine, b)
         tr("gv0 gv1", "vt32", T.vt32[:], T.gv[:])
         v = T.vt32[:, 0:C:16]
@@ -499,17 +494,18 @@ def rank_program(g, core, T, topo):
             break
         for e in range(2):
             tt("s3 s23", "swi%d" % e, T.swi[:, 32 * e:32 * e + 12], T.sm[:, 72 + e:96:2], T.sm[:, 552 + e:576:2], A.add)
-        tt("s3 s23", "pm", T.pm[:], sm(3), sm(23), A.add)
         steps[0]()
+        tt("s3 s23", "pm", T.pm[:], sm(3), sm(23), A.add)
         steps[1]()
         steps[2]()
         name = "pl%d" % (t + 1)
         to_list(name)
         send(t + 1, "p", name, [(T["plp%d" % (t + 1)][:], T[name][:, 0:24])], "plp%d" % (t + 1))
-        for b in (0, 1, 3):
-            gather_a("V", t + 1, True, b)
+        for b in (0, 1, 3, 2):
+            gather_a("VS"[b // 2], t + 1, True, b)
             double("G", t + 1, b)
-        gather_a("S", t + 1, True, 2)
-        double("G", t + 1, 2)
+        spread(t + 1)
+        if t == 0:
+            quant("vt", "vq", T.vq[:], T.vs[:], T.vt[:])
 
     wait("G", list(count.items()))

@@ -3,9 +3,13 @@ from concourse.mybir import dt, AluOpType, ActivationFunctionType
 C = 384
 H = C // 2
 STEP = [1, 2, 4]
-Q8, U8, BF, F32, F16, I32, U16 = "float8_e4m3fn_x4", "uint8", "bfloat16", "float32", "float16", "int32", "uint16"
-LS = 4096.0
+Q8, U8, BF, F32, I32, U16 = "float8_e4m3fn_x4", "uint8", "bfloat16", "float32", "int32", "uint16"
+LS = 2048.0
+Z = 2048 * LS
 NONE = 768 * LS
+BIG = 16384.0
+CYCLE, SAME, OTHER, SLACK = 0.86e-3, 0.19, 0.1, 0.01
+ISSUE, FIRST, LOAD, LOADX, NOTE, CODES = 0.2, 2.0, 1.8, 2.6, 1.8, 2.8
 
 
 def sb(n, d):
@@ -13,24 +17,23 @@ def sb(n, d):
 
 
 SCRATCH = {
-    "xin": sb(4 * C, BF), "xt": sb(4 * C, BF), "yt": sb(4 * C, BF), "ct": sb(4 * C, BF),
-    "ut": sb(512, BF), "vt": sb(512, BF), "e0": sb(528, BF), "et": sb(2048, BF), "kt": sb(512, BF),
-    "uq": sb(128, Q8), "us": sb(128, U8), "upq": sb(256, Q8), "ups": sb(256, U8),
+    "xin": sb(4 * C, BF), "xt": sb(4 * C, BF), "yt": sb(4 * C, BF),
+    "ut": sb(512, BF), "vt": sb(512, BF), "e0": sb(528, BF), "et": sb(2048, BF),
+    "uq": sb(128, Q8), "us": sb(128, U8), "upq": sb(128, Q8), "ups": sb(128, U8),
     "vq": sb(128, Q8), "vs": sb(128, U8), "eq": sb(512, Q8), "es": sb(512, U8),
-    "kq": sb(128, Q8), "ks": sb(128, U8), "wq": sb(512, Q8), "wsc": sb(512, U8),
-    "yq": sb(C, Q8), "ys": sb(C, U8), "cq": sb(C, Q8), "cs": sb(C, U8),
+    "wq": sb(512, Q8), "wsc": sb(512, U8), "yq": sb(C, Q8), "ys": sb(C, U8),
     "fw": sb(4 * 2 * C, BF), "aw": sb(4 * 2 * C, BF), "ac": sb(4 * C, BF),
-    "sa": sb(C, F32), "rl": sb(4 * C, F32), "yo": sb(C, F32),
-    "vgi": sb(24, I32), "t32": sb(C, F32), "key": sb(96, F32), "ksc": sb(96, F32), "p8": sb(96, F32),
-    "z32": sb(C, F16), "m32": sb(C, BF), "af": sb(C, F16), "ar": sb(C, F16),
-    "dd": sb(6 * C, BF), "ones": sb(C, BF), "so": sb(6 * C, F16), "rel": sb(24, F32), "selfd": sb(96, F32),
-    "low": sb(48, F32), "wb": sb(48, F32), "wf": sb(2 * C, F32),
-    "wr": sb(2 * C + 32, F32), "gv": sb(C, F32), "vt32": sb(C, F32), "vi": sb(48, I32),
-    "sm": sb(28 * 24, F32), "pm": sb(24, F32), "mseg": sb(96, F32),
-    "swi": sb(64, F32), "swx": sb(64, F32), "swz": sb(64, F32), "swo": sb(64, F32), "cand": sb(32, U16),
+    "sa": sb(192, F32), "cb": sb(192, BF), "sign": sb(192, BF), "pk": sb(192, BF), "rl": sb(4 * C, F32), "yo": sb(C, F32),
+    "vgi": sb(24, I32), "ksc": sb(24, F32), "p8": sb(96, F32), "ag": sb(96, F32),
+    "rp": sb(96, F32), "rt": sb(96, F32), "same": sb(288, BF), "mdup": sb(288, BF), "dup": sb(288, BF),
+    "val": sb(48, BF), "tab": sb(1024 + 2 * C, BF), "tb": sb(2 * C, BF), "ce": sb(192, F32), "oe": sb(96, F32), "rel": sb(24, F32),
+    "low": sb(48, F32), "sbz": sb(96, F32), "dpn": sb(96, F32), "dps": sb(96, F32), "wf": sb(2 * C, F32),
+    "wr": sb(2 * C + 32, F32), "gv": sb(C, F32), "vt32": sb(544, F32),
+    "sm": sb(16 * 32, F32), "s0": sb(96, F32), "s1": sb(96, F32), "npt": sb(72, F32), "xo": sb(32, F32),
+    "swi": sb(64, F32), "swx": sb(64, F32), "swz": sb(64, F32), "swo": sb(64, F32), "cand": sb(24, U16),
     "ovi": sb(32, F32), "ovo": sb(32, F32),
-    "ci": sb(448, I32), "sc": sb(32, I32), "cf": sb(512, F32), "kk": sb(256, F32), "lu": sb(16, U16),
-    "lsw": sb(4, U16), "lfin": sb(2, U16), "lrep": sb(48, U16), "lrel": sb(4, U16),
+    "sc": sb(16, I32), "cf": sb(768, F32), "kk": sb(32, F32), "lu": sb(8, U16),
+    "lsw": sb(4, U16), "lv": sb(2, U16), "lrp": sb(6, U16), "l8": sb(2, U16), "la": sb(2, U16), "off": sb(4, U16), "pp": sb(32, U16),
 }
 for _t in range(4):
     SCRATCH["xq%d" % _t] = sb(C, Q8)
@@ -38,14 +41,13 @@ for _t in range(4):
 for _t in range(3):
     SCRATCH["lq%d" % _t] = sb(C, Q8)
     SCRATCH["ls%d" % _t] = sb(C, U8)
-    SCRATCH["pl%d" % _t] = sb(32, U16)
+    SCRATCH["pl%d" % _t] = sb(24, U16)
     SCRATCH["plp%d" % _t] = sb(24, U16)
-    SCRATCH["h1s%d" % _t] = sb(72, F32)
-    SCRATCH["h1r%d" % _t] = sb(72, F32)
+    SCRATCH["hb%d" % _t] = sb(144, F32)
 for _b in range(8):
     SCRATCH["pb%d" % _b] = ("psum", [128, 512], F32)
 
-SEMAPHORES = (["sV", "sS", "sP", "sG", "sent", "st"] + ["ld%d" % i for i in range(7)]
+SEMAPHORES = (["sV", "sS", "sP", "sG", "sent", "sent0", "st"] + ["ld%d" % i for i in range(7)]
               + ["a%s%d" % (k, t) for k in "xph" for t in range(3)])
 
 A = AluOpType
@@ -57,455 +59,510 @@ def rank_program(g, core, T, topo):
     if rank is None:
         return
     eng = {"V": g.vector, "S": g.scalar, "P": g.tensor, "G": g, "Y": g.sync}
-    count, known, wrote, read = {}, {q: {} for q in eng}, {}, {}
+    nodes, wrote, read, total = [], {}, {}, {}
 
-    def wait(q, toks):
-        need = {}
-        for s, n in toks:
-            if n > need.get(s, 0):
-                need[s] = n
-        for s, n in need.items():
-            if known[q].get(s, 0) < n:
-                eng[q].wait_ge(T.sem[s], n)
-                known[q][s] = n
+    def node(q, busy, lat, deps, call=None, sem=None, inc=0):
+        nodes.append(dict(q=q, busy=busy, lat=lat, deps=sorted(deps), call=call, sem=sem, inc=inc))
+        return len(nodes) - 1
 
-    def op(q, r, w, call, sem=None, inc=1):
+    def op(q, r, w, call, busy, lat=None, sem=None, inc=1):
         r, w = r.split(), w.split()
-        toks = [wrote[k] for k in r + w if k in wrote]
+        deps = {wrote[k] for k in r + w if k in wrote}
         for k in w:
-            toks += read.get(k, [])
+            deps |= set(read.get(k, []))
         for k in r:
             if k.startswith("pb"):
-                toks += [x for x in read.get(k, []) if x[0] != "s" + q]
-        wait(q, toks)
-        sem = sem or "s" + q
-        count[sem] = count.get(sem, 0) + inc
-        call().then_inc(T.sem[sem], inc)
+                deps |= {x for x in read.get(k, []) if nodes[x]["q"] != q}
+        n = node(q, busy, lat or busy, deps, call, sem or "s" + q, inc)
         for k in r:
-            read.setdefault(k, []).append((sem, count[sem]))
+            read.setdefault(k, []).append(n)
         for k in w:
-            wrote[k] = (sem, count[sem])
+            wrote[k] = n
             read[k] = []
 
+    def ap(a):
+        return a[0].indirect(a[1]) if isinstance(a, tuple) else a
+
+    def cycles(out, ins, per=None):
+        if isinstance(out, tuple):
+            return 0.06 + 4 * CYCLE * 16 * out[1].shape[1]
+        if isinstance(ins[0], tuple):
+            return 0.06 + 1.6 * CYCLE * 16 * ins[0][1].shape[1]
+        if per is None:
+            per = 0.5 if all(a.dtype in (dt.bfloat16, dt.uint16) for a in [out] + ins) else 1.0
+        return 0.01 + CYCLE * max(64, per * out.shape[1])
+
     def tt(r, w, out, a, b, o):
-        op("V", r, w, lambda: g.vector.tensor_tensor(out, a, b, o))
+        op("V", r, w, lambda: g.vector.tensor_tensor(out, ap(a), b, o), cycles(out, [a], 1.0 if "pb" in r else 2.0))
 
     def ts(r, w, out, a, s1, o1, s2=None, o2=None):
         if o2 is None:
-            op("V", r, w, lambda: g.vector.tensor_scalar(out, a, s1, None, o1))
+            op("V", r, w, lambda: g.vector.tensor_scalar(out, ap(a), s1, None, o1), cycles(out, [a]))
         else:
-            op("V", r, w, lambda: g.vector.tensor_scalar(out, a, s1, s2, o1, o2))
+            op("V", r, w, lambda: g.vector.tensor_scalar(out, ap(a), s1, s2, o1, o2), cycles(out, [a]))
 
     def cp(r, w, out, a):
-        op("V", r, w, lambda: g.vector.tensor_copy(out, a))
+        op("V", r, w, lambda: g.vector.tensor_copy(ap(out), ap(a)), cycles(out, [a]))
 
     def tr(r, w, out, a):
-        op("V", r, w, lambda: g.vector.transpose(out, a))
+        op("V", r, w, lambda: g.vector.transpose(out, a), cycles(out, [a]))
 
     def ms(w, out, v):
-        op("V", "", w, lambda: g.vector.memset(out, v))
+        op("V", "", w, lambda: g.vector.memset(out, v), cycles(out, [out]))
 
     def scan(r, w, out, a, b, init, o0, o1):
-        op("V", r, w, lambda: g.vector.tensor_tensor_scan(out, a, b, init, o0, o1))
+        op("V", r, w, lambda: g.vector.tensor_tensor_scan(out, a, b, init, o0, o1), cycles(out, [a, b]))
 
     def quant(r, w, q, s, t):
-        op("V", r, w, lambda: g.vector.quantize_mx(q, s, t))
+        op("V", r, w, lambda: g.vector.quantize_mx(q, s, t), 0.02 + 0.22e-3 * t.shape[1])
 
     def act(r, w, out, a, fn, **kw):
-        op("S", r, w, lambda: g.scalar.activation(out, a, fn, **kw))
+        op("S", r, w, lambda: g.scalar.activation(out, ap(a), fn, **kw), cycles(out, [a], 1.0))
+
+    def affine(r, w, out, a, k, b):
+        act(r, w, out, a, FN.Identity, scale=k, bias=b)
 
     def move(q, r, w, out, a, k=1.0):
         if q == "S":
             act(r, w, out, a, FN.Copy, scale=k)
+        elif k == 1.0:
+            cp(r, w, out, a)
         else:
             ts(r, w, out, a, k, A.mult)
 
     def mm(r, bank, wq, ws, xq, xs, n=C):
-        op("P", r, "pb%d" % bank, lambda: g.tensor.matmul_mx(T["pb%d" % bank][:, 0:n], wq, ws, xq, xs, True, True))
+        op("P", r, "pb%d" % bank, lambda: g.tensor.matmul_mx(T["pb%d" % bank][:, 0:n], wq, ws, xq, xs, True, True), 0.07 + 0.75 * CYCLE * n)
 
-    def iota(w, out, pattern, base, cm):
-        op("G", "", w, lambda: g.iota(out, pattern, base, cm, allow_small_or_imprecise_dtypes=True))
+    def iota(w, out, pattern, base, cm=0):
+        op("G", "", w, lambda: g.iota(out, pattern, int(base), cm, allow_small_or_imprecise_dtypes=True), 0.14 + 2 * CYCLE * out.shape[1])
 
-    def fill(w, out, n, v):
-        iota(w, out, [[0, n]], v, 0)
+    def fill(w, out, v):
+        iota(w, out, [[0, out.shape[1]]], v)
 
-    def dma(q, r, w, out, a, sem):
-        op(q, r, w, lambda: eng[q].dma_start(out, a), sem, 16)
+    def select(r, w, out, a, pattern, cmp, other, base=0):
+        op("G", r, w, lambda: g.affine_select(out, a, pattern, cmp, other, base, 0), 0.18 + 2 * CYCLE * out.shape[1])
 
-    def send(t, kind, r, pairs, lands):
+    def dma(q, r, w, out, a, sem, lat=LOAD):
+        op(q, r, w, lambda: eng[q].dma_start(out, a), ISSUE, lat, sem, 16)
+
+    def send(t, kind, r, pairs, lands, flight, sent="sent", left=None):
         dst = T.cores[rank ^ STEP[t]]
         rid, pid, _ = topo.addr(dst)
         sem = "a%s%d" % (kind, t)
-        wait("G", [wrote[k] for k in r.split()])
+        calls = []
         for out, a in pairs:
-            g.remote_dma(out, a, T.sem[sem], T.sem.sent, pid, rid, topo.mask(core, dst))
-            count["sent"] = count.get("sent", 0) + len(topo.engines(core, dst))
-        count[sem] = len(pairs) * len(topo.engines(dst, core))
-        wrote[lands] = (sem, count[sem])
+            def call(out=out, a=a):
+                g.remote_dma(out, a, T.sem[sem], T.sem[sent], pid, rid, topo.mask(core, dst))
+            busy = ISSUE if total else FIRST
+            calls.append(node("G", busy, busy, {wrote[k] for k in r.split()} | set(calls), call))
+            total[sent] = total.get(sent, 0) + len(topo.engines(core, dst))
+        total[sem] = len(pairs) * len(topo.engines(dst, core))
+        wrote[lands] = node(None, 0.0, flight, calls[-1:], None, sem)
+        wrote["out" + kind] = calls[-1]
+        if left:
+            wrote[left] = node(None, 0.0, flight - 1.0, calls[-1:], None, sent)
+
+    def issue():
+        def gap(d, n):
+            a, b = nodes[d]["q"], nodes[n]["q"]
+            return 0.0 if a is None or b is None or nodes[d]["sem"] is None else SAME if a == b else OTHER
+
+        before = [[(d, gap(d, n)) for d in x["deps"]] for n, x in enumerate(nodes)]
+        after = [[] for x in nodes]
+        for n, e in enumerate(before):
+            for d, k in e:
+                after[d].append((n, k))
+
+        def lay(urgent, back):
+            pre, post = (after, before) if back else (before, after)
+            need = [len(e) for e in pre]
+            ready, at, taken = {n for n, k in enumerate(need) if k == 0}, {}, {q: [] for q in eng}
+            while ready:
+                n = min(ready, key=lambda n: (urgent[n], n))
+                ready.remove(n)
+                x = nodes[n]
+                shift = x["lat"] - x["busy"] if back else 0.0
+                s = max([0.0] + [at[d] + nodes[d]["lat"] + k for d, k in pre[n]]) + shift
+                if x["q"]:
+                    for a, b in taken[x["q"]]:
+                        if s + x["busy"] <= a + SLACK:
+                            break
+                        s = max(s, b)
+                    taken[x["q"]].append((s, s + x["busy"]))
+                    taken[x["q"]].sort()
+                at[n] = s - shift
+                for m, k in post[n]:
+                    need[m] -= 1
+                    if need[m] == 0:
+                        ready.add(m)
+            end = max(at[n] + x["lat"] for n, x in enumerate(nodes))
+            return [end - at[n] - x["lat"] if back else at[n] for n, x in enumerate(nodes)]
+
+        start = lay(lay([-n for n in range(len(nodes))], True), False)
+        count, known, token = dict(total), {q: {} for q in eng}, {}
+
+        def wait(q, toks):
+            need = {}
+            for s, k in toks:
+                need[s] = max(need.get(s, 0), k)
+            for s, k in need.items():
+                if known[q].get(s, 0) < k:
+                    eng[q].wait_ge(T.sem[s], k)
+                    known[q][s] = k
+
+        for n in sorted(range(len(nodes)), key=lambda n: (start[n], n)):
+            x = nodes[n]
+            if x["q"] is None:
+                token[n] = (x["sem"], total[x["sem"]])
+                continue
+            wait(x["q"], [token[d] for d in x["deps"] if d in token])
+            if x["sem"] is None:
+                x["call"]()
+            else:
+                count[x["sem"]] = count.get(x["sem"], 0) + x["inc"]
+                x["call"]().then_inc(T.sem[x["sem"]], x["inc"])
+                token[n] = (x["sem"], count[x["sem"]])
+        wait("G", list(count.items()))
 
     def u8(v):
         return v.bitcast(dt.uint8)
 
     def sm(i, n=24):
-        return T.sm[:, 24 * i:24 * i + n]
+        return T.sm[:, 32 * i:32 * i + n]
 
-    up = [(rank & s) != 0 for s in STEP]
-    cf, ci, sc = T.cf, T.ci, T.sc
-    c_row, c_gm, c_xk, c_xn, c_p = cf[:, 0:128], cf[:, 352:376], 376, 384, cf[:, 392:393]
-    k_i, k_j, k_r, k_15, k_q, k_odd, k_h, k_8 = (cf[:, 400 + k:401 + k] for k in range(8))
+    up = [int((rank & s) != 0) for s in STEP]
+    cf, sc = T.cf, T.sc
 
-    def cd(t, big):
-        return 256 + 24 * (2 * big + int(up[t]))
+    def col(k):
+        return cf[:, k:k + 1]
 
-    def exchange_x(t, tile, keys):
-        xq, xs = T["xq%d" % t], T["xs%d" % t]
-        quant(keys, "xq%d" % t, xq[:], xs[:], tile[:])
-        if t < 3:
-            send(t, "x", "xq%d" % t, [(u8(T["lq%d" % t][:]), u8(xq[:])), (T["ls%d" % t][:], xs[:])], "lq%d" % t)
+    c_row, c_gm, c_ys, th7, th4 = cf[:, 0:128], cf[:, 352:376], cf[:, 304:352], cf[:, 480:504], cf[:, 504:528]
+    k_j, k_r, k_15, k_q, k_8, k_g, k_odd, c_p = (col(400 + k) for k in range(8))
+    cx = "c_x0 c_x1 c_x2 c_x3"
+    wfk = "wfa wfb wfc wfd wfe wff wfg"
 
-    def decode(t, mine):
-        q, s = ("xq%d" % t, "xs%d" % t) if mine else ("lq%d" % t, "ls%d" % t)
-        for b in (0, 1, 3, 2):
-            mm("eq " + q, b + (0 if mine else 4), T.eq[:, 128 * b:128 * b + 128], T.es[:, 128 * b:128 * b + 128], T[q][:], T[s][:])
+    def c_y(t):
+        return cf[:, 256 + 24 * up[t]:280 + 24 * up[t]]
+
+    def c_x(t, k, n=32):
+        a = 576 + 32 * up[t] + 64 * k
+        return cf[:, a:a + n]
+
+    def c_8(u, k):
+        a = 128 + 24 * u + 48 * k
+        return cf[:, a:a + 24]
+
+    def pd(t, k):
+        a = 24 + 48 * up[t] + k
+        return T["hb%d" % t][:, a:a + 47:2]
+
+    def quant_x(t, h, tile, keys):
+        quant(keys, "xq%d%d" % (t, h), T["xq%d" % t][:, H * h:H * h + H], T["xs%d" % t][:, H * h:H * h + H], tile[:, 4 * H * h:4 * H * (h + 1)])
+
+    def send_x(t, r="", sent="sent", left=None):
+        send(t, "x", "xq%d0 xq%d1 " % (t, t) + r, [(u8(T["lq%d" % t][:]), u8(T["xq%d" % t][:])), (T["ls%d" % t][:], T["xs%d" % t][:])],
+             "lq%d" % t, CODES, sent, left)
 
     def half(t, mine):
         return C * int(up[t] == mine)
 
-    def unload(q, t, mine, b):
-        bank = b + (0 if mine else 4)
-        a = 2 * C * b + half(t, mine)
-        move(q, "pb%d" % bank, "fw%d%d" % (b, mine), T.fw[:, a:a + C], T["pb%d" % bank][:, 0:C], 0.5)
+    def unpack(t, mine, queues):
+        q, s = ("xq%d" % t, "xs%d" % t) if mine else ("lq%d" % t, "ls%d" % t)
+        for b, e in zip((0, 1, 3, 2), queues):
+            bank, a = b + (0 if mine else 4), 2 * C * b + half(t, mine)
+            mm("eq %s0 %s1" % (q, q) if mine else "eq " + q, bank, T.eq[:, 128 * b:128 * b + 128], T.es[:, 128 * b:128 * b + 128], T[q][:], T[s][:])
+            move(e, "pb%d" % bank, "fw%d%d" % (b, mine), T.fw[:, a:a + C], T["pb%d" % bank][:, 0:C], 0.5)
+
+    def plane(buf, b):
+        return buf[:, 2 * C * b:2 * C * (b + 1)]
 
     def gather_a(q, t, mine, b, lo=0, hi=24):
         name = ("pl%d" if mine else "plp%d") % t
         a = 2 * C * b + half(t, mine)
-        win = T.fw[:, 2 * C * b:2 * C * (b + 1)].indirect(T[name][:, lo:hi])
-        out = T.aw[:, a + 16 * lo:a + 16 * hi]
-        r = "fw%d0 fw%d1 %s" % (b, b, name)
         w = " ".join("aw%d%d%d" % (b, mine, k) for k in range(lo // 12, hi // 12))
-        if q == "S":
-            act(r, w, out, win, FN.Copy)
-        else:
-            cp(r, w, out, win)
+        move(q, "fw%d0 fw%d1 %s" % (b, b, name), w, T.aw[:, a + 16 * lo:a + 16 * hi], (plane(T.fw, b), T[name][:, lo:hi]))
 
     def double(q, t, b):
         a = 2 * C * b + half(t, True)
         r, w, out, src = "aw%d10 aw%d11" % (b, b), "ac%d" % b, T.ac[:, C * b:C * b + C], T.aw[:, a:a + C]
         if q == "G":
-            op("G", r, w, lambda: g.affine_select(out, src, [[0, C]], A.is_gt, 0.0, 1, 0))
+            select(r, w, out, src, [[0, C]], A.is_gt, 0.0, 1)
         else:
             move(q, r, w, out, src)
 
-    def gather_b(t, b, lo=0, hi=2):
-        r = " ".join("aw%d%d%d" % (b, m, k) for m in range(2) for k in range(2)) + " pl%d ac%d" % (t, b)
-        tt(r, " ".join("yt%d%d" % (b, h) for h in range(lo, hi)), T.yt[:, 4 * H * lo + b:4 * H * hi:4],
-           T.aw[:, 2 * C * b:2 * C * (b + 1)].indirect(T["pl%d" % t][:, 12 * lo:12 * hi]), T.ac[:, C * b + H * lo:C * b + H * hi], A.add)
+    def gather_b(t, b, lo=0, hi=3):
+        if t == 0:
+            r, win, lst = "fw%d0 fw%d1 pp" % (b, b), plane(T.fw, b), T.pp
+        else:
+            r, win, lst = " ".join("aw%d%d%d" % (b, m, k) for m in range(2) for k in range(2)) + " pl%d" % t, plane(T.aw, b), T["pl%d" % t]
+        tt(r + " ac%d" % b, " ".join("yt%d%d" % (b, k) for k in range(lo, hi)), T.yt[:, 512 * lo + b:512 * hi:4],
+           (win, lst[:, 8 * lo:8 * hi]), T.ac[:, C * b + 128 * lo:C * b + 128 * hi], A.add)
 
-    steps = [lambda: tr("swi0 swi1", "swx", T.swx[:], T.swi[:]),
-             lambda: cp("swx lsw", "swz", T.swz[:], T.swx[:].indirect(T.lsw[:])),
-             lambda: tr("swz", "swo", T.swo[:], T.swz[:])]
+    def to_block(r, a, b):
+        cp(r, "swi0", T.swi[:, 0:12], a)
+        cp(r, "swi1", T.swi[:, 32:44], b)
+        tr("swi0 swi1", "swx", T.swx[:], T.swi[:])
+        cp("swx lsw0 lsw1", "swz", T.swz[:], (T.swx[:], T.lsw[:]))
+        tr("swz", "swo", T.swo[:], T.swz[:])
 
-    def to_list(name):
-        cp("swo lfin", name, T[name][:], T.swo[:].indirect(T.lfin[:]))
+    def look_up():
+        tr(wfk, "wr", T.wr[:, 0:2 * C], T.wf[:])
+        act("wr wrc cand", "gv1", T.gv[:, H:C], (T.wr[:], T.cand[:, 12:24]), FN.Copy)
+        cp("wr wrc cand", "gv0", T.gv[:, 0:H], (T.wr[:], T.cand[:, 0:12]))
+        for h in range(2):
+            tr("gv%d" % h, "vt%d" % h, T.vt32[:, H * h:H * h + H], T.gv[:, H * h:H * h + H])
+        return T.vt32[:], T.lv[:]
 
-    def spread(t):
-        tt("pm cd0 cd1", "s24", sm(24), T.pm[:], cf[:, cd(t, 0):cd(t, 0) + 24], A.is_equal)
-        tt("pm c_gm", "s25", sm(25), T.pm[:], c_gm, A.add)
-        ts("s24", "s26", sm(26), sm(24), 1024.0, A.mult)
-        tt("s25 s26", "s27", sm(27), sm(25), sm(26), A.add)
-
-    def spread_out(e):
-        k = 1.0 / 2048
-        move(e, "s27", "p8a", T.p8[:, 0:96:4], sm(27), k)
-        move(e, "s27", "p8b", T.p8[0:64, 2:96:4], T.sm[64:128, 648:672], k)
-        move(e, "s27", "p8c", T.p8[64:128, 2:96:4], T.sm[0:64, 648:672], k)
+    def spread(buf, k):
+        move("S", k + "a", k + "b", buf[0:64, 2:96:4], buf[64:128, 0:96:4])
+        move("S", k + "a", k + "c", buf[64:128, 2:96:4], buf[0:64, 0:96:4])
         for q in range(4):
             s = 32 * ((q + 1) % 4)
-            move(e, "p8a p8b p8c", "p8d%d" % q, T.p8[32 * q:32 * q + 32, 1:96:2], T.p8[s:s + 32, 0:96:2])
+            move("S", "%sa %sb %sc" % (k, k, k), "%s%d" % (k, q), buf[32 * q:32 * q + 32, 1:96:2], buf[s:s + 32, 0:96:2])
+        return " ".join(k + x for x in "abc0123")
 
+    def own_pointers(t):
+        pm = "pm%d0 pm%d1" % (t, t)
+        for e in range(2):
+            cp("swo", "pm%d%d" % (t, e), pd(t, 1)[:, e:24:2], T.swo[:, 32 * e:32 * e + 12])
+        tt(pm + " cd0 cd1", "s0", sm(0), pd(t, 1), c_y(t), A.is_equal)
+        tt(pm + " c_gm", "s1", sm(1), pd(t, 1), c_gm, A.add)
+        ts("s0", "s2", sm(2), sm(0), 1024.0, A.mult)
+        tt("s1 s2", "p8a", T.p8[:, 0:96:4], sm(1), sm(2), A.add)
+        ts(spread(T.p8, "p8") + " l8", "s3", sm(3, 32), (T.p8[:], T.l8[:]), 1.0 / BIG, A.mult)
+        tt("s3", "d8", sm(4, 23), sm(3, 23), T.sm[:, 97:120], A.subtract)
+        affine("s3", "d8", T.sm[:, 135:152:8], T.sm[:, 103:120:8], 1.0, -0.5)
+
+    def none_local(u):
+        return NONE - (128 + C * u) * LS
+
+    dma("S", "", "xin0", T.xin[:, 0:4 * H], T.x[:, 0:4 * H], "ld2", LOADX)
     dma("Y", "", "vgi", T.vgi[:], T.vg[:], "ld0")
-    dma("Y", "", "xin0", T.xin[:, 0:768], T.x[:, 0:768], "ld1")
-    dma("S", "", "xin1", T.xin[:, 768:1536], T.x[:, 768:1536], "ld2")
-    wait("Y", [wrote["xin0"]])
-    dma("Y", "", "ut", T.ut[:], T.u[:], "ld3")
-    dma("Y", "", "wq", u8(T.wq[:]), T.wc[:], "ld4")
-    dma("Y", "", "wsc", T.wsc[:], T.ws[:], "ld5")
-    dma("Y", "", "vt", T.vt[:], T.v[:], "ld6")
+    dma("Y", "", "xin1", T.xin[:, 4 * H:4 * C], T.x[:, 4 * H:4 * C], "ld1", LOADX)
+    cp("vgi", "pl0", T.pl0[:], T.vgi[:])
+    send(0, "p", "pl0", [(T.plp0[:], T.pl0[:])], "plp0", NOTE)
+    for h in range(2):
+        quant_x(0, h, T.xin, "xin%d" % h)
+    send_x(0, "outp", "sent0", "left")
+    dma("Y", "left", "ut", T.ut[:], T.u[:], "ld3")
+    dma("Y", "left", "wq", u8(T.wq[:]), T.wc[:], "ld4", LOADX)
+    dma("Y", "left", "wsc", T.wsc[:], T.ws[:], "ld5")
+    dma("Y", "left", "vt", T.vt[:], T.v[:], "ld6")
 
-    ip = ci[:, 128:129]
+    ip = sc[:, 7:8]
     iota("i_p", ip, [[1, 1]], 0, 1)
-    iota("c_row", c_row, [[1, 128]], 0, 0)
-    iota("c_p", c_p, [[1, 1]], 0, 1)
-    iota("i_sw", ci[:, 312:316], [[16, 2], [32, 2]], 0, 0)
-    iota("i_cd", cf[:, 432:456], [[32, 12], [0, 2]], 0, 0)
-    iota("i_e", cf[:, 456:480], [[0, 12], [2048, 2]], 0, 0)
-    iota("i_16", ci[:, 304:312], [[0, 8]], 16, 0)
-    iota("c_x0", cf[:, c_xk:c_xk + 6], [[128, 6]], 0, 1)
+    iota("c_row", c_row, [[1, 128]], 0)
+    for k, ops in enumerate(((7, A.bitwise_and), (31, A.bitwise_and), (15, A.bitwise_and), (5, A.arith_shift_right), (8, A.bitwise_and),
+                             (4, A.arith_shift_right), (1, A.bitwise_and))):
+        ts("i_p", "k%d" % k, sc[:, k:k + 1], ip, *ops)
+    cp("k0 k1 k2 k3 k4 k5 k6 i_p", "kf", cf[:, 400:408], sc[:, 0:8])
     ms("e0", T.e0[:], 0.0)
-    ms("swi0 swi1", T.swi[:], 0.0)
-    ts("i_p", "k0", sc[:, 0:1], ip, 3, A.arith_shift_right)
-    ts("i_p", "k1", sc[:, 1:2], ip, 7, A.bitwise_and)
-    ts("i_p", "k2", sc[:, 2:3], ip, 31, A.bitwise_and)
-    ts("c_row c_p e0", "e0", T.e0[:, 3:515:4], c_row, c_p, A.is_equal)
+    ts("c_row kf e0", "e0", T.e0[:, 3:515:4], c_row, c_p, A.is_equal)
     for b in range(4):
-        act("e0", "et%d" % b, T.et[:, 512 * b:512 * b + 512], T.e0[:, 3 - b:515 - b], FN.Copy)
-    ts("i_p", "k3", sc[:, 3:4], ip, 15, A.bitwise_and)
-    ts("i_p", "k4", sc[:, 4:5], ip, 5, A.arith_shift_right)
-    ts("i_p", "k5", sc[:, 5:6], ip, 1, A.bitwise_and)
-    ts("i_p", "k6", sc[:, 6:7], ip, 1, A.arith_shift_right, 7, A.bitwise_and)
-    ts("i_p", "k7", sc[:, 7:8], ip, 8, A.bitwise_and)
-    cp("k0 k1 k2 k3 k4 k5 k6 k7", "kf", cf[:, 400:408], sc[:, 0:8])
-    ts("k6", "k21", sc[:, 26:27], sc[:, 6:7], 4, A.bitwise_and)
-    ts("i_sw kf", "lsw", T.lsw[:], ci[:, 312:316], k_15, A.add)
-    ts("kf", "k9", cf[:, 408:409], k_odd, 32.0, A.mult, k_h, A.add)
-    cp("vgi", "pl0", T.pl0[:, 0:24], T.vgi[:])
-    send(0, "p", "pl0", [(T.plp0[:], T.pl0[:, 0:24])], "plp0")
-    cp("vgi", "swi0", T.swi[:, 0:12], T.vgi[:, 0:24:2])
-    cp("vgi", "swi1", T.swi[:, 32:44], T.vgi[:, 1:24:2])
-    tt("kf", "k16", cf[:, 410:411], k_i, k_j, A.is_lt)
-    ts("c_row kf", "k11", cf[:, 424:432], c_row[:, 0:128:16], k_8, A.add, 56.0, A.min)
-    exchange_x(0, T.xin, "xin0 xin1")
-    iota("i_a", ci[:, 130:258], [[2, 4], [1, 2], [0, 16]], 0, 0)
-    iota("i_b", ci[:, 320:448], [[0, 8], [2, 4], [0, 4]], 0, 0)
-    fill("ones", T.ones[:], C, 1)
-    fill("kt", T.kt[:], 512, 0)
-    fill("ct", T.ct[:], 4 * C, 0)
-
-    steps[0]()
+        move("VS"[b != 0], "e0", "et%d" % b, T.et[:, 512 * b:512 * b + 512], T.e0[:, 3 - b:515 - b])
     quant("et0 et1 et2 et3", "eq", T.eq[:], T.es[:], T.et[:])
-    act("i_cd kf", "cd0", cf[:, 256:280], cf[:, 432:456], FN.Identity, bias=k_r)
-    act("kf", "k15", cf[:, 409:410], k_q, FN.Copy, scale=4096.0)
-    act("cd0", "cd1", cf[:, 280:304], cf[:, 256:280], FN.Identity, bias=float(C))
-    act("i_e k15", "c_gm", c_gm, cf[:, 456:480], FN.Identity, bias=cf[:, 409:410])
-    decode(0, True)
-    steps[1]()
-    ts("k11", "lua", T.lu[:, 0:8], cf[:, 424:432], 2.0, A.mult)
-    steps[2]()
-    ts("i_16 kf", "lub", T.lu[:, 8:16], ci[:, 304:312], k_j, A.mult)
-    cp("swo", "pma", T.pm[:, 0:24:2], T.swo[:, 0:12])
-    cp("swo", "pm", T.pm[:, 1:24:2], T.swo[:, 32:44])
-    for b in (0, 1, 3, 2):
-        unload("S", 0, True, b)
+    ms("swi0 swi1", T.swi[:], 0.0)
+    for k in range(2):
+        ts("c_row kf", "lsw%d" % k, T.lsw[:, 2 * k:2 * k + 2], c_row[:, 16 * k:64:32], k_15, A.add)
+    tt("i_p k5", "k8", sc[:, 8:9], ip, sc[:, 5:6], A.add)
+    ts("k8", "k9", sc[:, 9:10], sc[:, 8:9], 1, A.bitwise_and)
+    ts("k9", "k10", col(411), sc[:, 9:10], 8.0, A.add)
+    ts("kf k10", "k11", col(412), k_15, 16.0, A.mult, col(411), A.add)
+    ts("c_row k11", "lv", T.lv[:], c_row[:, 0:2], 256.0, A.mult, col(412), A.add)
+    ts("i_p", "k12", sc[:, 10:11], ip, 1, A.arith_shift_right, 3, A.bitwise_and)
+    ts("k12 kf", "k13", sc[:, 11:12], sc[:, 10:11], k_q, A.subtract, 4.0, A.add)
+    ts("k13", "k14", sc[:, 12:13], sc[:, 11:12], 3, A.bitwise_and)
+    ts("kf", "k15", col(413), k_odd, k_8, A.add, 4.0, A.mult)
+    ts("kf k15", "k16", col(414), k_q, 8.0, A.mult, col(413), A.add)
+    tt("k14 k16", "k17", col(415), sc[:, 12:13], col(414), A.add)
+    ts("c_row k17", "l8", T.l8[:], c_row[:, 0:128:64], col(415), A.add, 95.0, A.min)
+    ts("c_row kf", "la", T.la[:], c_row[:, 7:32:16], k_8, A.add, 23.0, A.min)
+    for e in range(2):
+        cp("c_row", "lrp%d" % e, T.lrp[:, e:6:2], c_row[:, 7:24:8])
+    affine("kf", "k18", col(416), k_8, 2.0, 0.0)
+    affine("kf", "k19", col(417), k_j, 16.0, 0.0)
+    for k, o in enumerate((A.max, A.min)):
+        ts("c_row k18 k19", "lu%d" % k, T.lu[:, 4 * k:4 * k + 4], c_row[:, 0:128:32], col(416), A.add, col(417), o)
+    fill("sign", T.sign[:], 1)
+    select("sign", "sign", T.sign[:], T.sign[:], [[0, 3], [-1, 8], [1, 8]], A.not_equal, -1.0)
+    select("sign", "sign", T.sign[:], T.sign[:], [[0, 24], [1, 8]], A.not_equal, 0.0)
+    iota("th7", th7, [[0, 3], [-1, 8]], 7)
+    iota("th4", th4, [[0, 3], [-1, 8]], 4)
+    iota("i_cd", cf[:, 432:456], [[32, 12], [0, 2]], 0)
+    iota("i_e", cf[:, 456:480], [[0, 12], [int(BIG), 2]], 0)
+    affine("i_cd kf", "cd0", cf[:, 256:280], cf[:, 432:456], 1.0, k_r)
+    affine("cd0", "cd1", cf[:, 280:304], cf[:, 256:280], 1.0, float(C))
+    affine("cd0 cd1", "c_ys", c_ys, cf[:, 256:304], LS, Z)
+    affine("kf", "k20", col(418), k_q, 2 * BIG, 0.0)
+    affine("i_e k20", "c_gm", c_gm, cf[:, 456:480], 1.0, col(418))
+    affine("kf", "k21", col(419), k_15, LS, Z)
+    affine("c_row k21", "c_x0", cf[:, 576:608], c_row[:, 0:128:4], 4 * LS, col(419))
+    for k, b in enumerate((C * LS, 1024.0, C * LS + 1024.0)):
+        affine("c_x0", "c_x%d" % (k + 1), cf[:, 608 + 32 * k:640 + 32 * k], cf[:, 576:608], 1.0, b)
+    ms("mdup0 mdup1 mdup2", T.mdup[:], 1.0)
+    ts("c_row kf", "k22", T.kk[:], c_row[:, 0:32], k_r, A.is_equal, 4095.0, A.mult)
+    for k in range(3):
+        affine("k22", "mdup%d" % k, T.mdup[:, 128 * k:128 * k + 32], T.kk[:], 1.0, 1.0)
+    ms("mdup0 mdup1 mdup2", T.mdup[:, 0:288:96], 0.0)
+    affine("kf", "k23", col(420), k_15, 1.0 / 4096, 768.0 / 4096)
+    affine("c_row k23", "k24", cf[:, 424:427], c_row[:, 0:48:16], 1.0 / 4096, col(420))
+    ts("kf", "k25", col(421), k_r, 0.0, A.not_equal)
+    affine("k25", "k26", col(422), col(421), LS, 0.0)
+    affine("kf", "k27", col(423), k_g, 16 * LS, Z - 128 * LS)
+    ts("c_row k27", "k28", cf[:, 528:531], c_row[:, 0:3], 128 * LS, A.mult, col(423), A.add)
+    ts("k28 k25", "k29", cf[:, 532:535], cf[:, 528:531], col(421), A.mult, -Z, A.add)
+    for k in range(3):
+        affine("c_row k26 k29", "val%d" % k, T.val[:, 16 * k:16 * k + 16], c_row[:, 0:16], col(422), col(532 + k))
+    affine("kf", "k30", col(427), c_p, LS, Z - 128 * LS)
+    affine("c_row k30", "k31", cf[:, 536:539], c_row[:, 0:3], 128 * LS, col(427))
+    ms("ce0 ce1", T.ce[:], 0.0)
+    for u in sorted(set(up)):
+        iota("c_8%d" % u, c_8(u, 0), [[128, 3], [0, 8]], C * u, 1)
+        affine("c_8%d" % u, "c_9%d" % u, c_8(u, 1), c_8(u, 0), -LS, NONE)
+        affine("k25", "k4%d" % u, col(428 + u), col(421), Z + none_local(u), -Z)
+        ms("ce%d" % u, T.ce[:, 96 * u:96 * u + 96:4], 2 * Z)
+        ms("ce%d" % u, T.ce[:, 96 * u + 3:96 * u + 96:4], Z + (128 + C * u) * LS)
+    affine("et0 et1 k4%d" % up[0], "tab", T.tab[:, 0:2 * C], T.et[:, 0:2 * C], 0.0, col(428 + up[0]))
+    move("S", "et0 et1", wfk, T.wf[:], T.et[:, 0:2 * C], 0.0)
+    ms("s0c", T.s0[:], 0.0)
+    ms("s0c", T.s0[:, 1:96:3], -1.0)
+    ms("sbz", T.sbz[:], 0.0)
+    fill("wrc", T.wr[:, 2 * C:2 * C + 32], Z + NONE)
+    fill("vtc", T.vt32[:, C:544], 0)
+    fill("xo", T.xo[:], 0)
+    fill("ovi", T.ovi[:], 0)
     quant("ut", "uq", T.uq[:], T.us[:], T.ut[:])
-    tt("i_a i_b", "k14", ci[:, 130:258], ci[:, 130:258], ci[:, 320:448], A.add)
-    cp("uq lua lub", "upq", T.upq[:].bitcast(dt.uint32), T.uq[:].bitcast(dt.uint32).indirect(T.lu[:]))
-    ts("k14", "k17", ci[:, 320:448], ci[:, 130:258], 7, A.bitwise_and)
-    spread(0)
-    ts("k17 kf k16", "k18", T.kk[:, 0:128], ci[:, 320:448], k_i, A.is_equal, cf[:, 410:411], A.mult)
-    ts("k17 kf k16", "k19", T.kk[:, 128:256], ci[:, 320:448], k_j, A.is_equal, cf[:, 410:411], A.mult)
-    ts("ones", "z32", T.z32[:], T.ones[:], 0.0, A.mult)
-    tt("k18 k19 kt", "kt", T.kt[:, 0:512:4], T.kk[:, 0:128], T.kk[:, 128:256], A.subtract)
+    cp("uq lu0 lu1", "upq", T.upq[:].bitcast(dt.uint32), (T.uq[:].bitcast(dt.uint32), T.lu[:]))
+    act("uq lu0 lu1", "ups", T.ups[:], (T.us[:], T.lu[:]), FN.Copy)
+    quant("vt", "vq", T.vq[:], T.vs[:], T.vt[:])
 
-    decode(0, False)
-    unload("V", 0, False, 0)
-    unload("S", 0, False, 1)
-    unload("V", 0, False, 3)
-    unload("S", 0, False, 2)
-    gather_a("V", 0, True, 0)
-    gather_a("S", 0, True, 1)
-    gather_a("V", 0, True, 3)
-    gather_a("S", 0, True, 2)
-    gather_a("V", 0, False, 0)
-    for b in (1, 3, 2):
-        gather_a("S", 0, False, b)
-    for b in (0, 1, 3):
-        double("G", 0, b)
-    double("S", 0, 2)
-    act("uq lua lub", "ups", T.ups[:], T.us[:].indirect(T.lu[:]), FN.Copy)
-    fill("mseg", T.mseg[:], 96, 0)
-    op("G", "mseg", "mseg", lambda: g.affine_select(T.mseg[:], T.mseg[:], [[0, 12], [1, 8]], A.not_equal, -100.0, 0, 0))
-    op("G", "ones", "m32", lambda: g.affine_select(T.m32[:], T.ones[:], [[0, C // 32], [1, 32]], A.not_equal, 0.0, 0, 0))
-    fill("selfd", T.selfd[:], 96, int(NONE))
-    fill("wrc", T.wr[:, 2 * C:2 * C + 32], 32, 0)
-    fill("ovi0 ovi1", T.ovi[:], 32, 0)
+    unpack(0, True, "SSSS")
+    to_block("vgi", T.vgi[:, 0:24:2], T.vgi[:, 1:24:2])
+    own_pointers(0)
+    a, o = half(0, True), half(0, False)
+    cp("pm00 pm01", "cand", T.cand[:], pd(0, 1))
+    cp("pm00 pm01", "wfa", T.wf[:, a + 8:a + C:16], pd(0, 1))
+    cp("pm00 pm01", "wfb", T.wf[:, a + 9:a + C:32], pd(0, 1)[:, 1:24:2])
+    cp("pm00 pm01", "wfc", T.wf[:, a + 25:a + C:32], pd(0, 1)[:, 0:24:2])
+    to_block("plp0", T.plp0[:, 0:24:2], T.plp0[:, 1:24:2])
+    for k, (at, e) in enumerate(((8, 0), (25, 0), (24, 1), (9, 1))):
+        cp("swo", "wf" + "defg"[k], T.wf[:, o + at:o + C:32], T.swo[:, 32 * e:32 * e + 12])
+    cp("vt0 vt1 vtc lv", "pp", T.pp[:], look_up())
+    unpack(0, False, "SSSV")
+    for b in (0, 1, 3, 2):
+        move("S", "fw%d0 fw%d1 pl0" % (b, b), "ac%d" % b, T.ac[:, C * b:C * b + C], (plane(T.fw, b), T.pl0[:]))
 
     for t in range(3):
-        own = 24 * int(up[t])
-        hs, hr = T["h1s%d" % t], T["h1r%d" % t]
-        ks_, kr = "h1s%d" % t, "h1r%d" % t
+        u = up[t]
+        hb, hk = T["hb%d" % t], "hb%d" % t
         if t > 0:
             gather_a("S", t, False, 0, 12, 24)
             gather_a("V", t, False, 0, 0, 12)
             for b in (1, 3, 2):
                 gather_a("S", t, False, b)
-            spread_out("S")
         for b in (0, 1, 3):
             gather_b(t, b)
-        for h in range(2):
-            gather_b(t, 2, h, h + 1)
-            cs = slice(H * h, H * h + H)
-            quant("yt0%d yt1%d yt2%d yt3%d" % (h, h, h, h), "yq%d" % h, T.yq[:, cs], T.ys[:, cs], T.yt[:, 4 * H * h:4 * H * (h + 1)])
-            for k in range(2):
-                mm("upq ups yq%d" % h, 4 + 2 * h + k, T.upq[:, 128 * k:128 * k + 128], T.ups[:, 128 * k:128 * k + 128], T.yq[:, cs], T.ys[:, cs], H)
-            act("pb%d" % (4 + 2 * h), "sa%d" % h, T.sa[:, cs], T["pb%d" % (4 + 2 * h)][:, 0:H], FN.Copy)
-        banks = (5, 7, 4, 6)
-
-        def layer(b):
-            mm("wq wsc yq0 yq1", banks[b], T.wq[:, 128 * b:128 * b + 128], T.wsc[:, 128 * b:128 * b + 128], T.yq[:], T.ys[:])
-
-        def relu(b):
-            act("pb%d" % banks[b], "rl%d" % b, T.rl[:, C * b:C * b + C], T["pb%d" % banks[b]][:, 0:C], FN.Relu, scale=0.03125)
-
-        def add(b):
-            tt("pb%d rl%d" % (b, b), "xt%d" % b, T.xt[:, b:4 * C:4], T["pb%d" % b][:, 0:C], T.rl[:, C * b:C * b + C], A.add)
-
-        if t == 0:
-            spread_out("S")
-            quant("kt", "kq", T.kq[:], T.ks[:], T.kt[:])
-        for h in range(2):
-            cs = slice(H * h, H * h + H)
-            tt("pb%d ct sa%d" % (5 + 2 * h, h), "ct%d" % h, T.ct[:, 4 * H * h:4 * H * (h + 1):4], T["pb%d" % (5 + 2 * h)][:, 0:H], T.sa[:, cs], A.is_gt)
-            quant("ct%d" % h, "cq%d" % h, T.cq[:, cs], T.cs[:, cs], T.ct[:, 4 * H * h:4 * H * (h + 1)])
-            if h == 0:
-                layer(0)
-            mm("kq cq%d" % h, 4 + 2 * h, T.kq[:], T.ks[:], T.cq[:, cs], T.cs[:, cs], H)
-        layer(1)
-        relu(0)
-        if t == 0:
-            act("cd0 cd1", "c_cd", cf[:, 304:352], cf[:, 256:304], FN.Copy, scale=LS)
-            act("c_x0", "c_x1", cf[:, c_xn:c_xn + 6], cf[:, c_xk:c_xk + 6], FN.Copy, scale=-1024.0)
-            ts("k6 kf", "k22", sc[:, 24:25], sc[:, 6:7], k_q, A.subtract, 4.0, A.add)
-        relu(1)
-        for h in range(2):
-            tr("pb%d" % (4 + 2 * h), "t32%d" % h, T.t32[:, H * h:H * h + H], T["pb%d" % (4 + 2 * h)][:, 0:H])
-            layer(2 + h)
-            tt("t32%d p8a p8b p8c p8d0 p8d1 p8d2 p8d3" % h, "key%d" % h, T.key[:, 48 * h:48 * h + 48], T.t32[:, H * h:H * h + H:4],
-               T.p8[:, 48 * h:48 * h + 48], A.add)
-        scan("key0 key1 mseg", "ksc", T.ksc[:], T.mseg[:], T.key[:], -100.0, A.add, A.max)
-        k0, k7 = T.key[:, 0:96:4], T.ksc[:, 7:96:8]
-        ts("key0 key1", "s4", sm(4), k0, 4.0, A.is_lt, 1024.0, A.mult)
-        ts("ksc", "z32", T.z32[:, 0:C:32], k7, 7.0, A.subtract, 2048.0, A.mult)
-        ts("key0 key1", "s5", sm(5), k0, 7.0, A.is_ge, 2048.0, A.mult)
-        scan("z32 m32", "af", T.af[:], T.m32[:], T.z32[:], 0.0, A.mult, A.add)
-        act("ksc", "s7", sm(7, 12), k7, FN.Identity, scale=2.0 ** 34, bias=-(7.5 - 1.0 / LS) * 2.0 ** 34)
-        if t == 0:
-            ts("k22", "k23", sc[:, 25:26], sc[:, 24:25], 3, A.bitwise_and)
-        tr("af", "ar", T.ar[:], T.af[:])
-        tt("s4 s5", "s6", sm(6), sm(4), sm(5), A.add)
-        rev = T.ar[:, ::-1]
-
-        def differ(q, k):
-            out = T.dd[:, C * k:C * k + C]
-            if q == "S":
-                act("ar c_x1", "dd%d" % k, out, rev, FN.Abs, scale=1024.0, bias=cf[:, c_xn + k:c_xn + k + 1])
-            else:
-                ts("ar c_x0", "dd%d" % k, out, rev, cf[:, c_xk + k:c_xk + k + 1], A.not_equal, 1024.0, A.mult)
-
-        def first(k):
-            scan("dd%d ones" % k, "so%d" % k, T.so[:, C * k:C * k + C], T.ones[:], T.dd[:, C * k:C * k + C],
-                 0.0 if up[t] else float(C), A.add, A.min)
-
-        for k in range(2, 6):
-            differ("S", k)
-        for k in range(2):
-            differ("V", k)
-        if t == 0:
-            tt("k21 k23", "k28", cf[:, 414:415], sc[:, 25:26], sc[:, 26:27], A.add)
-        for k in range(5):
-            first(k)
-        if t == 0:
-            ts("c_row k28", "lrel", T.lrel[:, 0:3], c_row[:, 0:24:8], cf[:, 414:415], A.add)
-        tt("s6 pm", ks_ + "p", hs[:, 48:72], sm(6), T.pm[:], A.add)
-        for e in range(2):
-            a = cd(t, 1)
-            tt("s7 c_cd selfd", "selfd%d" % e, T.selfd[:, 3 * own + e:3 * own + 24:2], sm(7, 12), cf[:, a:a + 24:2], A.max)
-        first(5)
-        sos = "so0 so1 so2 so3 so4 so5"
-        base = float(C) if up[t] else 0.0
-        ts(sos, "rel0", T.rel[:, 0:24:4], T.so[:, C - 1:6 * C:C], base, A.add, LS, A.mult)
-        ts(sos, "rel1", T.rel[0:64, 2:24:4], T.so[64:128, C - 1:6 * C:C], base, A.add, LS, A.mult)
-        act(sos, "rel2", T.rel[64:128, 2:24:4], T.so[0:64, C - 1:6 * C:C], FN.Identity, scale=LS, bias=base * LS)
-        for q in range(4):
-            s = 32 * ((q + 1) % 4)
-            move("VS"[q // 2], "rel0 rel1 rel2", "rel%d" % (3 + q), T.rel[32 * q:32 * q + 32, 1:24:2], T.rel[s:s + 32, 0:24:2])
-        tt("rel0 rel1 rel2 rel3 rel4 rel5 rel6 lrel selfd selfd0 selfd1", ks_ + "l", hs[:, 0:48],
-           T.rel[:].indirect(T.lrel[:, 0:3]), T.selfd[:, 2 * own:2 * own + 48], A.min)
-        relu(2)
-        relu(3)
-        send(t, "h", ks_ + "l " + ks_ + "p", [(hr[:], hs[:])], kr)
-        for b in range(4):
-            add(b)
-        exchange_x(t + 1, T.xt, "xt0 xt1 xt2 xt3")
-        act("ksc", "s8", sm(8, 12), k7, FN.Identity, scale=2048.0, bias=-14336.0)
-        ts("s6", "s9", sm(9), sm(6), 0.0, A.is_equal, LS, A.mult)
-        if t == 0:
-            ts("c_row k9", "lfin", T.lfin[:], c_row[:, 0:16:8], cf[:, 408:409], A.add)
-            cp("c_row", "lrep", T.lrep[:], c_row[:, 0:48])
-        tt("s8 cd0 cd1", "s10", sm(10, 12), sm(8, 12), cf[:, cd(t, 0):cd(t, 0) + 24:2], A.subtract)
-        act("s9", "s11", sm(11), sm(9), FN.Identity, bias=-1024.0)
+        for k in range(3):
+            cs, ps, bank = slice(128 * k, 128 * k + 128), slice(64 * k, 64 * k + 64), 4 + k % 2
+            gather_b(t, 2, k, k + 1)
+            quant("yt0%d yt1%d yt2%d yt3%d" % (k, k, k, k), "yq%d" % k, T.yq[:, cs], T.ys[:, cs], T.yt[:, 512 * k:512 * k + 512])
+            mm("upq ups yq%d" % k, bank, T.yq[:, cs], T.ys[:, cs], T.upq[:], T.ups[:], 128)
+            act("pb%d" % bank, "sa%d" % k, T.sa[:, ps], T["pb%d" % bank][:, 64:128], FN.Copy)
+            tt("pb%d sa%d" % (bank, k), "cb%d" % k, T.cb[:, ps], T["pb%d" % bank][:, 0:64], T.sa[:, ps], A.is_gt)
+        scan("cb0 cb1 cb2 sign", "pk", T.pk[:], T.sign[:], T.cb[:], 0.0, A.mult, A.add)
+        place = T.pk[:, 7:192:8]
+        scan("pk d8", "ksc", T.ksc[:], place, sm(4), 6.5, A.max, A.add)
+        ts("ksc lrp0 lrp1", "rp", T.rp[:], (T.ksc[:], T.lrp[:]), 6.5, A.subtract, BIG, A.mult)
+        tr("rp", "rt", T.rt[:], T.rp[:])
+        for k in range(3):
+            ts("rt rp", "same%d" % k, T.same[:, 96 * k:96 * k + 96], T.rt[:], T.rp[:, 32 * k:32 * k + 1], A.is_equal)
+        scan("same0 same1 same2 mdup0 mdup1 mdup2", "dup", T.dup[:], T.mdup[:], T.same[:], 0.0, A.mult, A.max)
+        for k in range(3):
+            ts("dup rp k24", "off%d" % k, T.off[:, k:k + 1], T.dup[:, 96 * k + 95:96 * k + 96], col(424 + k), A.mult, T.rp[:, 32 * k:32 * k + 1], A.max)
+        cp("off0 off1 off2 val0 val1 val2", "tab", (T.tab[:], T.off[:, 0:3]), T.val[:])
+        tr("tab", "tb", T.tb[:], T.tab[:, 0:2 * C])
         if t < 2:
-            decode(t + 1, True)
-            unload("S", t + 1, True, 0)
+            affine("tab k4%d" % up[t + 1], "tab", T.tab[:, 0:2 * C], T.tab[:, 0:2 * C], 0.0, col(428 + up[t + 1]))
+        affine("ksc", "s5", sm(5, 3), T.ksc[:, 7:24:8], 2.0 ** 38, -(6.5 + 1023.5 / BIG) * 2.0 ** 38)
+        tt("s5 k31", "s6", sm(6, 3), sm(5, 3), cf[:, 536:539], A.max)
+        for q in range(4):
+            a = 96 * u + 4 * (12 * u + q)
+            move("S", "s6 ce%d" % u, "cq%d%d" % (u, q), T.ce[32 * q:32 * q + 32, a:a + 33:16], T.sm[32 * q:32 * q + 32, 192:195])
+        scan("tb ce%d cq%d0 cq%d1 cq%d2 cq%d3" % (u, u, u, u, u), "oe", T.oe[:], T.tb[:, 0:2 * C:8], T.ce[:, 96 * u:96 * u + 96], 0.0, A.min, A.add)
+        tt("oe", "rel", T.rel[0:64, :], T.oe[0:64, 3:96:4], T.oe[64:128, 3:96:4], A.min)
+        for q in range(4):
+            tt("rel", hk + "o%d" % q, hb[32 * q:32 * q + 32, 120 * u:120 * u + 24], T.rel[0:32, :], T.rel[32:64, :], A.min)
+        tt("pk th7", "s7", sm(7), place, th7, A.is_ge)
+        tt("pk th4", "s8", sm(8), place, th4, A.is_lt)
+        affine("ksc la", "s9", sm(9, 32), (T.ksc[:], T.la[:]), BIG * LS, -(6.5 * BIG + 768) * LS)
+        affine("ksc la", "s10", sm(10, 32), (T.ksc[:], T.la[:]), -BIG, 6.5 * BIG)
+        tt("s7 s8", "s11", sm(11), sm(7), sm(8), A.add)
+        tt("s10 c_8%d" % u, "s12", sm(12), sm(10), c_8(u, 0), A.add)
+        tt("s11 s9", "s13", sm(13), sm(11), sm(9), A.mult)
+        tt("s7 s12", "s14", sm(14), sm(7), sm(12), A.mult)
+        tt("s13 c_9%d" % u, "s15", sm(15), sm(13), c_8(u, 1), A.add)
+        tt("s14 s15", "aga", T.ag[:, 0:96:4], sm(14), sm(15), A.add)
+        move("S", spread(T.ag, "ag") + " l8", "s9", sm(9, 32), (T.ag[:], T.l8[:]))
+        move("S", "s9", hk + "d", pd(t, 0), sm(9))
+        mine = "%so0 %so1 %so2 %so3 %sd pm%d0 pm%d1" % (hk, hk, hk, hk, hk, t, t)
+        send(t, "h", mine, [(hb[:, 72 * u:72 * u + 72], hb[:, 72 * u:72 * u + 72])], hk + "r", NOTE)
+        for h in range(2):
+            for b in range(4):
+                bank, cs, a = 6 + b % 2, slice(H * h, H * h + H), C * b + H * h
+                mm("wq wsc yq%d yq%d" % (h, h + 1), bank, T.wq[:, 128 * b:128 * b + 128], T.wsc[:, 128 * b:128 * b + 128], T.yq[:, cs], T.ys[:, cs], H)
+                act("pb%d" % bank, "rl%d%d" % (b, h), T.rl[:, a:a + H], T["pb%d" % bank][:, 0:H], FN.Relu, scale=0.03125)
+                tt("pb%d rl%d%d" % (b, b, h), "xt%d%d" % (b, h), T.xt[:, 4 * H * h + b:4 * H * (h + 1):4], T["pb%d" % b][:, cs], T.rl[:, a:a + H], A.add)
+            quant_x(t + 1, h, T.xt, " ".join("xt%d%d" % (b, h) for b in range(4)))
+        if t < 2:
+            send_x(t + 1, "outh")
+            unpack(t + 1, True, "VSSV")
+            unpack(t + 1, False, "SSSS")
         else:
-            mm("vq xq3", 4, T.vq[:], T.vs[:], T.xq3[:], T.xs3[:])
-            dma("Y", "xq3", "", T.oc[:], u8(T.xq3[:]), "st")
+            mm("vq xq30 xq31", 4, T.vq[:], T.vs[:], T.xq3[:], T.xs3[:])
+            dma("Y", "xq30 xq31", "", T.oc[:], u8(T.xq3[:]), "st")
             act("pb4", "yo", T.yo[:], T.pb4[:, 0:C], FN.Copy)
             for k in range(4):
-                dma("Y", "xq3", "", T.osc[4 * k:4 * k + 4, :], T.xs3[32 * k:32 * k + 4, :], "st")
+                dma("Y", "xq30 xq31", "", T.osc[4 * k:4 * k + 4, :], T.xs3[32 * k:32 * k + 4, :], "st")
             dma("Y", "yo", "", T.y[:], T.yo[:], "st")
-        lo_pf, up_pf = (hr, hs) if up[t] else (hs, hr)
-        both = ks_ + "l " + ks_ + "p " + kr
-        lown = T.low[:, own:own + 24]
-        tt(both, "low", T.low[:], hs[:, 0:48], hr[:, 0:48], A.min)
-        tt(both + " low", "wb0", T.wb[:, 0:24], T.low[:, 0:24], lo_pf[:, 48:72], A.add)
-        tt(both + " low", "wb1", T.wb[:, 24:48], T.low[:, 24:48], up_pf[:, 48:72], A.add)
-        act("lrep wb0", "wf0", T.wf[:, 0:C], T.wb[:, 0:24].indirect(T.lrep[:, 0:24]), FN.Copy)
-        act("lrep wb0 wb1", "wf1", T.wf[:, C:2 * C], T.wb[:].indirect(T.lrep[:, 24:48]), FN.Copy)
-        tt("low c_cd", "s12", sm(12), lown, cf[:, cd(t, 1):cd(t, 1) + 24], A.is_equal)
-        ts("low", "s13", sm(13), lown, 1.0 / LS, A.mult)
-        tt("s12 s10", "s14", sm(14, 12), T.sm[:, 24 * 12:24 * 13:2], sm(10, 12), A.mult)
-        ts("low", "s16", sm(16), lown, 1024.0, A.add)
+        old = T.npt[:, 2:72:3] if t else T.vgi[:]
+        cp("npt vgi", "own", T.s1[:, 2:72:3], old)
+        tt("npt vgi " + cx, "xo", T.xo[:, 0:24], old, c_x(t, 0, 24), A.add)
+        both = mine + " " + hk + "r"
         for e in range(2):
-            tt("s14 s13", "swi%d" % e, T.swi[:, 32 * e:32 * e + 12], sm(14, 12), T.sm[:, 24 * 13:24 * 14:2], A.add)
-        tt("s12 s11", "s15", sm(15), sm(12), sm(11), A.mult)
-        steps[0]()
-        ts("s12", "s17", sm(17), sm(12), LS, A.mult, 2048.0, A.add)
-        steps[1]()
-        tr("wf0", "wr0", T.wr[:, 0:C], T.wf[:, 0:C])
-        steps[2]()
-        tt("s15 s16", "s18", sm(18), sm(15), sm(16), A.add)
-        to_list("cand")
-        tr("wf1", "wr1", T.wr[:, C:2 * C], T.wf[:, C:2 * C])
-        tt("s17 low", "s19", sm(19), sm(17), lown, A.add)
-        act("wr0 wr1 wrc cand", "gv1", T.gv[:, H:C], T.wr[:].indirect(T.cand[:, 12:24]), FN.Copy)
-        cp("wr0 wr1 wrc cand", "gv0", T.gv[:, 0:H], T.wr[:].indirect(T.cand[:, 0:12]))
-        if t < 2:
-            decode(t + 1, False)
-            for mine, b in ((True, 1), (True, 3), (True, 2), (False, 0), (False, 1), (False, 3), (False, 2)):
-                unload("S", t + 1, mine, b)
-        tr("gv0 gv1", "vt32", T.vt32[:], T.gv[:])
-        v = T.vt32[:, 0:C:16]
-        cp("vt32", "vi", T.vi[:, 0:24], v)
-        tt("vt32 s18", "s20", sm(20), v, sm(18), A.is_ge)
-        tt("vt32 s19", "s21", sm(21), v, sm(19), A.is_ge)
-        tt("vt32 s18", "s22", sm(22), v, sm(18), A.is_lt)
-        ts("vi", "vi2", T.vi[:, 24:48], T.vi[:, 0:24], 1023, A.bitwise_and)
-        tt("s20 s21", "s0", sm(0), sm(20), sm(21), A.subtract)
-        tt("s21 s13", "s2", sm(2), sm(21), sm(13), A.mult)
-        tt("s22 pm", "s1", sm(1), sm(22), T.pm[:], A.mult)
-        tt("vi2 s0", "s3", sm(3), T.vi[:, 24:48], sm(0), A.mult)
-        tt("s1 s2", "s23", sm(23), sm(1), sm(2), A.add)
+            tt(both, "low%d" % e, T.low[:, e:48:2], hb[:, 0:24], hb[:, 120:144], A.min)
+        cp(both, "dpna", T.dpn[:, 0:96:2], hb[:, 24:120:2])
+        for e in range(2):
+            cp(both, "dpsa%d" % e, T.dps[:, 2 * e:96:4], hb[:, 26 - 2 * e:120:4])
+        tt("low0 low1 c_ys sbz", "sb", T.sbz[:, 1:96:2], T.low[:], c_ys, A.is_equal)
+        tt("low0 low1 " + both, "dpnb", T.dpn[:, 1:96:2], T.low[:], hb[:, 25:120:2], A.add)
+        for e in range(2):
+            tt("low0 " + both, "dpsb%d" % e, T.dps[:, 2 * e + 1:96:4], T.low[:, 0:48:2], hb[:, 27 - 2 * e:120:4], A.add)
+        scan("sb dpna dpnb", "wfa wfd wff", T.wf[:, 0:2 * C:8], T.sbz[:], T.dpn[:], 0.0, A.mult, A.add)
+        scan("sb dpsa0 dpsa1 dpsb0 dpsb1", "wfb wfc wfe wfg", T.wf[:, 1:2 * C:8], T.sbz[:], T.dps[:], 0.0, A.mult, A.add)
+        ts("wfa wfd wff", "cand", T.cand[:], T.wf[:, C * u + 8:C * u + C:16], 1.0 / LS, A.mult, -Z / LS, A.add)
+        v = look_up()
+        tt("vt0 vt1 lv " + cx, "s1a", T.s1[:, 0:96:3], v, c_x(t, 1), A.is_ge)
+        tt("vt0 vt1 lv " + cx, "s1b", T.s1[:, 1:96:3], v, c_x(t, 0), A.is_ge)
+        tt("vt0 vt1 lv xo s0c", "s0d", T.s0[:, 2:96:3], v, T.xo[:], A.subtract)
+        scan("s1a s1b s0d s0c own", "npt", T.npt[:], T.s0[:, 0:72], T.s1[:, 0:72], 0.0, A.mult, A.add)
+        new = T.npt[:, 2:72:3]
         if t == 2:
-            for e in range(2):
-                tt("s3 s23", "ovi%d" % e, T.ovi[:, 12 * e:12 * e + 12], T.sm[:, 72 + e:96:2], T.sm[:, 552 + e:576:2], A.add)
-            tr("ovi0 ovi1", "ovo", T.ovo[:], T.ovi[:])
-            for q in range(4):
-                dma("YS"[q % 2], "ovo", "", T.ov[2 * q:2 * q + 2, :], T.ovo[32 * q:32 * q + 24, :], "st")
+            cp("npt", "ovi", T.ovi[:, 0:24], new)
+            tr("ovi", "ovo", T.ovo[:], T.ovi[:])
+            for k in range(8):
+                q, e = k // 2, k % 2
+                dma("YS"[e], "ovo", "", T.ov[k:k + 1, :], T.ovo[32 * q:32 * q + 24, 16 * e:16 * e + 16], "st")
             break
-        for e in range(2):
-            tt("s3 s23", "swi%d" % e, T.swi[:, 32 * e:32 * e + 12], T.sm[:, 72 + e:96:2], T.sm[:, 552 + e:576:2], A.add)
-        steps[0]()
-        tt("s3 s23", "pm", T.pm[:], sm(3), sm(23), A.add)
-        steps[1]()
-        steps[2]()
         name = "pl%d" % (t + 1)
-        to_list(name)
-        send(t + 1, "p", name, [(T["plp%d" % (t + 1)][:], T[name][:, 0:24])], "plp%d" % (t + 1))
-        for b in (0, 1, 3, 2):
-            gather_a("VS"[b // 2], t + 1, True, b)
-            double("G", t + 1, b)
-        spread(t + 1)
-        if t == 0:
-            quant("vt", "vq", T.vq[:], T.vs[:], T.vt[:])
+        cp("npt", name, T[name][:], new)
+        send(t + 1, "p", name, [(T["plp%d" % (t + 1)][:], T[name][:])], "plp%d" % (t + 1), NOTE)
+        for b in (0, 1, 3):
+            gather_a("S", t + 1, True, b)
+        gather_a("V", t + 1, True, 2, 0, 12)
+        gather_a("V", t + 1, True, 2, 12, 24)
+        for b, q in zip((0, 1, 3, 2), "VVGG"):
+            double(q, t + 1, b)
+        to_block("npt", T.npt[:, 2:72:6], T.npt[:, 5:72:6])
+        own_pointers(t + 1)
 
-    wait("G", list(count.items()))
+    issue()

@@ -3,13 +3,13 @@ from concourse.mybir import dt, AluOpType, ActivationFunctionType
 C = 384
 H = C // 2
 STEP = [1, 2, 4]
-Q8, U8, BF, F32, I32, U16 = "float8_e4m3fn_x4", "uint8", "bfloat16", "float32", "int32", "uint16"
+Q8, U8, BF, F16, F32, I32, U16 = "float8_e4m3fn_x4", "uint8", "bfloat16", "float16", "float32", "int32", "uint16"
 LS = 2048.0
 Z = 2048 * LS
 NONE = 768 * LS
 BIG = 16384.0
-CYCLE, SAME, OTHER, SLACK = 0.86e-3, 0.19, 0.1, 0.01
-ISSUE, FIRST, LOAD, LOADX, NOTE, CODES = 0.2, 2.0, 1.8, 2.6, 1.8, 2.8
+CYCLE, SAME, OTHER, SLACK = 0.83e-3, 0.2, 0.14, 0.03
+ISSUE, FIRST, LOAD, LOADX, NOTE, CODES = 0.25, 2.0, 1.8, 2.6, 1.8, 2.8
 
 
 def sb(n, d):
@@ -24,8 +24,8 @@ SCRATCH = {
     "wq": sb(512, Q8), "wsc": sb(512, U8), "yq": sb(C, Q8), "ys": sb(C, U8),
     "fw": sb(4 * 2 * C, BF), "aw": sb(4 * 2 * C, BF), "ac": sb(4 * C, BF),
     "sa": sb(192, F32), "cb": sb(192, BF), "sign": sb(192, BF), "pk": sb(192, BF), "rl": sb(4 * C, F32), "yo": sb(C, F32),
-    "vgi": sb(24, I32), "ksc": sb(24, F32), "p8": sb(96, F32), "ag": sb(96, F32),
-    "rp": sb(96, F32), "rt": sb(96, F32), "same": sb(288, BF), "mdup": sb(288, BF), "dup": sb(288, BF),
+    "vgi": sb(24, I32), "ksc": sb(24, F32), "least": sb(56, F32), "p8": sb(96, F32), "ag": sb(96, F32),
+    "rp": sb(96, F16), "rt": sb(96, F16), "same": sb(291, F16), "mdup": sb(291, F16), "dup": sb(291, F16),
     "val": sb(48, BF), "tab": sb(1024 + 2 * C, BF), "tb": sb(2 * C, BF), "ce": sb(192, F32), "oe": sb(96, F32), "rel": sb(24, F32),
     "low": sb(48, F32), "sbz": sb(96, F32), "dpn": sb(96, F32), "dps": sb(96, F32), "wf": sb(2 * C, F32),
     "wr": sb(2 * C + 32, F32), "gv": sb(C, F32), "vt32": sb(544, F32),
@@ -42,7 +42,7 @@ for _t in range(3):
     SCRATCH["lq%d" % _t] = sb(C, Q8)
     SCRATCH["ls%d" % _t] = sb(C, U8)
     SCRATCH["pl%d" % _t] = sb(24, U16)
-    SCRATCH["plp%d" % _t] = sb(24, U16)
+    SCRATCH["plp%d" % _t] = sb(24, U16 if _t else I32)
     SCRATCH["hb%d" % _t] = sb(144, F32)
 for _b in range(8):
     SCRATCH["pb%d" % _b] = ("psum", [128, 512], F32)
@@ -59,7 +59,7 @@ def rank_program(g, core, T, topo):
     if rank is None:
         return
     eng = {"V": g.vector, "S": g.scalar, "P": g.tensor, "G": g, "Y": g.sync}
-    nodes, wrote, read, total = [], {}, {}, {}
+    nodes, wrote, read, total, turns = [], {}, {}, {}, []
 
     def node(q, busy, lat, deps, call=None, sem=None, inc=0):
         nodes.append(dict(q=q, busy=busy, lat=lat, deps=sorted(deps), call=call, sem=sem, inc=inc))
@@ -87,10 +87,10 @@ def rank_program(g, core, T, topo):
         if isinstance(out, tuple):
             return 0.06 + 4 * CYCLE * 16 * out[1].shape[1]
         if isinstance(ins[0], tuple):
-            return 0.06 + 1.6 * CYCLE * 16 * ins[0][1].shape[1]
+            return 0.07 + 1.75 * CYCLE * 16 * ins[0][1].shape[1]
         if per is None:
-            per = 0.5 if all(a.dtype in (dt.bfloat16, dt.uint16) for a in [out] + ins) else 1.0
-        return 0.01 + CYCLE * max(64, per * out.shape[1])
+            per = 0.5 if all(a.dtype in (dt.bfloat16, dt.float16, dt.uint16) for a in [out] + ins) else 1.0
+        return 0.02 + CYCLE * max(64, per * out.shape[1])
 
     def tt(r, w, out, a, b, o):
         op("V", r, w, lambda: g.vector.tensor_tensor(out, ap(a), b, o), cycles(out, [a], 1.0 if "pb" in r else 2.0))
@@ -168,6 +168,9 @@ def rank_program(g, core, T, topo):
             return 0.0 if a is None or b is None or nodes[d]["sem"] is None else SAME if a == b else OTHER
 
         before = [[(d, gap(d, n)) for d in x["deps"]] for n, x in enumerate(nodes)]
+        for names in turns:
+            for d, n in zip(names, names[1:]):
+                before[n].append((d, 0.0))
         after = [[] for x in nodes]
         for n, e in enumerate(before):
             for d, k in e:
@@ -326,12 +329,12 @@ def rank_program(g, core, T, topo):
         for e in range(2):
             cp("swo", "pm%d%d" % (t, e), pd(t, 1)[:, e:24:2], T.swo[:, 32 * e:32 * e + 12])
         tt(pm + " cd0 cd1", "s0", sm(0), pd(t, 1), c_y(t), A.is_equal)
-        tt(pm + " c_gm", "s1", sm(1), pd(t, 1), c_gm, A.add)
-        ts("s0", "s2", sm(2), sm(0), 1024.0, A.mult)
-        tt("s1 s2", "p8a", T.p8[:, 0:96:4], sm(1), sm(2), A.add)
-        ts(spread(T.p8, "p8") + " l8", "s3", sm(3, 32), (T.p8[:], T.l8[:]), 1.0 / BIG, A.mult)
+        move("S", "s0", "s2", sm(2), sm(0), 1024.0)
+        tt(pm + " s2", "p8a", T.p8[:, 0:96:4], pd(t, 1), sm(2), A.add)
+        move("S", spread(T.p8, "p8") + " l8", "s3", sm(3, 32), (T.p8[:], T.l8[:]))
         tt("s3", "d8", sm(4, 23), sm(3, 23), T.sm[:, 97:120], A.subtract)
-        affine("s3", "d8", T.sm[:, 135:152:8], T.sm[:, 103:120:8], 1.0, -0.5)
+        move("S", "s3", "d8", T.sm[:, 135:152:8], T.sm[:, 103:120:8])
+        tt("s3 c_8%d" % up[t], "s12", sm(12), c_8(up[t], 0), sm(3), A.subtract)
 
     def none_local(u):
         return NONE - (128 + C * u) * LS
@@ -340,11 +343,11 @@ def rank_program(g, core, T, topo):
     dma("Y", "", "vgi", T.vgi[:], T.vg[:], "ld0")
     dma("Y", "", "xin1", T.xin[:, 4 * H:4 * C], T.x[:, 4 * H:4 * C], "ld1", LOADX)
     cp("vgi", "pl0", T.pl0[:], T.vgi[:])
-    send(0, "p", "pl0", [(T.plp0[:], T.pl0[:])], "plp0", NOTE)
+    send(0, "p", "vgi", [(T.plp0[:], T.vgi[:])], "plp0", NOTE)
     for h in range(2):
         quant_x(0, h, T.xin, "xin%d" % h)
     send_x(0, "outp", "sent0", "left")
-    dma("Y", "left", "ut", T.ut[:], T.u[:], "ld3")
+    dma("Y", "left", "ut", T.ut[:], T.u[:], "ld3", CODES)
     dma("Y", "left", "wq", u8(T.wq[:]), T.wc[:], "ld4", LOADX)
     dma("Y", "left", "wsc", T.wsc[:], T.ws[:], "ld5")
     dma("Y", "left", "vt", T.vt[:], T.v[:], "ld6")
@@ -389,23 +392,21 @@ def rank_program(g, core, T, topo):
     iota("th7", th7, [[0, 3], [-1, 8]], 7)
     iota("th4", th4, [[0, 3], [-1, 8]], 4)
     iota("i_cd", cf[:, 432:456], [[32, 12], [0, 2]], 0)
-    iota("i_e", cf[:, 456:480], [[0, 12], [int(BIG), 2]], 0)
+    fill("zero", T.least[:, 24:32], 0)
     affine("i_cd kf", "cd0", cf[:, 256:280], cf[:, 432:456], 1.0, k_r)
     affine("cd0", "cd1", cf[:, 280:304], cf[:, 256:280], 1.0, float(C))
     affine("cd0 cd1", "c_ys", c_ys, cf[:, 256:304], LS, Z)
-    affine("kf", "k20", col(418), k_q, 2 * BIG, 0.0)
-    affine("i_e k20", "c_gm", c_gm, cf[:, 456:480], 1.0, col(418))
     affine("kf", "k21", col(419), k_15, LS, Z)
     affine("c_row k21", "c_x0", cf[:, 576:608], c_row[:, 0:128:4], 4 * LS, col(419))
     for k, b in enumerate((C * LS, 1024.0, C * LS + 1024.0)):
         affine("c_x0", "c_x%d" % (k + 1), cf[:, 608 + 32 * k:640 + 32 * k], cf[:, 576:608], 1.0, b)
-    ms("mdup0 mdup1 mdup2", T.mdup[:], 1.0)
-    ts("c_row kf", "k22", T.kk[:], c_row[:, 0:32], k_r, A.is_equal, 4095.0, A.mult)
+    ms("mdup0 mdup1 mdup2 mdup3", T.mdup[:], 1.0)
+    ts("c_row kf", "k22", T.kk[:], c_row[:, 0:32], k_r, A.is_equal, 2047.0, A.mult)
     for k in range(3):
-        affine("k22", "mdup%d" % k, T.mdup[:, 128 * k:128 * k + 32], T.kk[:], 1.0, 1.0)
-    ms("mdup0 mdup1 mdup2", T.mdup[:, 0:288:96], 0.0)
-    affine("kf", "k23", col(420), k_15, 1.0 / 4096, 768.0 / 4096)
-    affine("c_row k23", "k24", cf[:, 424:427], c_row[:, 0:48:16], 1.0 / 4096, col(420))
+        ts("k22", "mdup%d" % k, T.mdup[:, 129 * k:129 * k + 32], T.kk[:], 1.0, A.add)
+    ms("mdup0 mdup1 mdup2", T.mdup[:, 0:291:97], 0.0)
+    affine("kf", "k23", col(420), k_15, 1.0 / 2048, 768.0 / 2048)
+    ts("c_row k23", "mdup3", T.mdup[:, 96:291:97], c_row[:, 0:48:16], 1.0 / 2048, A.mult, col(420), A.add)
     ts("kf", "k25", col(421), k_r, 0.0, A.not_equal)
     affine("k25", "k26", col(422), col(421), LS, 0.0)
     affine("kf", "k27", col(423), k_g, 16 * LS, Z - 128 * LS)
@@ -451,6 +452,7 @@ def rank_program(g, core, T, topo):
     unpack(0, False, "SSSV")
     for b in (0, 1, 3, 2):
         move("S", "fw%d0 fw%d1 pl0" % (b, b), "ac%d" % b, T.ac[:, C * b:C * b + C], (plane(T.fw, b), T.pl0[:]))
+    turns.append([wrote[k] for k in "fw00 ac0 gv1 fw10 ac1 fw30 ac3 ac2".split()])
 
     for t in range(3):
         u = up[t]
@@ -463,27 +465,31 @@ def rank_program(g, core, T, topo):
         for b in (0, 1, 3):
             gather_b(t, b)
         for k in range(3):
-            cs, ps, bank = slice(128 * k, 128 * k + 128), slice(64 * k, 64 * k + 64), 4 + k % 2
-            gather_b(t, 2, k, k + 1)
+            cs, ps, bank = slice(128 * k, 128 * k + 128), slice(64 * k, 64 * k + 64), 4 + k
+            pb, scores = T["pb%d" % bank], T["pb%d" % bank][:, 0:64:9]
+            if k != 1:
+                gather_b(t, 2, k, k + 2 - k // 2)
             quant("yt0%d yt1%d yt2%d yt3%d" % (k, k, k, k), "yq%d" % k, T.yq[:, cs], T.ys[:, cs], T.yt[:, 512 * k:512 * k + 512])
             mm("upq ups yq%d" % k, bank, T.yq[:, cs], T.ys[:, cs], T.upq[:], T.ups[:], 128)
-            act("pb%d" % bank, "sa%d" % k, T.sa[:, ps], T["pb%d" % bank][:, 64:128], FN.Copy)
-            tt("pb%d sa%d" % (bank, k), "cb%d" % k, T.cb[:, ps], T["pb%d" % bank][:, 0:64], T.sa[:, ps], A.is_gt)
+            scan("pb%d zero" % bank, "least%d" % k, T.least[:, 8 * k:8 * k + 8], T.least[:, 24:32], scores, 1e29, A.add, A.min)
+            tt("pb%d least%d" % (bank, k), "above%d" % k, T.least[:, 32 + 8 * k:40 + 8 * k], scores, T.least[:, 8 * k:8 * k + 8], A.not_equal)
+            act("pb%d" % bank, "sa%d" % k, T.sa[:, ps], pb[:, 64:128], FN.Copy)
+            tt("pb%d sa%d" % (bank, k), "cb%d" % k, T.cb[:, ps], pb[:, 0:64], T.sa[:, ps], A.is_gt)
+        scan("above0 above1 above2 d8", "ksc", T.ksc[:], T.least[:, 32:56], sm(4), 0.0, A.mult, A.add)
         scan("cb0 cb1 cb2 sign", "pk", T.pk[:], T.sign[:], T.cb[:], 0.0, A.mult, A.add)
         place = T.pk[:, 7:192:8]
-        scan("pk d8", "ksc", T.ksc[:], place, sm(4), 6.5, A.max, A.add)
-        ts("ksc lrp0 lrp1", "rp", T.rp[:], (T.ksc[:], T.lrp[:]), 6.5, A.subtract, BIG, A.mult)
+        cp("ksc lrp0 lrp1", "rp", T.rp[:], (T.ksc[:], T.lrp[:]))
         tr("rp", "rt", T.rt[:], T.rp[:])
         for k in range(3):
-            ts("rt rp", "same%d" % k, T.same[:, 96 * k:96 * k + 96], T.rt[:], T.rp[:, 32 * k:32 * k + 1], A.is_equal)
-        scan("same0 same1 same2 mdup0 mdup1 mdup2", "dup", T.dup[:], T.mdup[:], T.same[:], 0.0, A.mult, A.max)
-        for k in range(3):
-            ts("dup rp k24", "off%d" % k, T.off[:, k:k + 1], T.dup[:, 96 * k + 95:96 * k + 96], col(424 + k), A.mult, T.rp[:, 32 * k:32 * k + 1], A.max)
-        cp("off0 off1 off2 val0 val1 val2", "tab", (T.tab[:], T.off[:, 0:3]), T.val[:])
+            ts("rt ksc", "same%d" % k, T.same[:, 97 * k:97 * k + 96], T.rt[:], T.ksc[:, 8 * k + 7:8 * k + 8], A.is_equal)
+        cp("ksc", "same3", T.same[:, 96:291:97], T.ksc[:, 7:24:8])
+        scan("same0 same1 same2 same3 mdup0 mdup1 mdup2 mdup3", "dup", T.dup[:], T.mdup[:], T.same[:], 0.0, A.mult, A.max)
+        cp("dup", "off", T.off[:, 0:3], T.dup[:, 96:291:97])
+        cp("off val0 val1 val2", "tab", (T.tab[:], T.off[:, 0:3]), T.val[:])
         tr("tab", "tb", T.tb[:], T.tab[:, 0:2 * C])
         if t < 2:
             affine("tab k4%d" % up[t + 1], "tab", T.tab[:, 0:2 * C], T.tab[:, 0:2 * C], 0.0, col(428 + up[t + 1]))
-        affine("ksc", "s5", sm(5, 3), T.ksc[:, 7:24:8], 2.0 ** 38, -(6.5 + 1023.5 / BIG) * 2.0 ** 38)
+        affine("ksc", "s5", sm(5, 3), T.ksc[:, 7:24:8], 2.0 ** 24, -1023.5 * 2.0 ** 24)
         tt("s5 k31", "s6", sm(6, 3), sm(5, 3), cf[:, 536:539], A.max)
         for q in range(4):
             a = 96 * u + 4 * (12 * u + q)
@@ -494,10 +500,8 @@ def rank_program(g, core, T, topo):
             tt("rel", hk + "o%d" % q, hb[32 * q:32 * q + 32, 120 * u:120 * u + 24], T.rel[0:32, :], T.rel[32:64, :], A.min)
         tt("pk th7", "s7", sm(7), place, th7, A.is_ge)
         tt("pk th4", "s8", sm(8), place, th4, A.is_lt)
-        affine("ksc la", "s9", sm(9, 32), (T.ksc[:], T.la[:]), BIG * LS, -(6.5 * BIG + 768) * LS)
-        affine("ksc la", "s10", sm(10, 32), (T.ksc[:], T.la[:]), -BIG, 6.5 * BIG)
+        affine("ksc la", "s9", sm(9, 32), (T.ksc[:], T.la[:]), LS, -NONE)
         tt("s7 s8", "s11", sm(11), sm(7), sm(8), A.add)
-        tt("s10 c_8%d" % u, "s12", sm(12), sm(10), c_8(u, 0), A.add)
         tt("s11 s9", "s13", sm(13), sm(11), sm(9), A.mult)
         tt("s7 s12", "s14", sm(14), sm(7), sm(12), A.mult)
         tt("s13 c_9%d" % u, "s15", sm(15), sm(13), c_8(u, 1), A.add)
@@ -515,7 +519,7 @@ def rank_program(g, core, T, topo):
             quant_x(t + 1, h, T.xt, " ".join("xt%d%d" % (b, h) for b in range(4)))
         if t < 2:
             send_x(t + 1, "outh")
-            unpack(t + 1, True, "VSSV")
+            unpack(t + 1, True, "SSSS")
             unpack(t + 1, False, "SSSS")
         else:
             mm("vq xq30 xq31", 4, T.vq[:], T.vs[:], T.xq3[:], T.xs3[:])

@@ -7,9 +7,8 @@ Q8, U8, BF, F16, F32, I32, U16 = "float8_e4m3fn_x4", "uint8", "bfloat16", "float
 LS = 2048.0
 Z = 2048 * LS
 NONE = 768 * LS
-BIG = 16384.0
-CYCLE, SAME, OTHER, SLACK = 0.83e-3, 0.2, 0.14, 0.03
-ISSUE, FIRST, LOAD, LOADX, NOTE, CODES = 0.25, 2.0, 1.8, 2.6, 1.8, 2.8
+CYCLE, SAME, OTHER, SLACK = 0.83e-3, 0.19, 0.17, 0.03
+ISSUE, FIRST, LOAD, LOADX, NOTE, CODES, NEAR = 0.2, 2.0, 1.5, 2.3, 1.5, 2.6, 2.0
 
 
 def sb(n, d):
@@ -18,22 +17,22 @@ def sb(n, d):
 
 SCRATCH = {
     "xin": sb(4 * C, BF), "xt": sb(4 * C, BF), "yt": sb(4 * C, BF),
-    "ut": sb(512, BF), "vt": sb(512, BF), "e0": sb(528, BF), "et": sb(2048, BF),
+    "ut": sb(512, BF), "vt": sb(512, BF), "e0": sb(528, BF),
     "uq": sb(128, Q8), "us": sb(128, U8), "upq": sb(128, Q8), "ups": sb(128, U8),
     "vq": sb(128, Q8), "vs": sb(128, U8), "eq": sb(512, Q8), "es": sb(512, U8),
     "wq": sb(512, Q8), "wsc": sb(512, U8), "yq": sb(C, Q8), "ys": sb(C, U8),
     "fw": sb(4 * 2 * C, BF), "aw": sb(4 * 2 * C, BF), "ac": sb(4 * C, BF),
     "sa": sb(192, F32), "cb": sb(192, BF), "sign": sb(192, BF), "pk": sb(192, BF), "rl": sb(4 * C, F32), "yo": sb(C, F32),
-    "vgi": sb(24, I32), "ksc": sb(24, F32), "least": sb(56, F32), "p8": sb(96, F32), "ag": sb(96, F32),
+    "vgi": sb(24, I32), "vg2": sb(48, I32), "ksc": sb(32, F32), "least": sb(56, F32), "p8": sb(128, F32), "ag": sb(128, F32),
     "rp": sb(96, F16), "rt": sb(96, F16), "same": sb(291, F16), "mdup": sb(291, F16), "dup": sb(291, F16),
     "val": sb(48, BF), "tab": sb(1024 + 2 * C, BF), "tb": sb(2 * C, BF), "ce": sb(192, F32), "oe": sb(96, F32), "rel": sb(24, F32),
-    "low": sb(48, F32), "sbz": sb(96, F32), "dpn": sb(96, F32), "dps": sb(96, F32), "wf": sb(2 * C, F32),
-    "wr": sb(2 * C + 32, F32), "gv": sb(C, F32), "vt32": sb(544, F32),
+    "low": sb(48, F32), "sbz": sb(96, F32), "dpn": sb(96, F32), "dps": sb(96, F32), "wf": sb(4 * C, F32),
+    "wr": sb(4 * C, F32), "gv": sb(C, F32), "vt32": sb(544, F32),
     "sm": sb(16 * 32, F32), "s0": sb(96, F32), "s1": sb(96, F32), "npt": sb(72, F32), "xo": sb(32, F32),
     "swi": sb(64, F32), "swx": sb(64, F32), "swz": sb(64, F32), "swo": sb(64, F32), "cand": sb(24, U16),
     "ovi": sb(32, F32), "ovo": sb(32, F32),
-    "sc": sb(16, I32), "cf": sb(768, F32), "kk": sb(32, F32), "lu": sb(8, U16),
-    "lsw": sb(4, U16), "lv": sb(2, U16), "lrp": sb(6, U16), "l8": sb(2, U16), "la": sb(2, U16), "off": sb(4, U16), "pp": sb(32, U16),
+    "sc": sb(16, I32), "cf": sb(768, F32), "lu": sb(8, U16),
+    "lsw": sb(4, U16), "lists": sb(12, U16), "off": sb(4, U16), "pp": sb(32, U16),
 }
 for _t in range(4):
     SCRATCH["xq%d" % _t] = sb(C, Q8)
@@ -87,10 +86,10 @@ def rank_program(g, core, T, topo):
         if isinstance(out, tuple):
             return 0.06 + 4 * CYCLE * 16 * out[1].shape[1]
         if isinstance(ins[0], tuple):
-            return 0.07 + 1.75 * CYCLE * 16 * ins[0][1].shape[1]
+            return 0.08 + 1.5 * CYCLE * 16 * ins[0][1].shape[1]
         if per is None:
             per = 0.5 if all(a.dtype in (dt.bfloat16, dt.float16, dt.uint16) for a in [out] + ins) else 1.0
-        return 0.02 + CYCLE * max(64, per * out.shape[1])
+        return 0.025 + CYCLE * max(64, per * out.shape[1])
 
     def tt(r, w, out, a, b, o):
         op("V", r, w, lambda: g.vector.tensor_tensor(out, ap(a), b, o), cycles(out, [a], 1.0 if "pb" in r else 2.0))
@@ -114,7 +113,7 @@ def rank_program(g, core, T, topo):
         op("V", r, w, lambda: g.vector.tensor_tensor_scan(out, a, b, init, o0, o1), cycles(out, [a, b]))
 
     def quant(r, w, q, s, t):
-        op("V", r, w, lambda: g.vector.quantize_mx(q, s, t), 0.02 + 0.22e-3 * t.shape[1])
+        op("V", r, w, lambda: g.vector.quantize_mx(q, s, t), 0.035 + 0.22e-3 * t.shape[1])
 
     def act(r, w, out, a, fn, **kw):
         op("S", r, w, lambda: g.scalar.activation(out, ap(a), fn, **kw), cycles(out, [a], 1.0))
@@ -239,10 +238,10 @@ def rank_program(g, core, T, topo):
     def col(k):
         return cf[:, k:k + 1]
 
-    c_row, c_gm, c_ys, th7, th4 = cf[:, 0:128], cf[:, 352:376], cf[:, 304:352], cf[:, 480:504], cf[:, 504:528]
-    k_j, k_r, k_15, k_q, k_8, k_g, k_odd, c_p = (col(400 + k) for k in range(8))
+    c_row, c_ys, th7, th4 = cf[:, 0:128], cf[:, 304:352], cf[:, 480:504], cf[:, 504:528]
+    k_j, k_15, k_q, k_odd, k_e, k_s, k_8, k_g, k_r, c_p = (col(400 + k) for k in range(10))
+    lv, l8, la, lrp = T.lists[:, 0:2], T.lists[:, 2:4], T.lists[:, 4:6], T.lists[:, 6:12]
     cx = "c_x0 c_x1 c_x2 c_x3"
-    wfk = "wfa wfb wfc wfd wfe wff wfg"
 
     def c_y(t):
         return cf[:, 256 + 24 * up[t]:280 + 24 * up[t]]
@@ -264,7 +263,7 @@ def rank_program(g, core, T, topo):
 
     def send_x(t, r="", sent="sent", left=None):
         send(t, "x", "xq%d0 xq%d1 " % (t, t) + r, [(u8(T["lq%d" % t][:]), u8(T["xq%d" % t][:])), (T["ls%d" % t][:], T["xs%d" % t][:])],
-             "lq%d" % t, CODES, sent, left)
+             "lq%d" % t, CODES if t else NEAR, sent, left)
 
     def half(t, mine):
         return C * int(up[t] == mine)
@@ -273,7 +272,7 @@ def rank_program(g, core, T, topo):
         q, s = ("xq%d" % t, "xs%d" % t) if mine else ("lq%d" % t, "ls%d" % t)
         for b, e in zip((0, 1, 3, 2), queues):
             bank, a = b + (0 if mine else 4), 2 * C * b + half(t, mine)
-            mm("eq %s0 %s1" % (q, q) if mine else "eq " + q, bank, T.eq[:, 128 * b:128 * b + 128], T.es[:, 128 * b:128 * b + 128], T[q][:], T[s][:])
+            mm("eq%d " % b + ("%s0 %s1" % (q, q) if mine else q), bank, T.eq[:, 128 * b:128 * b + 128], T.es[:, 128 * b:128 * b + 128], T[q][:], T[s][:])
             move(e, "pb%d" % bank, "fw%d%d" % (b, mine), T.fw[:, a:a + C], T["pb%d" % bank][:, 0:C], 0.5)
 
     def plane(buf, b):
@@ -304,17 +303,9 @@ def rank_program(g, core, T, topo):
     def to_block(r, a, b):
         cp(r, "swi0", T.swi[:, 0:12], a)
         cp(r, "swi1", T.swi[:, 32:44], b)
-        tr("swi0 swi1", "swx", T.swx[:], T.swi[:])
+        tr("swi0 swi1 swj0 swj1", "swx", T.swx[:], T.swi[:])
         cp("swx lsw0 lsw1", "swz", T.swz[:], (T.swx[:], T.lsw[:]))
         tr("swz", "swo", T.swo[:], T.swz[:])
-
-    def look_up():
-        tr(wfk, "wr", T.wr[:, 0:2 * C], T.wf[:])
-        act("wr wrc cand", "gv1", T.gv[:, H:C], (T.wr[:], T.cand[:, 12:24]), FN.Copy)
-        cp("wr wrc cand", "gv0", T.gv[:, 0:H], (T.wr[:], T.cand[:, 0:12]))
-        for h in range(2):
-            tr("gv%d" % h, "vt%d" % h, T.vt32[:, H * h:H * h + H], T.gv[:, H * h:H * h + H])
-        return T.vt32[:], T.lv[:]
 
     def spread(buf, k):
         move("S", k + "a", k + "b", buf[0:64, 2:96:4], buf[64:128, 0:96:4])
@@ -331,7 +322,7 @@ def rank_program(g, core, T, topo):
         tt(pm + " cd0 cd1", "s0", sm(0), pd(t, 1), c_y(t), A.is_equal)
         move("S", "s0", "s2", sm(2), sm(0), 1024.0)
         tt(pm + " s2", "p8a", T.p8[:, 0:96:4], pd(t, 1), sm(2), A.add)
-        move("S", spread(T.p8, "p8") + " l8", "s3", sm(3, 32), (T.p8[:], T.l8[:]))
+        move("S", spread(T.p8, "p8") + " lists pad0", "s3", sm(3, 32), (T.p8[:], l8))
         tt("s3", "d8", sm(4, 23), sm(3, 23), T.sm[:, 97:120], A.subtract)
         move("S", "s3", "d8", T.sm[:, 135:152:8], T.sm[:, 103:120:8])
         tt("s3 c_8%d" % up[t], "s12", sm(12), c_8(up[t], 0), sm(3), A.subtract)
@@ -355,34 +346,37 @@ def rank_program(g, core, T, topo):
     ip = sc[:, 7:8]
     iota("i_p", ip, [[1, 1]], 0, 1)
     iota("c_row", c_row, [[1, 128]], 0)
-    for k, ops in enumerate(((7, A.bitwise_and), (31, A.bitwise_and), (15, A.bitwise_and), (5, A.arith_shift_right), (8, A.bitwise_and),
-                             (4, A.arith_shift_right), (1, A.bitwise_and))):
-        ts("i_p", "k%d" % k, sc[:, k:k + 1], ip, *ops)
-    cp("k0 k1 k2 k3 k4 k5 k6 i_p", "kf", cf[:, 400:408], sc[:, 0:8])
+    iota("c_p", c_p, [[1, 1]], 0, 1)
     ms("e0", T.e0[:], 0.0)
-    ts("c_row kf e0", "e0", T.e0[:, 3:515:4], c_row, c_p, A.is_equal)
+    ts("c_row c_p e0", "e0", T.e0[:, 3:515:4], c_row, c_p, A.is_equal)
     for b in range(4):
-        move("VS"[b != 0], "e0", "et%d" % b, T.et[:, 512 * b:512 * b + 512], T.e0[:, 3 - b:515 - b])
-    quant("et0 et1 et2 et3", "eq", T.eq[:], T.es[:], T.et[:])
+        quant("e0", "eq%d" % b, T.eq[:, 128 * b:128 * b + 128], T.es[:, 128 * b:128 * b + 128], T.e0[:, 3 - b:515 - b])
+    for k, ops in enumerate(((7, A.bitwise_and), (15, A.bitwise_and), (5, A.arith_shift_right), (1, A.bitwise_and),
+                             (4, A.arith_shift_right, 1, A.bitwise_and), (1, A.arith_shift_right))):
+        ts("i_p", "k%d" % k, sc[:, k:k + 1], ip, *ops)
+    tt("k5 k2", "k6", sc[:, 6:7], sc[:, 5:6], sc[:, 2:3], A.subtract)
+    ts("k6", "k5", sc[:, 5:6], sc[:, 6:7], 3, A.bitwise_and)
+    cp("k0 k1 k2 k3 k4 k5", "kf", cf[:, 400:406], sc[:, 0:6])
+    affine("kf", "k_8", k_8, k_j, -1.0, k_15)
+    affine("kf", "k_g", k_g, k_q, 2.0, k_e)
+    affine("kf", "k_r", k_r, k_e, 16.0, k_15)
     ms("swi0 swi1", T.swi[:], 0.0)
     for k in range(2):
         ts("c_row kf", "lsw%d" % k, T.lsw[:, 2 * k:2 * k + 2], c_row[:, 16 * k:64:32], k_15, A.add)
-    tt("i_p k5", "k8", sc[:, 8:9], ip, sc[:, 5:6], A.add)
-    ts("k8", "k9", sc[:, 9:10], sc[:, 8:9], 1, A.bitwise_and)
-    ts("k9", "k10", col(411), sc[:, 9:10], 8.0, A.add)
-    ts("kf k10", "k11", col(412), k_15, 16.0, A.mult, col(411), A.add)
-    ts("c_row k11", "lv", T.lv[:], c_row[:, 0:2], 256.0, A.mult, col(412), A.add)
-    ts("i_p", "k12", sc[:, 10:11], ip, 1, A.arith_shift_right, 3, A.bitwise_and)
-    ts("k12 kf", "k13", sc[:, 11:12], sc[:, 10:11], k_q, A.subtract, 4.0, A.add)
-    ts("k13", "k14", sc[:, 12:13], sc[:, 11:12], 3, A.bitwise_and)
-    ts("kf", "k15", col(413), k_odd, k_8, A.add, 4.0, A.mult)
-    ts("kf k15", "k16", col(414), k_q, 8.0, A.mult, col(413), A.add)
-    tt("k14 k16", "k17", col(415), sc[:, 12:13], col(414), A.add)
-    ts("c_row k17", "l8", T.l8[:], c_row[:, 0:128:64], col(415), A.add, 95.0, A.min)
-    ts("c_row kf", "la", T.la[:], c_row[:, 7:32:16], k_8, A.add, 23.0, A.min)
-    for e in range(2):
-        cp("c_row", "lrp%d" % e, T.lrp[:, e:6:2], c_row[:, 7:24:8])
-    affine("kf", "k18", col(416), k_8, 2.0, 0.0)
+    affine("kf", "k10", col(410), k_e, -1.0, 0.0)
+    act("kf k10", "k11", col(411), k_odd, FN.Square, bias=col(410))
+    affine("kf k11", "k12", col(412), k_15, 16.0, col(411))
+    affine("c_row k12", "l0", cf[:, 540:542], c_row[:, 0:2], 256.0, col(412))
+    affine("kf k_8", "k13", col(413), k_8, 1.0, k_odd)
+    affine("kf k13", "k14", col(414), col(413), 4.0, k_s)
+    affine("kf k14", "k15", col(415), k_q, 8.0, col(414))
+    affine("c_row k15", "l1", cf[:, 542:544], c_row[:, 0:128:64], 1.0, col(415))
+    affine("c_row k_8", "l2", cf[:, 544:546], c_row[:, 7:32:16], 1.0, k_8)
+    iota("l3", cf[:, 546:552], [[8, 3], [0, 2]], 7)
+    cp("l0 l1 l2 l3", "lists", T.lists[:], cf[:, 540:552])
+    for k, pad in enumerate((T.p8[:, 96:128], T.ag[:, 96:128], T.ksc[:, 24:32], T.vt32[:, C:544], T.least[:, 24:32], T.xo[:], T.ovi[:], T.sbz[:])):
+        fill("pad%d" % k, pad, 0)
+    affine("k_8", "k18", col(416), k_8, 2.0, 0.0)
     affine("kf", "k19", col(417), k_j, 16.0, 0.0)
     for k, o in enumerate((A.max, A.min)):
         ts("c_row k18 k19", "lu%d" % k, T.lu[:, 4 * k:4 * k + 4], c_row[:, 0:128:32], col(416), A.add, col(417), o)
@@ -392,67 +386,67 @@ def rank_program(g, core, T, topo):
     iota("th7", th7, [[0, 3], [-1, 8]], 7)
     iota("th4", th4, [[0, 3], [-1, 8]], 4)
     iota("i_cd", cf[:, 432:456], [[32, 12], [0, 2]], 0)
-    fill("zero", T.least[:, 24:32], 0)
-    affine("i_cd kf", "cd0", cf[:, 256:280], cf[:, 432:456], 1.0, k_r)
+    affine("i_cd k_r", "cd0", cf[:, 256:280], cf[:, 432:456], 1.0, k_r)
     affine("cd0", "cd1", cf[:, 280:304], cf[:, 256:280], 1.0, float(C))
     affine("cd0 cd1", "c_ys", c_ys, cf[:, 256:304], LS, Z)
     affine("kf", "k21", col(419), k_15, LS, Z)
     affine("c_row k21", "c_x0", cf[:, 576:608], c_row[:, 0:128:4], 4 * LS, col(419))
     for k, b in enumerate((C * LS, 1024.0, C * LS + 1024.0)):
         affine("c_x0", "c_x%d" % (k + 1), cf[:, 608 + 32 * k:640 + 32 * k], cf[:, 576:608], 1.0, b)
-    ms("mdup0 mdup1 mdup2 mdup3", T.mdup[:], 1.0)
-    ts("c_row kf", "k22", T.kk[:], c_row[:, 0:32], k_r, A.is_equal, 2047.0, A.mult)
-    for k in range(3):
-        ts("k22", "mdup%d" % k, T.mdup[:, 129 * k:129 * k + 32], T.kk[:], 1.0, A.add)
-    ms("mdup0 mdup1 mdup2", T.mdup[:, 0:291:97], 0.0)
-    affine("kf", "k23", col(420), k_15, 1.0 / 2048, 768.0 / 2048)
-    ts("c_row k23", "mdup3", T.mdup[:, 96:291:97], c_row[:, 0:48:16], 1.0 / 2048, A.mult, col(420), A.add)
-    ts("kf", "k25", col(421), k_r, 0.0, A.not_equal)
+    iota("yo", T.yo[:, 0:291], [[-32, 3], [1, 97]], 0)
+    ts("yo k_r", "mdup0 mdup1", T.mdup[:], T.yo[:, 0:291], k_r, A.is_equal, 1024.0, A.mult)
+    ms("mdup0", T.mdup[:, 0:291:97], -4096.0)
+    ts("c_row kf", "mdup1", T.mdup[:, 96:291:97], c_row[:, 0:48:16], k_15, A.add, 768.0 - 2048.0, A.add)
+    act("k_r", "k25", col(421), k_r, FN.Sign)
     affine("k25", "k26", col(422), col(421), LS, 0.0)
-    affine("kf", "k27", col(423), k_g, 16 * LS, Z - 128 * LS)
-    ts("c_row k27", "k28", cf[:, 528:531], c_row[:, 0:3], 128 * LS, A.mult, col(423), A.add)
-    ts("k28 k25", "k29", cf[:, 532:535], cf[:, 528:531], col(421), A.mult, -Z, A.add)
+    affine("k_g", "k27", col(423), k_g, 16 * LS, Z - 128 * LS)
+    affine("c_row k27", "k28", cf[:, 528:531], c_row[:, 0:3], 128 * LS, col(423))
+    affine("k28 k25", "k29", cf[:, 532:535], cf[:, 528:531], col(421), -Z)
     for k in range(3):
         affine("c_row k26 k29", "val%d" % k, T.val[:, 16 * k:16 * k + 16], c_row[:, 0:16], col(422), col(532 + k))
-    affine("kf", "k30", col(427), c_p, LS, Z - 128 * LS)
+    affine("c_p", "k30", col(427), c_p, LS, Z - 128 * LS)
     affine("c_row k30", "k31", cf[:, 536:539], c_row[:, 0:3], 128 * LS, col(427))
-    ms("ce0 ce1", T.ce[:], 0.0)
     for u in sorted(set(up)):
+        ce = T.ce[:, 96 * u:96 * u + 96]
+        fill("ce%d" % u, ce, 0)
+        select("ce%d" % u, "ce%d" % u, ce, ce, [[0, 24], [1, 4]], A.not_equal, 2 * Z)
+        select("ce%d" % u, "ce%d" % u, ce, ce, [[0, 24], [1, 4]], A.not_equal, Z + (128 + C * u) * LS, -3)
         iota("c_8%d" % u, c_8(u, 0), [[128, 3], [0, 8]], C * u, 1)
         affine("c_8%d" % u, "c_9%d" % u, c_8(u, 1), c_8(u, 0), -LS, NONE)
         affine("k25", "k4%d" % u, col(428 + u), col(421), Z + none_local(u), -Z)
-        ms("ce%d" % u, T.ce[:, 96 * u:96 * u + 96:4], 2 * Z)
-        ms("ce%d" % u, T.ce[:, 96 * u + 3:96 * u + 96:4], Z + (128 + C * u) * LS)
-    affine("et0 et1 k4%d" % up[0], "tab", T.tab[:, 0:2 * C], T.et[:, 0:2 * C], 0.0, col(428 + up[0]))
-    move("S", "et0 et1", wfk, T.wf[:], T.et[:, 0:2 * C], 0.0)
-    ms("s0c", T.s0[:], 0.0)
-    ms("s0c", T.s0[:, 1:96:3], -1.0)
-    ms("sbz", T.sbz[:], 0.0)
-    fill("wrc", T.wr[:, 2 * C:2 * C + 32], Z + NONE)
-    fill("vtc", T.vt32[:, C:544], 0)
-    fill("xo", T.xo[:], 0)
-    fill("ovi", T.ovi[:], 0)
+    affine("xin0 k4%d" % up[0], "tab", T.tab[:, 0:2 * C], T.xin[:, 0:2 * C], 0.0, col(428 + up[0]))
+    for k in range(4):
+        a = (2 * half(0, False) + C * k) % (4 * C)
+        move("S", "e0", "wz%d%d" % (k // 2, k % 2), T.wf[:, a:a + C], T.e0[:, 0:C], 0.0)
+    iota("s0c", T.s0[:], [[0, 32], [-1, 3]], 0)
     quant("ut", "uq", T.uq[:], T.us[:], T.ut[:])
     cp("uq lu0 lu1", "upq", T.upq[:].bitcast(dt.uint32), (T.uq[:].bitcast(dt.uint32), T.lu[:]))
     act("uq lu0 lu1", "ups", T.ups[:], (T.us[:], T.lu[:]), FN.Copy)
     quant("vt", "vq", T.vq[:], T.vs[:], T.vt[:])
 
     unpack(0, True, "SSSS")
+    ts("vgi", "vg1", T.vg2[:, 0:24], T.vgi[:], 0xFFF0, A.bitwise_and)
+    tt("vgi vg1", "vg2", T.vg2[:, 24:48], T.vgi[:], T.vg2[:, 0:24], A.add)
+    affine("kf", "k32", col(430), k_e, 16.0, 0.0)
+    for e in range(2):
+        ts("vg2 k32 swi%d" % e, "swj%d" % e, T.swi[:, 32 * e + 12:32 * e + 24], T.vg2[:, 24 + e:48:2], col(430), A.add)
     to_block("vgi", T.vgi[:, 0:24:2], T.vgi[:, 1:24:2])
     own_pointers(0)
-    a, o = half(0, True), half(0, False)
-    cp("pm00 pm01", "cand", T.cand[:], pd(0, 1))
-    cp("pm00 pm01", "wfa", T.wf[:, a + 8:a + C:16], pd(0, 1))
-    cp("pm00 pm01", "wfb", T.wf[:, a + 9:a + C:32], pd(0, 1)[:, 1:24:2])
-    cp("pm00 pm01", "wfc", T.wf[:, a + 25:a + C:32], pd(0, 1)[:, 0:24:2])
-    to_block("plp0", T.plp0[:, 0:24:2], T.plp0[:, 1:24:2])
-    for k, (at, e) in enumerate(((8, 0), (25, 0), (24, 1), (9, 1))):
-        cp("swo", "wf" + "defg"[k], T.wf[:, o + at:o + C:32], T.swo[:, 32 * e:32 * e + 12])
-    cp("vt0 vt1 vtc lv", "pp", T.pp[:], look_up())
-    unpack(0, False, "SSSV")
+    for e in range(2):
+        cp("swo", "cand%d" % e, T.cand[:, e:24:2], T.swo[:, 32 * e + 12:32 * e + 24])
+    for mine, name in ((True, "vgi"), (False, "plp0")):
+        a = 2 * half(0, mine)
+        for e in range(2):
+            cp(name + " wz%d0 wz%d1" % (mine, mine), "wl%d%d" % (mine, e), T.wf[:, a + 8 + 16 * e:a + 2 * C:32], T[name][:])
+        tr("wl%d0 wl%d1" % (mine, mine), "wm%d" % mine, T.wr[:, a:a + 2 * C], T.wf[:, a:a + 2 * C])
+    cp("wm0 wm1 cand0 cand1", "gv0 gv1", T.gv[:], (T.wr[:], T.cand[:]))
+    tr("gv0 gv1", "vt0 vt1", T.vt32[:, 0:C], T.gv[:])
+    cp("vt0 vt1", "pp", T.pp[:, 0:24], T.vt32[:, 8:C:16])
+    fill("wrc wm0 wm1", T.wr[:, 2 * C:2 * C + 32], Z + NONE)
+    unpack(0, False, "SVSV")
     for b in (0, 1, 3, 2):
         move("S", "fw%d0 fw%d1 pl0" % (b, b), "ac%d" % b, T.ac[:, C * b:C * b + C], (plane(T.fw, b), T.pl0[:]))
-    turns.append([wrote[k] for k in "fw00 ac0 gv1 fw10 ac1 fw30 ac3 ac2".split()])
+    turns.append([wrote[k] for k in "fw00 ac0 ac1 fw30 ac3 ac2".split()])
 
     for t in range(3):
         u = up[t]
@@ -471,19 +465,19 @@ def rank_program(g, core, T, topo):
                 gather_b(t, 2, k, k + 2 - k // 2)
             quant("yt0%d yt1%d yt2%d yt3%d" % (k, k, k, k), "yq%d" % k, T.yq[:, cs], T.ys[:, cs], T.yt[:, 512 * k:512 * k + 512])
             mm("upq ups yq%d" % k, bank, T.yq[:, cs], T.ys[:, cs], T.upq[:], T.ups[:], 128)
-            scan("pb%d zero" % bank, "least%d" % k, T.least[:, 8 * k:8 * k + 8], T.least[:, 24:32], scores, 1e29, A.add, A.min)
+            scan("pb%d pad4" % bank, "least%d" % k, T.least[:, 8 * k:8 * k + 8], T.least[:, 24:32], scores, 1e29, A.add, A.min)
             tt("pb%d least%d" % (bank, k), "above%d" % k, T.least[:, 32 + 8 * k:40 + 8 * k], scores, T.least[:, 8 * k:8 * k + 8], A.not_equal)
             act("pb%d" % bank, "sa%d" % k, T.sa[:, ps], pb[:, 64:128], FN.Copy)
             tt("pb%d sa%d" % (bank, k), "cb%d" % k, T.cb[:, ps], pb[:, 0:64], T.sa[:, ps], A.is_gt)
-        scan("above0 above1 above2 d8", "ksc", T.ksc[:], T.least[:, 32:56], sm(4), 0.0, A.mult, A.add)
+        scan("above0 above1 above2 d8", "ksc", T.ksc[:, 0:24], T.least[:, 32:56], sm(4), 0.0, A.mult, A.add)
         scan("cb0 cb1 cb2 sign", "pk", T.pk[:], T.sign[:], T.cb[:], 0.0, A.mult, A.add)
         place = T.pk[:, 7:192:8]
-        cp("ksc lrp0 lrp1", "rp", T.rp[:], (T.ksc[:], T.lrp[:]))
+        cp("ksc lists pad2", "rp", T.rp[:], (T.ksc[:], lrp))
         tr("rp", "rt", T.rt[:], T.rp[:])
         for k in range(3):
-            ts("rt ksc", "same%d" % k, T.same[:, 97 * k:97 * k + 96], T.rt[:], T.ksc[:, 8 * k + 7:8 * k + 8], A.is_equal)
+            ts("rt ksc", "same%d" % k, T.same[:, 97 * k:97 * k + 96], T.rt[:], T.ksc[:, 8 * k + 7:8 * k + 8], A.is_equal, 1024.0, A.mult)
         cp("ksc", "same3", T.same[:, 96:291:97], T.ksc[:, 7:24:8])
-        scan("same0 same1 same2 same3 mdup0 mdup1 mdup2 mdup3", "dup", T.dup[:], T.mdup[:], T.same[:], 0.0, A.mult, A.max)
+        scan("same0 same1 same2 same3 mdup0 mdup1", "dup", T.dup[:], T.mdup[:], T.same[:], 0.0, A.add, A.max)
         cp("dup", "off", T.off[:, 0:3], T.dup[:, 96:291:97])
         cp("off val0 val1 val2", "tab", (T.tab[:], T.off[:, 0:3]), T.val[:])
         tr("tab", "tb", T.tb[:], T.tab[:, 0:2 * C])
@@ -500,19 +494,19 @@ def rank_program(g, core, T, topo):
             tt("rel", hk + "o%d" % q, hb[32 * q:32 * q + 32, 120 * u:120 * u + 24], T.rel[0:32, :], T.rel[32:64, :], A.min)
         tt("pk th7", "s7", sm(7), place, th7, A.is_ge)
         tt("pk th4", "s8", sm(8), place, th4, A.is_lt)
-        affine("ksc la", "s9", sm(9, 32), (T.ksc[:], T.la[:]), LS, -NONE)
+        affine("ksc lists pad2", "s9", sm(9, 32), (T.ksc[:], la), LS, -NONE)
         tt("s7 s8", "s11", sm(11), sm(7), sm(8), A.add)
         tt("s11 s9", "s13", sm(13), sm(11), sm(9), A.mult)
         tt("s7 s12", "s14", sm(14), sm(7), sm(12), A.mult)
         tt("s13 c_9%d" % u, "s15", sm(15), sm(13), c_8(u, 1), A.add)
         tt("s14 s15", "aga", T.ag[:, 0:96:4], sm(14), sm(15), A.add)
-        move("S", spread(T.ag, "ag") + " l8", "s9", sm(9, 32), (T.ag[:], T.l8[:]))
+        move("S", spread(T.ag, "ag") + " lists pad1", "s9", sm(9, 32), (T.ag[:], l8))
         move("S", "s9", hk + "d", pd(t, 0), sm(9))
         mine = "%so0 %so1 %so2 %so3 %sd pm%d0 pm%d1" % (hk, hk, hk, hk, hk, t, t)
         send(t, "h", mine, [(hb[:, 72 * u:72 * u + 72], hb[:, 72 * u:72 * u + 72])], hk + "r", NOTE)
         for h in range(2):
             for b in range(4):
-                bank, cs, a = 6 + b % 2, slice(H * h, H * h + H), C * b + H * h
+                bank, cs, a = (7, 4, 5, 6)[b], slice(H * h, H * h + H), C * b + H * h
                 mm("wq wsc yq%d yq%d" % (h, h + 1), bank, T.wq[:, 128 * b:128 * b + 128], T.wsc[:, 128 * b:128 * b + 128], T.yq[:, cs], T.ys[:, cs], H)
                 act("pb%d" % bank, "rl%d%d" % (b, h), T.rl[:, a:a + H], T["pb%d" % bank][:, 0:H], FN.Relu, scale=0.03125)
                 tt("pb%d rl%d%d" % (b, b, h), "xt%d%d" % (b, h), T.xt[:, 4 * H * h + b:4 * H * (h + 1):4], T["pb%d" % b][:, cs], T.rl[:, a:a + H], A.add)
@@ -530,29 +524,34 @@ def rank_program(g, core, T, topo):
             dma("Y", "yo", "", T.y[:], T.yo[:], "st")
         old = T.npt[:, 2:72:3] if t else T.vgi[:]
         cp("npt vgi", "own", T.s1[:, 2:72:3], old)
-        tt("npt vgi " + cx, "xo", T.xo[:, 0:24], old, c_x(t, 0, 24), A.add)
+        tt("npt vgi " + cx, "pad5", T.xo[:, 0:24], old, c_x(t, 0, 24), A.add)
         both = mine + " " + hk + "r"
         for e in range(2):
             tt(both, "low%d" % e, T.low[:, e:48:2], hb[:, 0:24], hb[:, 120:144], A.min)
         cp(both, "dpna", T.dpn[:, 0:96:2], hb[:, 24:120:2])
         for e in range(2):
             cp(both, "dpsa%d" % e, T.dps[:, 2 * e:96:4], hb[:, 26 - 2 * e:120:4])
-        tt("low0 low1 c_ys sbz", "sb", T.sbz[:, 1:96:2], T.low[:], c_ys, A.is_equal)
+        tt("low0 low1 c_ys pad7", "sb", T.sbz[:, 1:96:2], T.low[:], c_ys, A.is_equal)
         tt("low0 low1 " + both, "dpnb", T.dpn[:, 1:96:2], T.low[:], hb[:, 25:120:2], A.add)
         for e in range(2):
             tt("low0 " + both, "dpsb%d" % e, T.dps[:, 2 * e + 1:96:4], T.low[:, 0:48:2], hb[:, 27 - 2 * e:120:4], A.add)
-        scan("sb dpna dpnb", "wfa wfd wff", T.wf[:, 0:2 * C:8], T.sbz[:], T.dpn[:], 0.0, A.mult, A.add)
-        scan("sb dpsa0 dpsa1 dpsb0 dpsb1", "wfb wfc wfe wfg", T.wf[:, 1:2 * C:8], T.sbz[:], T.dps[:], 0.0, A.mult, A.add)
-        ts("wfa wfd wff", "cand", T.cand[:], T.wf[:, C * u + 8:C * u + C:16], 1.0 / LS, A.mult, -Z / LS, A.add)
-        v = look_up()
-        tt("vt0 vt1 lv " + cx, "s1a", T.s1[:, 0:96:3], v, c_x(t, 1), A.is_ge)
-        tt("vt0 vt1 lv " + cx, "s1b", T.s1[:, 1:96:3], v, c_x(t, 0), A.is_ge)
-        tt("vt0 vt1 lv xo s0c", "s0d", T.s0[:, 2:96:3], v, T.xo[:], A.subtract)
+        scan("sb dpna dpnb", "wfa wl00 wl01 wl10 wl11", T.wf[:, 0:2 * C:8], T.sbz[:], T.dpn[:], 0.0, A.mult, A.add)
+        scan("sb dpsa0 dpsa1 dpsb0 dpsb1 wm0 wm1", "wfb", T.wf[:, 1:2 * C:8], T.sbz[:], T.dps[:], 0.0, A.mult, A.add)
+        ts("wfa", "cand cand0 cand1", T.cand[:], T.wf[:, C * u + 8:C * u + C:16], 1.0 / LS, A.mult, -Z / LS, A.add)
+        tr("wfa wfb", "wr wm0 wm1", T.wr[:, 0:2 * C], T.wf[:, 0:2 * C])
+        act("wr wrc cand", "gv1", T.gv[:, H:C], (T.wr[:], T.cand[:, 12:24]), FN.Copy)
+        cp("wr wrc cand", "gv0", T.gv[:, 0:H], (T.wr[:], T.cand[:, 0:12]))
+        for h in range(2):
+            tr("gv%d" % h, "vt%d" % h, T.vt32[:, H * h:H * h + H], T.gv[:, H * h:H * h + H])
+        v = T.vt32[:, 8:544], lv
+        tt("vt0 vt1 pad3 lists " + cx, "s1a", T.s1[:, 0:96:3], v, c_x(t, 1), A.is_ge)
+        tt("vt0 vt1 pad3 lists " + cx, "s1b", T.s1[:, 1:96:3], v, c_x(t, 0), A.is_ge)
+        tt("vt0 vt1 pad3 lists pad5 s0c", "s0d", T.s0[:, 2:96:3], v, T.xo[:], A.subtract)
         scan("s1a s1b s0d s0c own", "npt", T.npt[:], T.s0[:, 0:72], T.s1[:, 0:72], 0.0, A.mult, A.add)
         new = T.npt[:, 2:72:3]
         if t == 2:
-            cp("npt", "ovi", T.ovi[:, 0:24], new)
-            tr("ovi", "ovo", T.ovo[:], T.ovi[:])
+            cp("npt", "pad6", T.ovi[:, 0:24], new)
+            tr("pad6", "ovo", T.ovo[:], T.ovi[:])
             for k in range(8):
                 q, e = k // 2, k % 2
                 dma("YS"[e], "ovo", "", T.ov[k:k + 1, :], T.ovo[32 * q:32 * q + 24, 16 * e:16 * e + 16], "st")

@@ -8,7 +8,7 @@ LS = 2048.0
 Z = 2048 * LS
 NONE = 768 * LS
 CYCLE, SAME, OTHER, SLACK = 0.83e-3, 0.19, 0.17, 0.03
-ISSUE, FIRST, LOAD, LOADX, NOTE, CODES, NEAR = 0.2, 2.0, 1.5, 2.3, 1.5, 2.6, 2.0
+ISSUE, FIRST, SECOND, LOAD, LOADX, NOTE, CODES, NEAR = 0.2, 1.4, 0.8, 1.5, 2.3, 1.5, 2.6, 2.0
 
 
 def sb(n, d):
@@ -24,15 +24,16 @@ SCRATCH = {
     "fw": sb(4 * 2 * C, BF), "aw": sb(4 * 2 * C, BF), "ac": sb(4 * C, BF),
     "sa": sb(192, F32), "cb": sb(192, BF), "sign": sb(192, BF), "pk": sb(192, BF), "rl": sb(4 * C, F32), "yo": sb(C, F32),
     "vgi": sb(24, I32), "vg2": sb(48, I32), "ksc": sb(32, F32), "least": sb(56, F32), "p8": sb(128, F32), "ag": sb(128, F32),
+    "fa": sb(128, F32), "fb": sb(96, F32),
     "rp": sb(96, F16), "rt": sb(96, F16), "same": sb(291, F16), "mdup": sb(291, F16), "dup": sb(291, F16),
     "val": sb(48, BF), "tab": sb(1024 + 2 * C, BF), "tb": sb(2 * C, BF), "ce": sb(192, F32), "oe": sb(96, F32), "rel": sb(24, F32),
     "low": sb(48, F32), "sbz": sb(96, F32), "dpn": sb(96, F32), "dps": sb(96, F32), "wf": sb(4 * C, F32),
     "wr": sb(4 * C, F32), "gv": sb(C, F32), "vt32": sb(544, F32),
-    "sm": sb(16 * 32, F32), "s0": sb(96, F32), "s1": sb(96, F32), "npt": sb(72, F32), "xo": sb(32, F32),
+    "sm": sb(16 * 32, F32), "s0": sb(128, F32), "s1": sb(96, F32), "npt": sb(96, F32), "xo": sb(32, F32),
     "swi": sb(64, F32), "swx": sb(64, F32), "swz": sb(64, F32), "swo": sb(64, F32), "cand": sb(24, U16),
     "ovi": sb(32, F32), "ovo": sb(32, F32),
     "sc": sb(16, I32), "cf": sb(768, F32), "lu": sb(8, U16),
-    "lsw": sb(4, U16), "lists": sb(12, U16), "off": sb(4, U16), "pp": sb(32, U16),
+    "lsw": sb(4, U16), "lists": sb(15, U16), "off": sb(4, U16), "pp": sb(32, U16),
 }
 for _t in range(4):
     SCRATCH["xq%d" % _t] = sb(C, Q8)
@@ -47,7 +48,7 @@ for _b in range(8):
     SCRATCH["pb%d" % _b] = ("psum", [128, 512], F32)
 
 SEMAPHORES = (["sV", "sS", "sP", "sG", "sent", "sent0", "st"] + ["ld%d" % i for i in range(7)]
-              + ["a%s%d" % (k, t) for k in "xph" for t in range(3)])
+              + ["a%s%d" % (k, t) for k in "xph" for t in range(3)] + ["ay1", "ay2"])
 
 A = AluOpType
 FN = ActivationFunctionType
@@ -144,18 +145,18 @@ def rank_program(g, core, T, topo):
     def dma(q, r, w, out, a, sem, lat=LOAD):
         op(q, r, w, lambda: eng[q].dma_start(out, a), ISSUE, lat, sem, 16)
 
-    def send(t, kind, r, pairs, lands, flight, sent="sent", left=None):
+    def send(t, kind, r, pairs, lands, flight, sent="sent", left=None, few=None):
         dst = T.cores[rank ^ STEP[t]]
         rid, pid, _ = topo.addr(dst)
         sem = "a%s%d" % (kind, t)
-        calls = []
+        calls, lanes = [], topo.engines(core, dst)[:few]
         for out, a in pairs:
             def call(out=out, a=a):
-                g.remote_dma(out, a, T.sem[sem], T.sem[sent], pid, rid, topo.mask(core, dst))
-            busy = ISSUE if total else FIRST
+                g.remote_dma(out, a, T.sem[sem], T.sem[sent], pid, rid, sum(1 << e for e in lanes))
+            busy = ISSUE if len(total) > 2 else SECOND if total else FIRST
             calls.append(node("G", busy, busy, {wrote[k] for k in r.split()} | set(calls), call))
-            total[sent] = total.get(sent, 0) + len(topo.engines(core, dst))
-        total[sem] = len(pairs) * len(topo.engines(dst, core))
+            total[sent] = total.get(sent, 0) + len(lanes)
+        total[sem] = len(pairs) * len(topo.engines(dst, core)[:few])
         wrote[lands] = node(None, 0.0, flight, calls[-1:], None, sem)
         wrote["out" + kind] = calls[-1]
         if left:
@@ -169,7 +170,7 @@ def rank_program(g, core, T, topo):
         before = [[(d, gap(d, n)) for d in x["deps"]] for n, x in enumerate(nodes)]
         for names in turns:
             for d, n in zip(names, names[1:]):
-                before[n].append((d, 0.0))
+                before[n].append((d, nodes[d]["busy"] - nodes[d]["lat"]))
         after = [[] for x in nodes]
         for n, e in enumerate(before):
             for d, k in e:
@@ -239,16 +240,14 @@ def rank_program(g, core, T, topo):
         return cf[:, k:k + 1]
 
     c_row, c_ys, th7, th4 = cf[:, 0:128], cf[:, 304:352], cf[:, 480:504], cf[:, 504:528]
-    k_j, k_15, k_q, k_odd, k_e, k_s, k_8, k_g, k_r, c_p = (col(400 + k) for k in range(10))
-    lv, l8, la, lrp = T.lists[:, 0:2], T.lists[:, 2:4], T.lists[:, 4:6], T.lists[:, 6:12]
-    cx = "c_x0 c_x1 c_x2 c_x3"
+    k_j, k_15, k_q, k_odd, k_e, k_s, k_h, k_b, k_8, k_g, k_r, c_p = (col(392 + k) for k in range(12))
+    lv, l8, la, lrp, lw = T.lists[:, 0:2], T.lists[:, 2:4], T.lists[:, 4:6], T.lists[:, 6:12], T.lists[:, 12:15]
 
     def c_y(t):
         return cf[:, 256 + 24 * up[t]:280 + 24 * up[t]]
 
-    def c_x(t, k, n=32):
-        a = 576 + 32 * up[t] + 64 * k
-        return cf[:, a:a + n]
+    def c_x(u):
+        return cf[:, 576 + 48 * u:624 + 48 * u]
 
     def c_8(u, k):
         a = 128 + 24 * u + 48 * k
@@ -262,8 +261,11 @@ def rank_program(g, core, T, topo):
         quant(keys, "xq%d%d" % (t, h), T["xq%d" % t][:, H * h:H * h + H], T["xs%d" % t][:, H * h:H * h + H], tile[:, 4 * H * h:4 * H * (h + 1)])
 
     def send_x(t, r="", sent="sent", left=None):
-        send(t, "x", "xq%d0 xq%d1 " % (t, t) + r, [(u8(T["lq%d" % t][:]), u8(T["xq%d" % t][:])), (T["ls%d" % t][:], T["xs%d" % t][:])],
-             "lq%d" % t, CODES if t else NEAR, sent, left)
+        lq, xq, a = T["lq%d" % t], T["xq%d" % t], H if t else 0
+        if t:
+            send(t, "y", "xq%d0" % t, [(u8(lq[:, 0:H]), u8(xq[:, 0:H]))], "lr%d" % t, CODES - 0.8)
+        send(t, "x", "xq%d0 xq%d1 " % (t, t) + r, [(u8(lq[:, a:C]), u8(xq[:, a:C])), (T["ls%d" % t][:], T["xs%d" % t][:])],
+             "lq%d" % t, CODES - 0.5 if t else NEAR, sent, left)
 
     def half(t, mine):
         return C * int(up[t] == mine)
@@ -272,7 +274,7 @@ def rank_program(g, core, T, topo):
         q, s = ("xq%d" % t, "xs%d" % t) if mine else ("lq%d" % t, "ls%d" % t)
         for b, e in zip((0, 1, 3, 2), queues):
             bank, a = b + (0 if mine else 4), 2 * C * b + half(t, mine)
-            mm("eq%d " % b + ("%s0 %s1" % (q, q) if mine else q), bank, T.eq[:, 128 * b:128 * b + 128], T.es[:, 128 * b:128 * b + 128], T[q][:], T[s][:])
+            mm("eq%d " % b + ("%s0 %s1" % (q, q) if mine else q + " lr%d" % t), bank, T.eq[:, 128 * b:128 * b + 128], T.es[:, 128 * b:128 * b + 128], T[q][:], T[s][:])
             move(e, "pb%d" % bank, "fw%d%d" % (b, mine), T.fw[:, a:a + C], T["pb%d" % bank][:, 0:C], 0.5)
 
     def plane(buf, b):
@@ -308,20 +310,20 @@ def rank_program(g, core, T, topo):
         tr("swz", "swo", T.swo[:], T.swz[:])
 
     def spread(buf, k):
-        move("S", k + "a", k + "b", buf[0:64, 2:96:4], buf[64:128, 0:96:4])
-        move("S", k + "a", k + "c", buf[64:128, 2:96:4], buf[0:64, 0:96:4])
+        move("S", k + "a", k + "b", buf[0:64, 1:96:4], buf[64:128, 3:96:4])
+        move("S", k + "a", k + "c", buf[64:128, 1:96:4], buf[0:64, 3:96:4])
         for q in range(4):
             s = 32 * ((q + 1) % 4)
-            move("S", "%sa %sb %sc" % (k, k, k), "%s%d" % (k, q), buf[32 * q:32 * q + 32, 1:96:2], buf[s:s + 32, 0:96:2])
+            move("S", "%sa %sb %sc" % (k, k, k), "%s%d" % (k, q), buf[32 * q:32 * q + 32, 0:96:2], buf[s:s + 32, 1:96:2])
         return " ".join(k + x for x in "abc0123")
 
     def own_pointers(t):
         pm = "pm%d0 pm%d1" % (t, t)
         for e in range(2):
             cp("swo", "pm%d%d" % (t, e), pd(t, 1)[:, e:24:2], T.swo[:, 32 * e:32 * e + 12])
-        tt(pm + " cd0 cd1", "s0", sm(0), pd(t, 1), c_y(t), A.is_equal)
-        move("S", "s0", "s2", sm(2), sm(0), 1024.0)
-        tt(pm + " s2", "p8a", T.p8[:, 0:96:4], pd(t, 1), sm(2), A.add)
+        tt(pm + " cd0 cd1", "hb%dd" % t, pd(t, 0), pd(t, 1), c_y(t), A.is_equal)
+        a = 24 + 48 * up[t]
+        scan(pm + " c_k hb%dd" % t, "p8a p8b p8c", T.p8[:, 1:96:2], cf[:, 704:752], T["hb%d" % t][:, a:a + 48], 0.0, A.mult, A.add)
         move("S", spread(T.p8, "p8") + " lists pad0", "s3", sm(3, 32), (T.p8[:], l8))
         tt("s3", "d8", sm(4, 23), sm(3, 23), T.sm[:, 97:120], A.subtract)
         move("S", "s3", "d8", T.sm[:, 135:152:8], T.sm[:, 103:120:8])
@@ -334,16 +336,17 @@ def rank_program(g, core, T, topo):
     dma("Y", "", "vgi", T.vgi[:], T.vg[:], "ld0")
     dma("Y", "", "xin1", T.xin[:, 4 * H:4 * C], T.x[:, 4 * H:4 * C], "ld1", LOADX)
     cp("vgi", "pl0", T.pl0[:], T.vgi[:])
-    send(0, "p", "vgi", [(T.plp0[:], T.vgi[:])], "plp0", NOTE)
+    send(0, "p", "vgi", [(T.plp0[:], T.vgi[:])], "plp0", NOTE, few=4)
     for h in range(2):
         quant_x(0, h, T.xin, "xin%d" % h)
     send_x(0, "outp", "sent0", "left")
-    dma("Y", "left", "ut", T.ut[:], T.u[:], "ld3", CODES)
+    dma("Y", "", "ut", T.ut[:], T.u[:], "ld3", LOADX)
+    turns.append([wrote[k] for k in "vgi xin1 ut".split()])
     dma("Y", "left", "wq", u8(T.wq[:]), T.wc[:], "ld4", LOADX)
     dma("Y", "left", "wsc", T.wsc[:], T.ws[:], "ld5")
-    dma("Y", "left", "vt", T.vt[:], T.v[:], "ld6")
+    dma("Y", "left", "vt", T.vt[:], T.v[:], "ld6", 4 * LOAD)
 
-    ip = sc[:, 7:8]
+    ip = sc[:, 15:16]
     iota("i_p", ip, [[1, 1]], 0, 1)
     iota("c_row", c_row, [[1, 128]], 0)
     iota("c_p", c_p, [[1, 1]], 0, 1)
@@ -352,11 +355,12 @@ def rank_program(g, core, T, topo):
     for b in range(4):
         quant("e0", "eq%d" % b, T.eq[:, 128 * b:128 * b + 128], T.es[:, 128 * b:128 * b + 128], T.e0[:, 3 - b:515 - b])
     for k, ops in enumerate(((7, A.bitwise_and), (15, A.bitwise_and), (5, A.arith_shift_right), (1, A.bitwise_and),
-                             (4, A.arith_shift_right, 1, A.bitwise_and), (1, A.arith_shift_right))):
+                             (4, A.arith_shift_right, 1, A.bitwise_and), (1, A.arith_shift_right),
+                             (1, A.arith_shift_right, 7, A.bitwise_and), (1, A.arith_shift_right, 1, A.bitwise_and))):
         ts("i_p", "k%d" % k, sc[:, k:k + 1], ip, *ops)
-    tt("k5 k2", "k6", sc[:, 6:7], sc[:, 5:6], sc[:, 2:3], A.subtract)
-    ts("k6", "k5", sc[:, 5:6], sc[:, 6:7], 3, A.bitwise_and)
-    cp("k0 k1 k2 k3 k4 k5", "kf", cf[:, 400:406], sc[:, 0:6])
+    tt("k5 k2", "k9", sc[:, 9:10], sc[:, 5:6], sc[:, 2:3], A.subtract)
+    ts("k9", "k5", sc[:, 5:6], sc[:, 9:10], 3, A.bitwise_and)
+    cp("k0 k1 k2 k3 k4 k5 k6 k7", "kf", cf[:, 392:400], sc[:, 0:8])
     affine("kf", "k_8", k_8, k_j, -1.0, k_15)
     affine("kf", "k_g", k_g, k_q, 2.0, k_e)
     affine("kf", "k_r", k_r, k_e, 16.0, k_15)
@@ -368,12 +372,17 @@ def rank_program(g, core, T, topo):
     affine("kf k11", "k12", col(412), k_15, 16.0, col(411))
     affine("c_row k12", "l0", cf[:, 540:542], c_row[:, 0:2], 256.0, col(412))
     affine("kf k_8", "k13", col(413), k_8, 1.0, k_odd)
-    affine("kf k13", "k14", col(414), col(413), 4.0, k_s)
+    affine("kf", "k16", col(418), k_s, -1.0, 3.0)
+    affine("k13 k16", "k14", col(414), col(413), 4.0, col(418))
     affine("kf k14", "k15", col(415), k_q, 8.0, col(414))
     affine("c_row k15", "l1", cf[:, 542:544], c_row[:, 0:128:64], 1.0, col(415))
     affine("c_row k_8", "l2", cf[:, 544:546], c_row[:, 7:32:16], 1.0, k_8)
     iota("l3", cf[:, 546:552], [[8, 3], [0, 2]], 7)
-    cp("l0 l1 l2 l3", "lists", T.lists[:], cf[:, 540:552])
+    affine("kf k10", "k33", col(556), k_b, 1.0, col(410))
+    act("k33", "k34", col(557), col(556), FN.Square)
+    affine("kf k34", "k35", col(558), k_h, 16.0, col(557))
+    affine("c_row k35", "l4", cf[:, 552:555], c_row[:, 0:3], 128.0, col(558))
+    cp("l0 l1 l2 l3 l4", "lists", T.lists[:], cf[:, 540:555])
     for k, pad in enumerate((T.p8[:, 96:128], T.ag[:, 96:128], T.ksc[:, 24:32], T.vt32[:, C:544], T.least[:, 24:32], T.xo[:], T.ovi[:], T.sbz[:])):
         fill("pad%d" % k, pad, 0)
     affine("k_8", "k18", col(416), k_8, 2.0, 0.0)
@@ -383,6 +392,7 @@ def rank_program(g, core, T, topo):
     fill("sign", T.sign[:], 1)
     select("sign", "sign", T.sign[:], T.sign[:], [[0, 3], [-1, 8], [1, 8]], A.not_equal, -1.0)
     select("sign", "sign", T.sign[:], T.sign[:], [[0, 24], [1, 8]], A.not_equal, 0.0)
+    iota("c_k", cf[:, 704:752], [[0, 24], [1024, 2]], 0)
     iota("th7", th7, [[0, 3], [-1, 8]], 7)
     iota("th4", th4, [[0, 3], [-1, 8]], 4)
     iota("i_cd", cf[:, 432:456], [[32, 12], [0, 2]], 0)
@@ -390,9 +400,9 @@ def rank_program(g, core, T, topo):
     affine("cd0", "cd1", cf[:, 280:304], cf[:, 256:280], 1.0, float(C))
     affine("cd0 cd1", "c_ys", c_ys, cf[:, 256:304], LS, Z)
     affine("kf", "k21", col(419), k_15, LS, Z)
-    affine("c_row k21", "c_x0", cf[:, 576:608], c_row[:, 0:128:4], 4 * LS, col(419))
-    for k, b in enumerate((C * LS, 1024.0, C * LS + 1024.0)):
-        affine("c_x0", "c_x%d" % (k + 1), cf[:, 608 + 32 * k:640 + 32 * k], cf[:, 576:608], 1.0, b)
+    iota("c_x1", c_x(1), [[32, 24], [-1, 2]], 1)
+    affine("c_x1 k21", "c_x0", c_x(0), c_x(1), 1024.0, col(419))
+    affine("c_x0", "c_x1", c_x(1), c_x(0), 1.0, C * LS)
     iota("yo", T.yo[:, 0:291], [[-32, 3], [1, 97]], 0)
     ts("yo k_r", "mdup0 mdup1", T.mdup[:], T.yo[:, 0:291], k_r, A.is_equal, 1024.0, A.mult)
     ms("mdup0", T.mdup[:, 0:291:97], -4096.0)
@@ -418,7 +428,11 @@ def rank_program(g, core, T, topo):
     for k in range(4):
         a = (2 * half(0, False) + C * k) % (4 * C)
         move("S", "e0", "wz%d%d" % (k // 2, k % 2), T.wf[:, a:a + C], T.e0[:, 0:C], 0.0)
-    iota("s0c", T.s0[:], [[0, 32], [-1, 3]], 0)
+    fill("f0", T.fa[:], 1)
+    select("f0", "f0", T.fa[:], T.fa[:], [[0, 32], [1, 4]], A.not_equal, 0.0)
+    iota("s0c", T.s0[:], [[0, 32], [1, 4]], 0)
+    select("s0c", "s0c", T.s0[:], T.s0[:], [[0, 32], [1, 4]], A.not_equal, -1.0, -2)
+    fill("s1c", T.s1[:], 0)
     quant("ut", "uq", T.uq[:], T.us[:], T.ut[:])
     cp("uq lu0 lu1", "upq", T.upq[:].bitcast(dt.uint32), (T.uq[:].bitcast(dt.uint32), T.lu[:]))
     act("uq lu0 lu1", "ups", T.ups[:], (T.us[:], T.lu[:]), FN.Copy)
@@ -442,11 +456,12 @@ def rank_program(g, core, T, topo):
     cp("wm0 wm1 cand0 cand1", "gv0 gv1", T.gv[:], (T.wr[:], T.cand[:]))
     tr("gv0 gv1", "vt0 vt1", T.vt32[:, 0:C], T.gv[:])
     cp("vt0 vt1", "pp", T.pp[:, 0:24], T.vt32[:, 8:C:16])
+    turns.append([wrote[k] for k in "xq01 wm1 swz uq".split()])
     fill("wrc wm0 wm1", T.wr[:, 2 * C:2 * C + 32], Z + NONE)
     unpack(0, False, "SVSV")
     for b in (0, 1, 3, 2):
         move("S", "fw%d0 fw%d1 pl0" % (b, b), "ac%d" % b, T.ac[:, C * b:C * b + C], (plane(T.fw, b), T.pl0[:]))
-    turns.append([wrote[k] for k in "fw00 ac0 ac1 fw30 ac3 ac2".split()])
+    turns.append([wrote[k] for k in "fw00 ac0 fw30 ac1 ac3 ac2".split()])
 
     for t in range(3):
         u = up[t]
@@ -458,17 +473,18 @@ def rank_program(g, core, T, topo):
                 gather_a("S", t, False, b)
         for b in (0, 1, 3):
             gather_b(t, b)
+        gather_b(t, 2, 0, 2)
+        gather_b(t, 2, 2, 3)
         for k in range(3):
             cs, ps, bank = slice(128 * k, 128 * k + 128), slice(64 * k, 64 * k + 64), 4 + k
             pb, scores = T["pb%d" % bank], T["pb%d" % bank][:, 0:64:9]
-            if k != 1:
-                gather_b(t, 2, k, k + 2 - k // 2)
             quant("yt0%d yt1%d yt2%d yt3%d" % (k, k, k, k), "yq%d" % k, T.yq[:, cs], T.ys[:, cs], T.yt[:, 512 * k:512 * k + 512])
             mm("upq ups yq%d" % k, bank, T.yq[:, cs], T.ys[:, cs], T.upq[:], T.ups[:], 128)
             scan("pb%d pad4" % bank, "least%d" % k, T.least[:, 8 * k:8 * k + 8], T.least[:, 24:32], scores, 1e29, A.add, A.min)
             tt("pb%d least%d" % (bank, k), "above%d" % k, T.least[:, 32 + 8 * k:40 + 8 * k], scores, T.least[:, 8 * k:8 * k + 8], A.not_equal)
             act("pb%d" % bank, "sa%d" % k, T.sa[:, ps], pb[:, 64:128], FN.Copy)
             tt("pb%d sa%d" % (bank, k), "cb%d" % k, T.cb[:, ps], pb[:, 0:64], T.sa[:, ps], A.is_gt)
+        turns.append([wrote[k] for k in "yt20 yt22 yq0 yq1 yq2".split()])
         scan("above0 above1 above2 d8", "ksc", T.ksc[:, 0:24], T.least[:, 32:56], sm(4), 0.0, A.mult, A.add)
         scan("cb0 cb1 cb2 sign", "pk", T.pk[:], T.sign[:], T.cb[:], 0.0, A.mult, A.add)
         place = T.pk[:, 7:192:8]
@@ -492,14 +508,12 @@ def rank_program(g, core, T, topo):
         tt("oe", "rel", T.rel[0:64, :], T.oe[0:64, 3:96:4], T.oe[64:128, 3:96:4], A.min)
         for q in range(4):
             tt("rel", hk + "o%d" % q, hb[32 * q:32 * q + 32, 120 * u:120 * u + 24], T.rel[0:32, :], T.rel[32:64, :], A.min)
-        tt("pk th7", "s7", sm(7), place, th7, A.is_ge)
-        tt("pk th4", "s8", sm(8), place, th4, A.is_lt)
-        affine("ksc lists pad2", "s9", sm(9, 32), (T.ksc[:], la), LS, -NONE)
-        tt("s7 s8", "s11", sm(11), sm(7), sm(8), A.add)
-        tt("s11 s9", "s13", sm(13), sm(11), sm(9), A.mult)
-        tt("s7 s12", "s14", sm(14), sm(7), sm(12), A.mult)
-        tt("s13 c_9%d" % u, "s15", sm(15), sm(13), c_8(u, 1), A.add)
-        tt("s14 s15", "aga", T.ag[:, 0:96:4], sm(14), sm(15), A.add)
+        tt("pk th7", "s7", T.fb[:, 1:96:4], place, th7, A.is_ge)
+        tt("pk th4", "s8", T.fb[:, 0:96:4], place, th4, A.is_lt)
+        affine("ksc lists pad2 f0", "s9a", T.fa[:, 2:128:4], (T.ksc[:], la), LS, -NONE)
+        tt("s7 s12", "s14", T.fb[:, 3:96:4], T.fb[:, 1:96:4], sm(12), A.mult)
+        move("S", "c_9%d" % u, "s15", T.fb[:, 2:96:4], c_8(u, 1))
+        scan("s7 s8 s9a s14 s15", "aga agb agc ag0 ag1 ag2 ag3", T.ag[:, 0:96], T.fa[:, 0:96], T.fb[:], 0.0, A.mult, A.add)
         move("S", spread(T.ag, "ag") + " lists pad1", "s9", sm(9, 32), (T.ag[:], l8))
         move("S", "s9", hk + "d", pd(t, 0), sm(9))
         mine = "%so0 %so1 %so2 %so3 %sd pm%d0 pm%d1" % (hk, hk, hk, hk, hk, t, t)
@@ -512,6 +526,7 @@ def rank_program(g, core, T, topo):
                 tt("pb%d rl%d%d" % (b, b, h), "xt%d%d" % (b, h), T.xt[:, 4 * H * h + b:4 * H * (h + 1):4], T["pb%d" % b][:, cs], T.rl[:, a:a + H], A.add)
             quant_x(t + 1, h, T.xt, " ".join("xt%d%d" % (b, h) for b in range(4)))
         if t < 2:
+            turns.append([wrote["xq%d0" % (t + 1)], wrote["xt01"]])
             send_x(t + 1, "outh")
             unpack(t + 1, True, "SSSS")
             unpack(t + 1, False, "SSSS")
@@ -522,9 +537,9 @@ def rank_program(g, core, T, topo):
             for k in range(4):
                 dma("Y", "xq30 xq31", "", T.osc[4 * k:4 * k + 4, :], T.xs3[32 * k:32 * k + 4, :], "st")
             dma("Y", "yo", "", T.y[:], T.yo[:], "st")
-        old = T.npt[:, 2:72:3] if t else T.vgi[:]
-        cp("npt vgi", "own", T.s1[:, 2:72:3], old)
-        tt("npt vgi " + cx, "pad5", T.xo[:, 0:24], old, c_x(t, 0, 24), A.add)
+        old = T.npt[:, 3:96:4] if t else T.vgi[:]
+        cp("npt vgi s1c", "own", T.s1[:, 3:96:4], old)
+        tt("npt vgi c_x%d" % u, "pad5", T.xo[:, 0:24], old, c_x(u)[:, 1:48:2], A.add)
         both = mine + " " + hk + "r"
         for e in range(2):
             tt(both, "low%d" % e, T.low[:, e:48:2], hb[:, 0:24], hb[:, 120:144], A.min)
@@ -544,11 +559,10 @@ def rank_program(g, core, T, topo):
         for h in range(2):
             tr("gv%d" % h, "vt%d" % h, T.vt32[:, H * h:H * h + H], T.gv[:, H * h:H * h + H])
         v = T.vt32[:, 8:544], lv
-        tt("vt0 vt1 pad3 lists " + cx, "s1a", T.s1[:, 0:96:3], v, c_x(t, 1), A.is_ge)
-        tt("vt0 vt1 pad3 lists " + cx, "s1b", T.s1[:, 1:96:3], v, c_x(t, 0), A.is_ge)
-        tt("vt0 vt1 pad3 lists pad5 s0c", "s0d", T.s0[:, 2:96:3], v, T.xo[:], A.subtract)
-        scan("s1a s1b s0d s0c own", "npt", T.npt[:], T.s0[:, 0:72], T.s1[:, 0:72], 0.0, A.mult, A.add)
-        new = T.npt[:, 2:72:3]
+        tt("vt0 vt1 lists s1c c_x%d" % u, "s1a", T.s1[:, 0:96:2], (v[0], lw), c_x(u), A.is_ge)
+        tt("vt0 vt1 pad3 lists pad5 s0c", "s0d", T.s0[:, 3:128:4], v, T.xo[:], A.subtract)
+        scan("s1a s0d s0c own", "npt", T.npt[:], T.s0[:, 0:96], T.s1[:], 0.0, A.mult, A.add)
+        new = T.npt[:, 3:96:4]
         if t == 2:
             cp("npt", "pad6", T.ovi[:, 0:24], new)
             tr("pad6", "ovo", T.ovo[:], T.ovi[:])
@@ -565,7 +579,8 @@ def rank_program(g, core, T, topo):
         gather_a("V", t + 1, True, 2, 12, 24)
         for b, q in zip((0, 1, 3, 2), "VVGG"):
             double(q, t + 1, b)
-        to_block("npt", T.npt[:, 2:72:6], T.npt[:, 5:72:6])
+        to_block("npt", T.npt[:, 3:96:8], T.npt[:, 7:96:8])
         own_pointers(t + 1)
+        turns.append([wrote[k] for k in "swi1 aw210 swx aw211 swz".split()])
 
     issue()

from concourse.mybir import dt, AluOpType, ActivationFunctionType

C = 384
H = C // 2
STEP = [1, 2, 4]
Q8, U8, BF, F16, F32, I32, U16 = "float8_e4m3fn_x4", "uint8", "bfloat16", "float16", "float32", "int32", "uint16"
LS = 2048.0
Z = 2048 * LS
NONE = 768 * LS
CYCLE, SAME, OTHER, SLACK = 0.83e-3, 0.19, 0.17, 0.03
ISSUE, FIRST, SECOND, LOAD, LOADX, NOTE, CODES, NEAR = 0.2, 1.4, 0.8, 1.5, 2.3, 1.5, 2.6, 2.0


def sb(n, d):
    return ("sbuf", [128, n], d)


SCRATCH = {
    "xin": sb(4 * C, BF), "xt": sb(4 * C, BF), "yt": sb(4 * C, BF),
    "ut": sb(512, BF), "vt": sb(512, BF), "e0": sb(528, BF),
    "uq": sb(128, Q8), "us": sb(128, U8), "upq": sb(128, Q8), "ups": sb(128, U8),
    "vq": sb(128, Q8), "vs": sb(128, U8), "eq": sb(512, Q8), "es": sb(512, U8),
    "wq": sb(512, Q8), "wsc": sb(512, U8), "yq": sb(C, Q8), "ys": sb(C, U8),
    "fw": sb(4 * 2 * C, BF), "aw": sb(4 * 2 * C, BF), "ac": sb(4 * C, BF),
    "sa": sb(192, F32), "cb": sb(192, BF), "sign": sb(192, BF), "pk": sb(192, BF), "rl": sb(4 * C, F32), "yo": sb(C, F32),
    "vgi": sb(24, I32), "vg2": sb(48, I32), "ksc": sb(32, F32), "least": sb(56, F32), "p8": sb(128, F32), "ag": sb(128, F32),
    "fa": sb(128, F32), "fb": sb(96, F32),
    "rp": sb(96, F16), "rt": sb(96, F16), "same": sb(291, F16), "mdup": sb(291, F16), "dup": sb(291, F16),
    "val": sb(48, BF), "tab": sb(1024 + 2 * C, BF), "tb": sb(2 * C, BF), "ce": sb(192, F32), "oe": sb(96, F32), "rel": sb(24, F32),
    "low": sb(48, F32), "sbz": sb(96, F32), "dpn": sb(96, F32), "dps": sb(96, F32), "wf": sb(4 * C, F32),
    "wr": sb(4 * C, F32), "gv": sb(C, F32), "vt32": sb(544, F32),
    "sm": sb(16 * 32, F32), "s0": sb(128, F32), "s1": sb(96, F32), "npt": sb(96, F32), "xo": sb(32, F32),
    "swi": sb(64, F32), "swx": sb(64, F32), "swz": sb(64, F32), "swo": sb(64, F32), "cand": sb(24, U16),
    "ovi": sb(32, F32), "ovo": sb(32, F32),
    "sc": sb(16, I32), "cf": sb(768, F32), "lu": sb(8, U16),
    "lsw": sb(4, U16), "lists": sb(15, U16), "off": sb(4, U16), "pp": sb(32, U16),
}
for _t in range(4):
    SCRATCH["xq%d" % _t] = sb(C, Q8)
    SCRATCH["xs%d" % _t] = sb(C, U8)
for _t in range(3):
    SCRATCH["lq%d" % _t] = sb(C, Q8)
    SCRATCH["ls%d" % _t] = sb(C, U8)
    SCRATCH["pl%d" % _t] = sb(24, U16)
    SCRATCH["plp%d" % _t] = sb(24, U16 if _t else I32)
    SCRATCH["hb%d" % _t] = sb(144, F32)
for _b in range(8):
    SCRATCH["pb%d" % _b] = ("psum", [128, 512], F32)

SEMAPHORES = (["sV", "sS", "sP", "sG", "sent", "sent0", "st"] + ["ld%d" % i for i in range(7)]
              + ["a%s%d" % (k, t) for k in "xph" for t in range(3)] + ["ay1", "ay2"])

A = AluOpType
FN = ActivationFunctionType


def rank_program(g, core, T, topo):
    rank = T.rank_of(core)
    if rank is None:
        return
    eng = {"V": g.vector, "S": g.scalar, "P": g.tensor, "G": g, "Y": g.sync}
    nodes, wrote, read, total, turns = [], {}, {}, {}, []

    def node(q, busy, lat, deps, call=None, sem=None, inc=0):
        nodes.append(dict(q=q, busy=busy, lat=lat, deps=sorted(deps), call=call, sem=sem, inc=inc))
        return len(nodes) - 1

    def op(q, r, w, call, busy, lat=None, sem=None, inc=1):
        r, w = r.split(), w.split()
        deps = {wrote[k] for k in r + w if k in wrote}
        for k in w:
            deps |= set(read.get(k, []))
        for k in r:
            if k.startswith("pb"):
                deps |= {x for x in read.get(k, []) if nodes[x]["q"] != q}
        n = node(q, busy, lat or busy, deps, call, sem or "s" + q, inc)
        for k in r:
            read.setdefault(k, []).append(n)
        for k in w:
            wrote[k] = n
            read[k] = []

    def ap(a):
        return a[0].indirect(a[1]) if isinstance(a, tuple) else a

    def cycles(out, ins, per=None):
        if isinstance(out, tuple):
            return 0.06 + 4 * CYCLE * 16 * out[1].shape[1]
        if isinstance(ins[0], tuple):
            return 0.08 + 1.5 * CYCLE * 16 * ins[0][1].shape[1]
        if per is None:
            per = 0.5 if all(a.dtype in (dt.bfloat16, dt.float16, dt.uint16) for a in [out] + ins) else 1.0
        return 0.025 + CYCLE * max(64, per * out.shape[1])

    def tt(r, w, out, a, b, o):
        op("V", r, w, lambda: g.vector.tensor_tensor(out, ap(a), b, o), cycles(out, [a], 1.0 if "pb" in r else 2.0))

    def ts(r, w, out, a, s1, o1, s2=None, o2=None):
        if o2 is None:
            op("V", r, w, lambda: g.vector.tensor_scalar(out, ap(a), s1, None, o1), cycles(out, [a]))
        else:
            op("V", r, w, lambda: g.vector.tensor_scalar(out, ap(a), s1, s2, o1, o2), cycles(out, [a]))

    def cp(r, w, out, a):
        op("V", r, w, lambda: g.vector.tensor_copy(ap(out), ap(a)), cycles(out, [a]))

    def tr(r, w, out, a):
        op("V", r, w, lambda: g.vector.transpose(out, a), cycles(out, [a]))

    def ms(w, out, v):
        op("V", "", w, lambda: g.vector.memset(out, v), cycles(out, [out]))

    def scan(r, w, out, a, b, init, o0, o1):
        op("V", r, w, lambda: g.vector.tensor_tensor_scan(out, a, b, init, o0, o1), cycles(out, [a, b]))

    def quant(r, w, q, s, t):
        op("V", r, w, lambda: g.vector.quantize_mx(q, s, t), 0.035 + 0.22e-3 * t.shape[1])

    def act(r, w, out, a, fn, **kw):
        op("S", r, w, lambda: g.scalar.activation(out, ap(a), fn, **kw), cycles(out, [a], 1.0))

    def affine(r, w, out, a, k, b):
        act(r, w, out, a, FN.Identity, scale=k, bias=b)

    def move(q, r, w, out, a, k=1.0):
        if q == "S":
            act(r, w, out, a, FN.Copy, scale=k)
        elif k == 1.0:
            cp(r, w, out, a)
        else:
            ts(r, w, out, a, k, A.mult)

    def mm(r, bank, wq, ws, xq, xs, n=C):
        op("P", r, "pb%d" % bank, lambda: g.tensor.matmul_mx(T["pb%d" % bank][:, 0:n], wq, ws, xq, xs, True, True), 0.07 + 0.75 * CYCLE * n)

    def iota(w, out, pattern, base, cm=0):
        op("G", "", w, lambda: g.iota(out, pattern, int(base), cm, allow_small_or_imprecise_dtypes=True), 0.14 + 2 * CYCLE * out.shape[1])

    def fill(w, out, v):
        iota(w, out, [[0, out.shape[1]]], v)

    def select(r, w, out, a, pattern, cmp, other, base=0):
        op("G", r, w, lambda: g.affine_select(out, a, pattern, cmp, other, base, 0), 0.18 + 2 * CYCLE * out.shape[1])

    def dma(q, r, w, out, a, sem, lat=LOAD):
        op(q, r, w, lambda: eng[q].dma_start(out, a), ISSUE, lat, sem, 16)

    def send(t, kind, r, pairs, lands, flight, sent="sent", left=None, few=None):
        dst = T.cores[rank ^ STEP[t]]
        rid, pid, _ = topo.addr(dst)
        sem = "a%s%d" % (kind, t)
        calls, lanes = [], topo.engines(core, dst)[:few]
        for out, a in pairs:
            def call(out=out, a=a):
                g.remote_dma(out, a, T.sem[sem], T.sem[sent], pid, rid, sum(1 << e for e in lanes))
            busy = ISSUE if len(total) > 2 else SECOND if total else FIRST
            calls.append(node("G", busy, busy, {wrote[k] for k in r.split()} | set(calls), call))
            total[sent] = total.get(sent, 0) + len(lanes)
        total[sem] = len(pairs) * len(topo.engines(dst, core)[:few])
        wrote[lands] = node(None, 0.0, flight, calls[-1:], None, sem)
        wrote["out" + kind] = calls[-1]
        if left:
            wrote[left] = node(None, 0.0, flight - 1.0, calls[-1:], None, sent)

    def issue():
        def gap(d, n):
            a, b = nodes[d]["q"], nodes[n]["q"]
            return 0.0 if a is None or b is None or nodes[d]["sem"] is None else SAME if a == b else OTHER

        before = [[(d, gap(d, n)) for d in x["deps"]] for n, x in enumerate(nodes)]
        for names in turns:
            for d, n in zip(names, names[1:]):
                before[n].append((d, nodes[d]["busy"] - nodes[d]["lat"]))
        after = [[] for x in nodes]
        for n, e in enumerate(before):
            for d, k in e:
                after[d].append((n, k))

        def lay(urgent, back):
            pre, post = (after, before) if back else (before, after)
            need = [len(e) for e in pre]
            ready, at, taken = {n for n, k in enumerate(need) if k == 0}, {}, {q: [] for q in eng}
            while ready:
                n = min(ready, key=lambda n: (urgent[n], n))
                ready.remove(n)
                x = nodes[n]
                shift = x["lat"] - x["busy"] if back else 0.0
                s = max([0.0] + [at[d] + nodes[d]["lat"] + k for d, k in pre[n]]) + shift
                if x["q"]:
                    for a, b in taken[x["q"]]:
                        if s + x["busy"] <= a + SLACK:
                            break
                        s = max(s, b)
                    taken[x["q"]].append((s, s + x["busy"]))
                    taken[x["q"]].sort()
                at[n] = s - shift
                for m, k in post[n]:
                    need[m] -= 1
                    if need[m] == 0:
                        ready.add(m)
            end = max(at[n] + x["lat"] for n, x in enumerate(nodes))
            return [end - at[n] - x["lat"] if back else at[n] for n, x in enumerate(nodes)]

        start = lay(lay([-n for n in range(len(nodes))], True), False)
        count, known, token = dict(total), {q: {} for q in eng}, {}

        def wait(q, toks):
            need = {}
            for s, k in toks:
                need[s] = max(need.get(s, 0), k)
            for s, k in need.items():
                if known[q].get(s, 0) < k:
                    eng[q].wait_ge(T.sem[s], k)
                    known[q][s] = k

        for n in sorted(range(len(nodes)), key=lambda n: (start[n], n)):
            x = nodes[n]
            if x["q"] is None:
                token[n] = (x["sem"], total[x["sem"]])
                continue
            wait(x["q"], [token[d] for d in x["deps"] if d in token])
            if x["sem"] is None:
                x["call"]()
            else:
                count[x["sem"]] = count.get(x["sem"], 0) + x["inc"]
                x["call"]().then_inc(T.sem[x["sem"]], x["inc"])
                token[n] = (x["sem"], count[x["sem"]])
        wait("G", list(count.items()))

    def u8(v):
        return v.bitcast(dt.uint8)

    def sm(i, n=24):
        return T.sm[:, 32 * i:32 * i + n]

    up = [int((rank & s) != 0) for s in STEP]
    cf, sc = T.cf, T.sc

    def col(k):
        return cf[:, k:k + 1]

    c_row, c_ys, th7, th4 = cf[:, 0:128], cf[:, 304:352], cf[:, 480:504], cf[:, 504:528]
    k_j, k_15, k_q, k_odd, k_e, k_s, k_h, k_b, k_8, k_g, k_r, c_p = (col(392 + k) for k in range(12))
    lv, l8, la, lrp, lw = T.lists[:, 0:2], T.lists[:, 2:4], T.lists[:, 4:6], T.lists[:, 6:12], T.lists[:, 12:15]

    def c_y(t):
        return cf[:, 256 + 24 * up[t]:280 + 24 * up[t]]

    def c_x(u):
        return cf[:, 576 + 48 * u:624 + 48 * u]

    def c_8(u, k):
        a = 128 + 24 * u + 48 * k
        return cf[:, a:a + 24]

    def pd(t, k):
        a = 24 + 48 * up[t] + k
        return T["hb%d" % t][:, a:a + 47:2]

    def quant_x(t, h, tile, keys):
        quant(keys, "xq%d%d" % (t, h), T["xq%d" % t][:, H * h:H * h + H], T["xs%d" % t][:, H * h:H * h + H], tile[:, 4 * H * h:4 * H * (h + 1)])

    def send_x(t, r="", sent="sent", left=None):
        lq, xq, a = T["lq%d" % t], T["xq%d" % t], H if t else 0
        if t:
            send(t, "y", "xq%d0" % t, [(u8(lq[:, 0:H]), u8(xq[:, 0:H]))], "lr%d" % t, CODES - 0.8)
        send(t, "x", "xq%d0 xq%d1 " % (t, t) + r, [(u8(lq[:, a:C]), u8(xq[:, a:C])), (T["ls%d" % t][:], T["xs%d" % t][:])],
             "lq%d" % t, CODES - 0.5 if t else NEAR, sent, left)

    def half(t, mine):
        return C * int(up[t] == mine)

    def unpack(t, mine, queues):
        q, s = ("xq%d" % t, "xs%d" % t) if mine else ("lq%d" % t, "ls%d" % t)
        for b, e in zip((0, 1, 3, 2), queues):
            bank, a = b + (0 if mine else 4), 2 * C * b + half(t, mine)
            mm("eq%d " % b + ("%s0 %s1" % (q, q) if mine else q + " lr%d" % t), bank, T.eq[:, 128 * b:128 * b + 128], T.es[:, 128 * b:128 * b + 128], T[q][:], T[s][:])
            move(e, "pb%d" % bank, "fw%d%d" % (b, mine), T.fw[:, a:a + C], T["pb%d" % bank][:, 0:C], 0.5)

    def plane(buf, b):
        return buf[:, 2 * C * b:2 * C * (b + 1)]

    def gather_a(q, t, mine, b, lo=0, hi=24):
        name = ("pl%d" if mine else "plp%d") % t
        a = 2 * C * b + half(t, mine)
        w = " ".join("aw%d%d%d" % (b, mine, k) for k in range(lo // 12, hi // 12))
        move(q, "fw%d0 fw%d1 %s" % (b, b, name), w, T.aw[:, a + 16 * lo:a + 16 * hi], (plane(T.fw, b), T[name][:, lo:hi]))

    def double(q, t, b):
        a = 2 * C * b + half(t, True)
        r, w, out, src = "aw%d10 aw%d11" % (b, b), "ac%d" % b, T.ac[:, C * b:C * b + C], T.aw[:, a:a + C]
        if q == "G":
            select(r, w, out, src, [[0, C]], A.is_gt, 0.0, 1)
        else:
            move(q, r, w, out, src)

    def gather_b(t, b, lo=0, hi=3):
        if t == 0:
            r, win, lst = "fw%d0 fw%d1 pp" % (b, b), plane(T.fw, b), T.pp
        else:
            r, win, lst = " ".join("aw%d%d%d" % (b, m, k) for m in range(2) for k in range(2)) + " pl%d" % t, plane(T.aw, b), T["pl%d" % t]
        tt(r + " ac%d" % b, " ".join("yt%d%d" % (b, k) for k in range(lo, hi)), T.yt[:, 512 * lo + b:512 * hi:4],
           (win, lst[:, 8 * lo:8 * hi]), T.ac[:, C * b + 128 * lo:C * b + 128 * hi], A.add)

    def to_block(r, a, b):
        cp(r, "swi0", T.swi[:, 0:12], a)
        cp(r, "swi1", T.swi[:, 32:44], b)
        tr("swi0 swi1 swj0 swj1", "swx", T.swx[:], T.swi[:])
        cp("swx lsw0 lsw1", "swz", T.swz[:], (T.swx[:], T.lsw[:]))
        tr("swz", "swo", T.swo[:], T.swz[:])

    def spread(buf, k):
        move("S", k + "a", k + "b", buf[0:64, 1:96:4], buf[64:128, 3:96:4])
        move("S", k + "a", k + "c", buf[64:128, 1:96:4], buf[0:64, 3:96:4])
        for q in range(4):
            s = 32 * ((q + 1) % 4)
            move("S", "%sa %sb %sc" % (k, k, k), "%s%d" % (k, q), buf[32 * q:32 * q + 32, 0:96:2], buf[s:s + 32, 1:96:2])
        return " ".join(k + x for x in "abc0123")

    def own_pointers(t):
        pm = "pm%d0 pm%d1" % (t, t)
        for e in range(2):
            cp("swo", "pm%d%d" % (t, e), pd(t, 1)[:, e:24:2], T.swo[:, 32 * e:32 * e + 12])
        tt(pm + " cd0 cd1", "hb%dd" % t, pd(t, 0), pd(t, 1), c_y(t), A.is_equal)
        a = 24 + 48 * up[t]
        scan(pm + " c_k hb%dd" % t, "p8a p8b p8c", T.p8[:, 1:96:2], cf[:, 704:752], T["hb%d" % t][:, a:a + 48], 0.0, A.mult, A.add)
        move("S", spread(T.p8, "p8") + " lists pad0", "s3", sm(3, 32), (T.p8[:], l8))
        tt("s3", "d8", sm(4, 23), sm(3, 23), T.sm[:, 97:120], A.subtract)
        move("S", "s3", "d8", T.sm[:, 135:152:8], T.sm[:, 103:120:8])
        tt("s3 c_8%d" % up[t], "s12", sm(12), c_8(up[t], 0), sm(3), A.subtract)

    def none_local(u):
        return NONE - (128 + C * u) * LS

    dma("S", "", "xin0", T.xin[:, 0:4 * H], T.x[:, 0:4 * H], "ld2", LOADX)
    dma("Y", "", "vgi", T.vgi[:], T.vg[:], "ld0")
    dma("Y", "", "xin1", T.xin[:, 4 * H:4 * C], T.x[:, 4 * H:4 * C], "ld1", LOADX)
    cp("vgi", "pl0", T.pl0[:], T.vgi[:])
    send(0, "p", "vgi", [(T.plp0[:], T.vgi[:])], "plp0", NOTE, few=4)
    for h in range(2):
        quant_x(0, h, T.xin, "xin%d" % h)
    send_x(0, "outp", "sent0", "left")
    dma("Y", "", "ut", T.ut[:], T.u[:], "ld3", LOADX)
    turns.append([wrote[k] for k in "vgi xin1 ut".split()])
    dma("Y", "left", "wq", u8(T.wq[:]), T.wc[:], "ld4", LOADX)
    dma("Y", "left", "wsc", T.wsc[:], T.ws[:], "ld5")
    dma("Y", "left", "vt", T.vt[:], T.v[:], "ld6", 4 * LOAD)

    ip = sc[:, 15:16]
    iota("i_p", ip, [[1, 1]], 0, 1)
    iota("c_row", c_row, [[1, 128]], 0)
    iota("c_p", c_p, [[1, 1]], 0, 1)
    ms("e0", T.e0[:], 0.0)
    ts("c_row c_p e0", "e0", T.e0[:, 3:515:4], c_row, c_p, A.is_equal)
    for b in range(4):
        quant("e0", "eq%d" % b, T.eq[:, 128 * b:128 * b + 128], T.es[:, 128 * b:128 * b + 128], T.e0[:, 3 - b:515 - b])
    for k, ops in enumerate(((7, A.bitwise_and), (15, A.bitwise_and), (5, A.arith_shift_right), (1, A.bitwise_and),
                             (4, A.arith_shift_right, 1, A.bitwise_and), (1, A.arith_shift_right),
                             (1, A.arith_shift_right, 7, A.bitwise_and), (1, A.arith_shift_right, 1, A.bitwise_and))):
        ts("i_p", "k%d" % k, sc[:, k:k + 1], ip, *ops)
    tt("k5 k2", "k9", sc[:, 9:10], sc[:, 5:6], sc[:, 2:3], A.subtract)
    ts("k9", "k5", sc[:, 5:6], sc[:, 9:10], 3, A.bitwise_and)
    cp("k0 k1 k2 k3 k4 k5 k6 k7", "kf", cf[:, 392:400], sc[:, 0:8])
    affine("kf", "k_8", k_8, k_j, -1.0, k_15)
    affine("kf", "k_g", k_g, k_q, 2.0, k_e)
    affine("kf", "k_r", k_r, k_e, 16.0, k_15)
    ms("swi0 swi1", T.swi[:], 0.0)
    for k in range(2):
        ts("c_row kf", "lsw%d" % k, T.lsw[:, 2 * k:2 * k + 2], c_row[:, 16 * k:64:32], k_15, A.add)
    affine("kf", "k10", col(410), k_e, -1.0, 0.0)
    act("kf k10", "k11", col(411), k_odd, FN.Square, bias=col(410))
    affine("kf k11", "k12", col(412), k_15, 16.0, col(411))
    affine("c_row k12", "l0", cf[:, 540:542], c_row[:, 0:2], 256.0, col(412))
    affine("kf k_8", "k13", col(413), k_8, 1.0, k_odd)
    affine("kf", "k16", col(418), k_s, -1.0, 3.0)
    affine("k13 k16", "k14", col(414), col(413), 4.0, col(418))
    affine("kf k14", "k15", col(415), k_q, 8.0, col(414))
    affine("c_row k15", "l1", cf[:, 542:544], c_row[:, 0:128:64], 1.0, col(415))
    affine("c_row k_8", "l2", cf[:, 544:546], c_row[:, 7:32:16], 1.0, k_8)
    iota("l3", cf[:, 546:552], [[8, 3], [0, 2]], 7)
    affine("kf k10", "k33", col(556), k_b, 1.0, col(410))
    act("k33", "k34", col(557), col(556), FN.Square)
    affine("kf k34", "k35", col(558), k_h, 16.0, col(557))
    affine("c_row k35", "l4", cf[:, 552:555], c_row[:, 0:3], 128.0, col(558))
    cp("l0 l1 l2 l3 l4", "lists", T.lists[:], cf[:, 540:555])
    for k, pad in enumerate((T.p8[:, 96:128], T.ag[:, 96:128], T.ksc[:, 24:32], T.vt32[:, C:544], T.least[:, 24:32], T.xo[:], T.ovi[:], T.sbz[:])):
        fill("pad%d" % k, pad, 0)
    affine("k_8", "k18", col(416), k_8, 2.0, 0.0)
    affine("kf", "k19", col(417), k_j, 16.0, 0.0)
    for k, o in enumerate((A.max, A.min)):
        ts("c_row k18 k19", "lu%d" % k, T.lu[:, 4 * k:4 * k + 4], c_row[:, 0:128:32], col(416), A.add, col(417), o)
    fill("sign", T.sign[:], 1)
    select("sign", "sign", T.sign[:], T.sign[:], [[0, 3], [-1, 8], [1, 8]], A.not_equal, -1.0)
    select("sign", "sign", T.sign[:], T.sign[:], [[0, 24], [1, 8]], A.not_equal, 0.0)
    iota("c_k", cf[:, 704:752], [[0, 24], [1024, 2]], 0)
    iota("th7", th7, [[0, 3], [-1, 8]], 7)
    iota("th4", th4, [[0, 3], [-1, 8]], 4)
    iota("i_cd", cf[:, 432:456], [[32, 12], [0, 2]], 0)
    affine("i_cd k_r", "cd0", cf[:, 256:280], cf[:, 432:456], 1.0, k_r)
    affine("cd0", "cd1", cf[:, 280:304], cf[:, 256:280], 1.0, float(C))
    affine("cd0 cd1", "c_ys", c_ys, cf[:, 256:304], LS, Z)
    affine("kf", "k21", col(419), k_15, LS, Z)
    iota("c_x1", c_x(1), [[32, 24], [-1, 2]], 1)
    affine("c_x1 k21", "c_x0", c_x(0), c_x(1), 1024.0, col(419))
    affine("c_x0", "c_x1", c_x(1), c_x(0), 1.0, C * LS)
    iota("yo", T.yo[:, 0:291], [[-32, 3], [1, 97]], 0)
    ts("yo k_r", "mdup0 mdup1", T.mdup[:], T.yo[:, 0:291], k_r, A.is_equal, 1024.0, A.mult)
    ms("mdup0", T.mdup[:, 0:291:97], -4096.0)
    ts("c_row kf", "mdup1", T.mdup[:, 96:291:97], c_row[:, 0:48:16], k_15, A.add, 768.0 - 2048.0, A.add)
    act("k_r", "k25", col(421), k_r, FN.Sign)
    affine("k25", "k26", col(422), col(421), LS, 0.0)
    affine("k_g", "k27", col(423), k_g, 16 * LS, Z - 128 * LS)
    affine("c_row k27", "k28", cf[:, 528:531], c_row[:, 0:3], 128 * LS, col(423))
    affine("k28 k25", "k29", cf[:, 532:535], cf[:, 528:531], col(421), -Z)
    for k in range(3):
        affine("c_row k26 k29", "val%d" % k, T.val[:, 16 * k:16 * k + 16], c_row[:, 0:16], col(422), col(532 + k))
    affine("c_p", "k30", col(427), c_p, LS, Z - 128 * LS)
    affine("c_row k30", "k31", cf[:, 536:539], c_row[:, 0:3], 128 * LS, col(427))
    for u in sorted(set(up)):
        ce = T.ce[:, 96 * u:96 * u + 96]
        fill("ce%d" % u, ce, 0)
        select("ce%d" % u, "ce%d" % u, ce, ce, [[0, 24], [1, 4]], A.not_equal, 2 * Z)
        select("ce%d" % u, "ce%d" % u, ce, ce, [[0, 24], [1, 4]], A.not_equal, Z + (128 + C * u) * LS, -3)
        iota("c_8%d" % u, c_8(u, 0), [[128, 3], [0, 8]], C * u, 1)
        affine("c_8%d" % u, "c_9%d" % u, c_8(u, 1), c_8(u, 0), -LS, NONE)
        affine("k25", "k4%d" % u, col(428 + u), col(421), Z + none_local(u), -Z)
    affine("xin0 k4%d" % up[0], "tab", T.tab[:, 0:2 * C], T.xin[:, 0:2 * C], 0.0, col(428 + up[0]))
    for k in range(4):
        a = (2 * half(0, False) + C * k) % (4 * C)
        move("S", "e0", "wz%d%d" % (k // 2, k % 2), T.wf[:, a:a + C], T.e0[:, 0:C], 0.0)
    fill("f0", T.fa[:], 1)
    select("f0", "f0", T.fa[:], T.fa[:], [[0, 32], [1, 4]], A.not_equal, 0.0)
    iota("s0c", T.s0[:], [[0, 32], [1, 4]], 0)
    select("s0c", "s0c", T.s0[:], T.s0[:], [[0, 32], [1, 4]], A.not_equal, -1.0, -2)
    fill("s1c", T.s1[:], 0)
    quant("ut", "uq", T.uq[:], T.us[:], T.ut[:])
    cp("uq lu0 lu1", "upq", T.upq[:].bitcast(dt.uint32), (T.uq[:].bitcast(dt.uint32), T.lu[:]))
    act("uq lu0 lu1", "ups", T.ups[:], (T.us[:], T.lu[:]), FN.Copy)
    quant("vt", "vq", T.vq[:], T.vs[:], T.vt[:])

    unpack(0, True, "SSSS")
    ts("vgi", "vg1", T.vg2[:, 0:24], T.vgi[:], 0xFFF0, A.bitwise_and)
    tt("vgi vg1", "vg2", T.vg2[:, 24:48], T.vgi[:], T.vg2[:, 0:24], A.add)
    affine("kf", "k32", col(430), k_e, 16.0, 0.0)
    for e in range(2):
        ts("vg2 k32 swi%d" % e, "swj%d" % e, T.swi[:, 32 * e + 12:32 * e + 24], T.vg2[:, 24 + e:48:2], col(430), A.add)
    to_block("vgi", T.vgi[:, 0:24:2], T.vgi[:, 1:24:2])
    own_pointers(0)
    for e in range(2):
        cp("swo", "cand%d" % e, T.cand[:, e:24:2], T.swo[:, 32 * e + 12:32 * e + 24])
    for mine, name in ((True, "vgi"), (False, "plp0")):
        a = 2 * half(0, mine)
        for e in range(2):
            cp(name + " wz%d0 wz%d1" % (mine, mine), "wl%d%d" % (mine, e), T.wf[:, a + 8 + 16 * e:a + 2 * C:32], T[name][:])
        tr("wl%d0 wl%d1" % (mine, mine), "wm%d" % mine, T.wr[:, a:a + 2 * C], T.wf[:, a:a + 2 * C])
    cp("wm0 wm1 cand0 cand1", "gv0 gv1", T.gv[:], (T.wr[:], T.cand[:]))
    tr("gv0 gv1", "vt0 vt1", T.vt32[:, 0:C], T.gv[:])
    cp("vt0 vt1", "pp", T.pp[:, 0:24], T.vt32[:, 8:C:16])
    turns.append([wrote[k] for k in "xq01 wm1 swz uq".split()])
    fill("wrc wm0 wm1", T.wr[:, 2 * C:2 * C + 32], Z + NONE)
    unpack(0, False, "SVSV")
    for b in (0, 1, 3, 2):
        move("S", "fw%d0 fw%d1 pl0" % (b, b), "ac%d" % b, T.ac[:, C * b:C * b + C], (plane(T.fw, b), T.pl0[:]))
    turns.append([wrote[k] for k in "fw00 ac0 fw30 ac1 ac3 ac2".split()])

    for t in range(3):
        u = up[t]
        hb, hk = T["hb%d" % t], "hb%d" % t
        if t > 0:
            gather_a("S", t, False, 0, 12, 24)
            gather_a("V", t, False, 0, 0, 12)
            for b in (1, 3, 2):
                gather_a("S", t, False, b)
        for b in (0, 1, 3):
            gather_b(t, b)
        gather_b(t, 2, 0, 2)
        gather_b(t, 2, 2, 3)
        for k in range(3):
            cs, ps, bank = slice(128 * k, 128 * k + 128), slice(64 * k, 64 * k + 64), 4 + k
            pb, scores = T["pb%d" % bank], T["pb%d" % bank][:, 0:64:9]
            quant("yt0%d yt1%d yt2%d yt3%d" % (k, k, k, k), "yq%d" % k, T.yq[:, cs], T.ys[:, cs], T.yt[:, 512 * k:512 * k + 512])
            mm("upq ups yq%d" % k, bank, T.yq[:, cs], T.ys[:, cs], T.upq[:], T.ups[:], 128)
            scan("pb%d pad4" % bank, "least%d" % k, T.least[:, 8 * k:8 * k + 8], T.least[:, 24:32], scores, 1e29, A.add, A.min)
            tt("pb%d least%d" % (bank, k), "above%d" % k, T.least[:, 32 + 8 * k:40 + 8 * k], scores, T.least[:, 8 * k:8 * k + 8], A.not_equal)
            act("pb%d" % bank, "sa%d" % k, T.sa[:, ps], pb[:, 64:128], FN.Copy)
            tt("pb%d sa%d" % (bank, k), "cb%d" % k, T.cb[:, ps], pb[:, 0:64], T.sa[:, ps], A.is_gt)
        turns.append([wrote[k] for k in "yt20 yt22 yq0 yq1 yq2".split()])
        scan("above0 above1 above2 d8", "ksc", T.ksc[:, 0:24], T.least[:, 32:56], sm(4), 0.0, A.mult, A.add)
        scan("cb0 cb1 cb2 sign", "pk", T.pk[:], T.sign[:], T.cb[:], 0.0, A.mult, A.add)
        place = T.pk[:, 7:192:8]
        cp("ksc lists pad2", "rp", T.rp[:], (T.ksc[:], lrp))
        tr("rp", "rt", T.rt[:], T.rp[:])
        for k in range(3):
            ts("rt ksc", "same%d" % k, T.same[:, 97 * k:97 * k + 96], T.rt[:], T.ksc[:, 8 * k + 7:8 * k + 8], A.is_equal, 1024.0, A.mult)
        cp("ksc", "same3", T.same[:, 96:291:97], T.ksc[:, 7:24:8])
        scan("same0 same1 same2 same3 mdup0 mdup1", "dup", T.dup[:], T.mdup[:], T.same[:], 0.0, A.add, A.max)
        cp("dup", "off", T.off[:, 0:3], T.dup[:, 96:291:97])
        cp("off val0 val1 val2", "tab", (T.tab[:], T.off[:, 0:3]), T.val[:])
        tr("tab", "tb", T.tb[:], T.tab[:, 0:2 * C])
        if t < 2:
            affine("tab k4%d" % up[t + 1], "tab", T.tab[:, 0:2 * C], T.tab[:, 0:2 * C], 0.0, col(428 + up[t + 1]))
        affine("ksc", "s5", sm(5, 3), T.ksc[:, 7:24:8], 2.0 ** 24, -1023.5 * 2.0 ** 24)
        tt("s5 k31", "s6", sm(6, 3), sm(5, 3), cf[:, 536:539], A.max)
        for q in range(4):
            a = 96 * u + 4 * (12 * u + q)
            move("S", "s6 ce%d" % u, "cq%d%d" % (u, q), T.ce[32 * q:32 * q + 32, a:a + 33:16], T.sm[32 * q:32 * q + 32, 192:195])
        scan("tb ce%d cq%d0 cq%d1 cq%d2 cq%d3" % (u, u, u, u, u), "oe", T.oe[:], T.tb[:, 0:2 * C:8], T.ce[:, 96 * u:96 * u + 96], 0.0, A.min, A.add)
        tt("oe", "rel", T.rel[0:64, :], T.oe[0:64, 3:96:4], T.oe[64:128, 3:96:4], A.min)
        for q in range(4):
            tt("rel", hk + "o%d" % q, hb[32 * q:32 * q + 32, 120 * u:120 * u + 24], T.rel[0:32, :], T.rel[32:64, :], A.min)
        tt("pk th7", "s7", T.fb[:, 1:96:4], place, th7, A.is_ge)
        tt("pk th4", "s8", T.fb[:, 0:96:4], place, th4, A.is_lt)
        affine("ksc lists pad2 f0", "s9a", T.fa[:, 2:128:4], (T.ksc[:], la), LS, -NONE)
        tt("s7 s12", "s14", T.fb[:, 3:96:4], T.fb[:, 1:96:4], sm(12), A.mult)
        move("S", "c_9%d" % u, "s15", T.fb[:, 2:96:4], c_8(u, 1))
        scan("s7 s8 s9a s14 s15", "aga agb agc ag0 ag1 ag2 ag3", T.ag[:, 0:96], T.fa[:, 0:96], T.fb[:], 0.0, A.mult, A.add)
        move("S", spread(T.ag, "ag") + " lists pad1", "s9", sm(9, 32), (T.ag[:], l8))
        move("S", "s9", hk + "d", pd(t, 0), sm(9))
        mine = "%so0 %so1 %so2 %so3 %sd pm%d0 pm%d1" % (hk, hk, hk, hk, hk, t, t)
        send(t, "h", mine, [(hb[:, 72 * u:72 * u + 72], hb[:, 72 * u:72 * u + 72])], hk + "r", NOTE)
        for h in range(2):
            for b in range(4):
                bank, cs, a = (7, 4, 5, 6)[b], slice(H * h, H * h + H), C * b + H * h
                mm("wq wsc yq%d yq%d" % (h, h + 1), bank, T.wq[:, 128 * b:128 * b + 128], T.wsc[:, 128 * b:128 * b + 128], T.yq[:, cs], T.ys[:, cs], H)
                act("pb%d" % bank, "rl%d%d" % (b, h), T.rl[:, a:a + H], T["pb%d" % bank][:, 0:H], FN.Relu, scale=0.03125)
                tt("pb%d rl%d%d" % (b, b, h), "xt%d%d" % (b, h), T.xt[:, 4 * H * h + b:4 * H * (h + 1):4], T["pb%d" % b][:, cs], T.rl[:, a:a + H], A.add)
            quant_x(t + 1, h, T.xt, " ".join("xt%d%d" % (b, h) for b in range(4)))
        if t < 2:
            turns.append([wrote["xq%d0" % (t + 1)], wrote["xt01"]])
            send_x(t + 1, "outh")
            unpack(t + 1, True, "SSSS")
            unpack(t + 1, False, "SSSS")
        else:
            mm("vq xq30 xq31", 4, T.vq[:], T.vs[:], T.xq3[:], T.xs3[:])
            dma("Y", "xq30 xq31", "", T.oc[:], u8(T.xq3[:]), "st")
            act("pb4", "yo", T.yo[:], T.pb4[:, 0:C], FN.Copy)
            for k in range(4):
                dma("Y", "xq30 xq31", "", T.osc[4 * k:4 * k + 4, :], T.xs3[32 * k:32 * k + 4, :], "st")
            dma("Y", "yo", "", T.y[:], T.yo[:], "st")
        old = T.npt[:, 3:96:4] if t else T.vgi[:]
        cp("npt vgi s1c", "own", T.s1[:, 3:96:4], old)
        tt("npt vgi c_x%d" % u, "pad5", T.xo[:, 0:24], old, c_x(u)[:, 1:48:2], A.add)
        both = mine + " " + hk + "r"
        for e in range(2):
            tt(both, "low%d" % e, T.low[:, e:48:2], hb[:, 0:24], hb[:, 120:144], A.min)
        cp(both, "dpna", T.dpn[:, 0:96:2], hb[:, 24:120:2])
        for e in range(2):
            cp(both, "dpsa%d" % e, T.dps[:, 2 * e:96:4], hb[:, 26 - 2 * e:120:4])
        tt("low0 low1 c_ys pad7", "sb", T.sbz[:, 1:96:2], T.low[:], c_ys, A.is_equal)
        tt("low0 low1 " + both, "dpnb", T.dpn[:, 1:96:2], T.low[:], hb[:, 25:120:2], A.add)
        for e in range(2):
            tt("low0 " + both, "dpsb%d" % e, T.dps[:, 2 * e + 1:96:4], T.low[:, 0:48:2], hb[:, 27 - 2 * e:120:4], A.add)
        scan("sb dpna dpnb", "wfa wl00 wl01 wl10 wl11", T.wf[:, 0:2 * C:8], T.sbz[:], T.dpn[:], 0.0, A.mult, A.add)
        scan("sb dpsa0 dpsa1 dpsb0 dpsb1 wm0 wm1", "wfb", T.wf[:, 1:2 * C:8], T.sbz[:], T.dps[:], 0.0, A.mult, A.add)
        ts("wfa", "cand cand0 cand1", T.cand[:], T.wf[:, C * u + 8:C * u + C:16], 1.0 / LS, A.mult, -Z / LS, A.add)
        tr("wfa wfb", "wr wm0 wm1", T.wr[:, 0:2 * C], T.wf[:, 0:2 * C])
        act("wr wrc cand", "gv1", T.gv[:, H:C], (T.wr[:], T.cand[:, 12:24]), FN.Copy)
        cp("wr wrc cand", "gv0", T.gv[:, 0:H], (T.wr[:], T.cand[:, 0:12]))
        for h in range(2):
            tr("gv%d" % h, "vt%d" % h, T.vt32[:, H * h:H * h + H], T.gv[:, H * h:H * h + H])
        v = T.vt32[:, 8:544], lv
        tt("vt0 vt1 lists s1c c_x%d" % u, "s1a", T.s1[:, 0:96:2], (v[0], lw), c_x(u), A.is_ge)
        tt("vt0 vt1 pad3 lists pad5 s0c", "s0d", T.s0[:, 3:128:4], v, T.xo[:], A.subtract)
        scan("s1a s0d s0c own", "npt", T.npt[:], T.s0[:, 0:96], T.s1[:], 0.0, A.mult, A.add)
        new = T.npt[:, 3:96:4]
        if t == 2:
            cp("npt", "pad6", T.ovi[:, 0:24], new)
            tr("pad6", "ovo", T.ovo[:], T.ovi[:])
            for k in range(8):
                q, e = k // 2, k % 2
                dma("YS"[e], "ovo", "", T.ov[k:k + 1, :], T.ovo[32 * q:32 * q + 24, 16 * e:16 * e + 16], "st")
            break
        name = "pl%d" % (t + 1)
        cp("npt", name, T[name][:], new)
        send(t + 1, "p", name, [(T["plp%d" % (t + 1)][:], T[name][:])], "plp%d" % (t + 1), NOTE)
        for b in (0, 1, 3):
            gather_a("S", t + 1, True, b)
        gather_a("V", t + 1, True, 2, 0, 12)
        gather_a("V", t + 1, True, 2, 12, 24)
        for b, q in zip((0, 1, 3, 2), "VVGG"):
            double(q, t + 1, b)
        to_block("npt", T.npt[:, 3:96:8], T.npt[:, 7:96:8])
        own_pointers(t + 1)
        turns.append([wrote[k] for k in "swi1 aw210 swx aw211 swz".split()])

    issue()
